import numpy as np, ml_dtypes
CORES = [24,25,26,27,28,29,30,31]
N = 8
BF = ml_dtypes.bfloat16
def gentries(a):
    return np.ascontiguousarray(a.reshape(8, 16, -1).transpose(0, 2, 1)).reshape(8, -1)
def gtable(e):
    e = np.asarray(e); return np.ascontiguousarray(e.reshape(8, -1, 16).transpose(0, 2, 1)).reshape(128, -1).astype(np.int32)
W, Q, L, C, S, ST, RO, TH = 4096, 8, 512, 128, 256, 2, 2, 7
K = Q * C
GM = (W - L) // (C - 1)
def val(rng, shape, even):
    if even: return rng.integers(0, 256, shape)
    return np.minimum(np.exp2(8.01 * rng.random(shape)).astype(np.int64) - 1, 255)
def items(rng, B, z, share, even):
    v = np.ascontiguousarray(B[np.arange(8)[None, :, None], z].transpose(0, 2 - 1, 3, 2))
    return np.where(rng.random(v.shape, dtype=np.float32) < share, val(rng, v.shape, even), v)
def parts(rng, even):
    per = rng.integers(7, 41, 8); V = rng.integers(0, 4, (8, 40)); ph = rng.integers(0, 40, (N, 8)); e = rng.integers(0, 40, (N, 8, Q)); G8 = np.arange(8)[None, :, None]
    B = np.repeat(val(rng, (8, 1, 16), even), 4, axis=1); B = np.where(rng.random(B.shape) < (0.6 if even else 0.75), val(rng, B.shape, even), B)
    z = V[G8, (np.arange(W) + ph[..., None]) % per[None, :, None]]
    z = np.where(rng.random(z.shape) < rng.choice(np.array([0.01, 0.02, 0.04, 0.06]), (N, 8, 1)), rng.integers(0, 4, z.shape), z)
    u = V[G8[..., None], (np.arange(L) + e[..., None]) % per[None, :, None, None]]
    u = np.where(rng.random(u.shape) < 0.015, rng.integers(0, 4, u.shape), u).reshape(N, 8, Q * L)
    T = items(rng, B, z, 0.08, even); P = items(rng, B, u, 0.08, even)
    eb = e[(np.arange(N)[:, None] + np.arange(RO)[None, :]) % N].transpose(0, 2, 1, 3)
    h = (ph[:, :, None, None] - eb).astype(np.int32)[..., None] + np.arange(W - L + 1, dtype=np.int32)
    hit = h % per.astype(np.int32)[None, :, None, None, None] == 0
    sc = rng.random(hit.shape, dtype=np.float32); f = rng.choice(np.array([0.02, 0.05, 0.15, 0.4], np.float32), (N, 8, 1, 1, 1))
    st = np.sort(np.argpartition(np.where(hit, sc * f, sc), C, axis=-1)[..., :C], axis=-1)
    x = rng.random((N, 8, Q, L)); y = rng.random((N, 8, 16, Q))
    if not even: x = x ** rng.choice(np.array([0.2, 1.0, 5.0]), (N, 8, Q, 1)); y = y ** rng.choice(np.array([0.3, 1.0, 4.0]), (N, 8, 1, Q))
    d = np.arange(L); wt = np.minimum(d + (x * (L - d)).astype(np.int64), L - 1)
    wt = np.where(rng.random(wt.shape) < 0.4, 0, wt)
    return T, P, wt, np.minimum((L * y).astype(np.int64), L - 1), np.ascontiguousarray(st).astype(np.int64)
def pack(T, P, wt, O, st):
    return {"txt": np.ascontiguousarray(T.reshape(N, 128, W)).astype(np.float32).astype(BF), "pat": np.ascontiguousarray(P.reshape(N, 128, Q * L)).astype(np.float32).astype(BF),
            "wit": np.ascontiguousarray(wt.reshape(N, 8, Q * L)).astype(np.int32), "prb": np.ascontiguousarray(O.reshape(N, 128, Q)).astype(np.int32),
            "cd": np.stack([gtable(a.reshape(8, RO * K)) for a in st])}
def runs(rng, n):
    gap = np.ones(C, np.int64); gap[0] = 0
    gap[1 + rng.permutation(C - 1)[:n - 1]] = 2 + rng.integers(0, GM - 1, n - 1)
    a = np.add.accumulate(gap); return a + int(rng.integers(0, W - L - int(a[-1]) + 1))
def still(rng, T, P, wt, O, g):
    X = rng.integers(0, 256, (1, 16, 1)); T[:, g] = X; P[:, g] = X; P[:, g, :, L - 1::L] = 255 - X
    wt[:, g] = 0; wt[:, g, :, 1] = L - 1; O[:, g] = rng.integers(0, L - 2, (N, 16, Q)); return X
def shares(rng, n):
    if rng.random() < 0.5:
        c = np.full(Q, n // Q); c[rng.permutation(Q)[:n - Q * (n // Q)]] += 1; return c
    c = np.ones(Q, np.int64); left = n - Q
    for p in rng.permutation(Q):
        k = min(C - 1, left); c[p] += k; left -= k
    return c
def setup_inputs(rng):
    return pack(*parts(rng, True))
def setup_inputs_spread(rng):
    return pack(*parts(rng, False))
def setup_inputs_ends(rng):
    cut = np.array([0, TH - 1, TH, 16]); row = np.arange(16)[:, None]
    def rec(n):
        v = 255 * (row < cut[rng.choice(4, (N, 8, 1, n), p=np.array([0.45, 0.3, 0.1, 0.15]))])
        return np.where(rng.random((N, 8, 1, n)) < 0.06, 255 * rng.integers(0, 2, (N, 8, 16, n)), v)
    T = rec(W); P = rec(Q * L); wt = (L - 1) * rng.integers(0, 2, (N, 8, Q, L)); O = (L - 1) * rng.integers(0, 2, (N, 8, 16, Q))
    O = np.where(rng.random(O.shape) < 0.1, rng.choice(np.array([1, L - 2]), O.shape), O)
    st = np.zeros((N, 8, RO, Q, C), np.int64); lo = np.arange(C); hi = W - L - lo[::-1]; last = np.concatenate([lo[:C - 2], np.array([W - 2 * L + 1, W - L])])
    for q in range(N):
        for g in range(8):
            for t in range(RO):
                for p in range(Q):
                    k = int(rng.integers(0, 4)); h = int(rng.integers(1, C))
                    if g == 7 or k == 2: st[q, g, t, p] = last
                    elif k == 0: st[q, g, t, p] = np.concatenate([lo[:h], hi[h:]])
                    elif k == 1: st[q, g, t, p] = np.concatenate([np.array([0, L - 1]), hi[2:]])
                    else: st[q, g, t, p] = np.concatenate([2 * lo[:h], W - L - 2 * lo[:C - h][::-1]])
    T[:, 7, :, :C + L] = 0; T[:, 7, :, W - 2 * L + 1] = 0; T[:, 7, :, W - L] = 255; T[:, 7, :, W - 1] = 255
    P[:, 7, :, 0::L] = 0; P[:, 7, :, L - 2::L] = 0; P[:, 7, :, L - 1::L] = 255
    wt[:, 7, :, 1] = L - 1; wt[:, 7, :, L - 1] = 0
    O[:, 7] = (L - 1) * rng.integers(0, 2, (N, 16, Q)); O[:, 7, 5] = 0; O[:, 7, 6] = L - 1
    return pack(T, P, wt, O, st)
def setup_inputs_corners(rng):
    T, P, wt, O, st = parts(rng, True); goal = (S, S + 1, S - 1, K, Q)
    for g in range(6):
        X = still(rng, T, P, wt, O, g)[0, :, 0]
        for q in range(N):
            for p in range(Q):
                if (g < 5 and rng.random() < 0.3) or (g == 5 and q % 2 == 0):
                    P[q, g, :, p * L + int(O[q, g, int(rng.choice(np.array([0, 7, 15]))), p])] = 255 - X
            for t in range(RO):
                c = shares(rng, S if g == 5 else goal[(g + q + t) % 5])
                for p in range(Q): st[q, g, t, p] = runs(rng, int(c[p]))
    X = still(rng, T, P, wt, O, 6); P[::2, 6, :, L - 2::L] = 255 - X; H = W // 2
    for q in range(N):
        for t in range(RO):
            for p in range(Q):
                s0 = int(rng.integers(0, H - L - C + 2)) if (q + t) % 2 == 0 else int(rng.integers(H, W - L - C + 2))
                st[q, 6, t, p] = s0 + np.arange(C)
    k = rng.integers(0, 3, (N, Q, L)); wt[:, 7] = np.where(k == 0, 0, np.where(k == 1, np.arange(L), L - 1))
    v = rng.choice(np.array([0, L - 1, L // 2, 3]), (2, N, 1, Q)); O[:, 7] = np.where(rng.random((N, 16, Q)) < 0.5, v[0], v[1])
    for q in range(N):
        for t in range(0, RO, 2):
            s0 = int(rng.integers(0, W - L - K + 2)); st[q, 7, t] = s0 + np.arange(K).reshape(Q, C)
    wt[0, 7, 0, 1] = L - 1; wt[0, 7, 1, 1] = 0; wt[0, 7, 2, 1] = L - 1; O[0, 7, :, 1] = 3 * rng.integers(0, 2, 16)
    tx, pt = T[0, 7], P[0, 7]; a, b = int(st[0, 7, 0, 1, 0]), int(st[0, 7, 0, 1, C - 1])
    for s in (a, b):
        for o in (0, 3): tx[:, s + o] = pt[:, L + o]
    pt[:, 2 * L - 2] = 255 - tx[:, a + L - 2]; pt[:, 2 * L - 1] = 255 - tx[:, b + L - 1]
    return pack(T, P, wt, O, st)
def setup_inputs_crowd(rng):
    T, P, wt, O, st = parts(rng, True)
    for g in range(8):
        if g % 2 == 0:
            still(rng, T, P, wt, O, g); o = int(rng.integers(0, L - 2)); O[:, g, 0] = o
            for q in range(N):
                if g % 4 == 2: O[q, g, 0, int(rng.integers(0, Q))] = (o + 1) % (L - 2)
                for t in range(RO): st[q, g, t] = runs(rng, S // Q)[None, :]
        else:
            D = int(rng.integers(8, min(28, GM) + 1)); z = int(rng.integers(0, D))
            X = rng.integers(0, 256, 16); Y = X.copy(); i = rng.permutation(16)[:TH]; Y[i] = 255 - Y[i]; XY = np.stack([X, Y], axis=1)
            h = rng.integers(0, 2, D); v = np.concatenate([h, h]); v[z] = 0; v[z + D] = 1
            P[:, g] = XY[:, v[np.arange(Q * L) % L % (2 * D)]]; wt[:, g] = 0
            o = rng.integers(0, L - 1, (N, 16, Q)); o = o + (o % D == z); o[:, 15] = z + D * rng.integers(0, 2, (N, Q)); O[:, g] = o
            for q in range(N):
                s0 = int(rng.integers(0, W - L - (C - 1) * D + 1)); st[q, g] = s0 + D * np.arange(C)
                u = v[(np.arange(W) - s0) % (2 * D)]
                if g % 4 == 3: u = np.where(rng.random(W) < 0.01, 1 - u, u)
                T[q, g] = XY[:, u]
    return pack(T, P, wt, O, st)
def check_inputs(d):
    bad = []
    for k, lo, hi in (("txt", 0, 255), ("pat", 0, 255), ("wit", 0, L - 1), ("prb", 0, L - 1), ("cd", 0, W - L)):
        v = np.asarray(d[k]).astype(np.float64)
        if not (np.min(v) >= lo and np.max(v) <= hi): bad.append("range of " + k)
        if np.any(v != np.floor(v)): bad.append("whole numbers of " + k)
    w = np.asarray(d["wit"]).astype(np.int64).reshape(N, 8, Q, L)
    if np.any((w != 0) & (w < np.arange(L))): bad.append("a witness of wit is 0 or at least its distance")
    s = np.stack([gentries(a) for a in d["cd"]]).astype(np.int64).reshape(N, 8, RO, Q, C)
    if np.any(s[..., 1:] <= s[..., :-1]): bad.append("rising starts of cd")
    return bad
def unlike(x, y):
    return np.add.reduce((x != y).astype(np.int64), axis=0) >= TH
def reference(txt, pat, wit, prb, cd):
    T = txt.astype(np.float32).astype(np.int64).reshape(N, 8, 16, W); P = pat.astype(np.float32).astype(np.int64).reshape(N, 8, 16, Q * L)
    wt = wit.astype(np.int64).reshape(N, 8, Q * L); O = prb.astype(np.int64).reshape(N, 8, 16, Q)
    st = np.stack([gentries(a) for a in cd]).astype(np.int64).reshape(N, 8, RO, K); pl = np.arange(K) // C
    for t in range(RO):
        for r in range(N):
            b = (r + t) % N
            for g in range(8):
                tx, pt, wv, ov, a = T[r, g], P[b, g], wt[b, g], O[b, g], st[r, g, t]
                live = np.arange(K)
                for stage in range(ST):
                    i, j = live[:-1], live[1:]; d = a[j] - a[i]
                    ok = (pl[i] == pl[j]) & (d < L); i, j, d = i[ok], j[ok], d[ok]
                    w = wv[pl[i] * L + d]; ok = w > 0; i, j, d, w = i[ok], j[ok], d[ok], w[ok]
                    y = tx[:, a[i] + w]; dead = np.zeros(K, bool)
                    dead[i[unlike(pt[:, pl[i] * L + w], y)]] = True
                    dead[j[unlike(pt[:, pl[j] * L + w - d], y)]] = True
                    live = live[~dead[live]]
                s = live[:S]
                if len(s) == 0: continue
                p = pl[s]; o = ov[:, p]
                bad = unlike(tx[:, a[s] + o], pt[:, p * L + o])
                fail = np.any(bad, axis=0); m = np.argmax(bad, axis=0); of = o[m, np.arange(len(s))]
                x = np.unique((a[s] + o[0])[~fail]); tx[:, x] = 255 - tx[:, x]
                d = a[s][1:] - a[s][:-1]; c = (p[1:] == p[:-1]) & fail[1:] & ~fail[:-1] & (of[1:] + d < L)
                place, first = np.unique((p[1:] * L + d)[c], return_index=True); wv[place] = (of[1:] + d)[c][first]
                who, first = np.unique(p[fail], return_index=True); mf = m[fail][first]
                for q, k in zip(who, mf): ov[:, q] = np.concatenate([ov[k:k + 1, q], ov[:k, q], ov[k + 1:, q]])
    return {"yt": T.reshape(N, 128, W).astype(np.float32).astype(BF), "yw": wt.astype(np.float32), "yo": O.reshape(N, 128, Q).astype(np.float32)}

@@ -1,0 +1,575 @@
+from concourse.bass import DstId, RemoteDMATransfer
+from concourse.mybir import dt, AluOpType, AxisListType, ActivationFunctionType
+
+F, B, I, U, H = "float32", "bfloat16", "int32", "uint16", "float16"
+_SB = {
+    "TX": (4352, B), "PA0": (4096, B), "PA1": (4096, B), "FN": (4360, B), "FO": (4360, F),
+    "DTI": (512, I), "DT": (520, B), "DN": (520, B), "DTF": (512, F), "CD": (128, I), "PRI": (8, I), "PF": (8, F),
+    "KI": (8, I), "CL": (24, F), "RM": (16, F), "IS": (256, F), "GM": (128, F), "MM": (256, F),
+    "Z": (144, B), "ZP": (16 * 144, B), "ZH": (288, H), "R0H": (128, H), "BR": (2048, F),
+    "ON": (128, B), "TRI": (128, B), "TGE": (128, B), "WF": (128, B), "IDF": (128, F), "UP": (128, F), "FC": (128, F),
+    "BC": (128, B), "SW": (128, F), "SD": (128, F), "R0C": (128, F), "TM": (128, F),
+    "ONH": (128, H), "NI": (128, B), "IDB": (128, B), "O9": (128, B), "O10": (128, B), "O11": (128, B), "ISB": (256, B),
+    "DM": (256, B), "RS": (256, B), "ZR": (256, B), "K1": (64, F), "NEG1": (64, F), "IL": (16, F), "TR": (32, F),
+    "P21": (8, F), "XT": (128, F), "YT": (128, F),
+    "AE0": (66, F), "AE1": (66, F), "DE": (66, F), "OW0": (66, U), "OW1": (66, U), "AX0": (66, F), "AX1": (66, F),
+    "C20": (64, F), "C21": (64, F), "A10": (64, F), "A11": (64, F), "AB0": (64, F), "AB1": (64, F),
+    "WG": (1040, B), "Y": (1040, B), "NQ": (4096, B), "PX": (4096, B), "E": (4096, B),
+    "T1": (66, F), "T2": (66, F), "T3": (66, F), "OY": (66, U), "O1": (64, U), "O2": (64, U), "TH": (128, F), "OK": (128, F),
+    "AL": (64, F), "UB": (66, F), "S1": (66, F), "UN": (64, F), "M2": (32, F), "PV": (32, F), "DD": (32, F), "OW2": (32, U),
+    "PVX": (32, F), "C2B": (32, F), "KB": (66, F), "EB": (34, F), "SR": (34, B), "SQ": (34, F), "AO1": (32, F), "NE": (32, F),
+    "AEV": (32, F), "AOD": (32, F), "AL2": (64, F), "LOC": (64, B), "OC": (64, U), "TOT": (2, F), "ACT": (16, F),
+    "BI": (8, F), "VT": (1024, F), "VS": (1024, I), "W1": (256, I), "W2": (256, I), "W3": (256, I), "W4": (256, I),
+    "PO16": (256, U), "TO16": (256, U), "DW": (256, F), "HK": (800, H), "XW": (256, H), "NM": (256, B),
+    "LS": (34, F), "LIM": (16, F), "SB": (256, B), "FI": (258, B), "XP": (256, H), "MK": (256, F), "QS": (256, F),
+    "L1": (32, F), "L2": (32, F), "PR": (32, F), "NN": (32, F), "OT": (16, U), "NV": (256, B), "EV": (512, B),
+    "R1": (8, F), "SP": (2, U), "F1": (16, B), "YO": (8, F), "DF": (8, F), "GD": (8, F),
+    "MA0": (256, F), "MA1": (256, F), "MB0": (16, U), "MB1": (16, U), "MC0": (8, F), "MC1": (8, F),
+    "LA0": (256, F), "LA1": (256, F), "LB0": (16, U), "LB1": (16, U), "LC0": (8, F), "LC1": (8, F),
+}
+_AT = {}
+for _k, (_n, _d) in _SB.items():
+    if _d == F and _n <= 66 and _k[:2] not in ("MC", "LC", "R1") and _k not in ("AE0", "AE1"):
+        _AT[_k] = 72 * len(_AT)
+SCRATCH = {k: ("sbuf", [128, n], d) for k, (n, d) in _SB.items() if k not in _AT}
+SCRATCH["POOL"] = ("sbuf", [128, 72 * len(_AT)], F)
+for _b in range(8):
+    SCRATCH["B%d" % _b] = ("psum", [128, 512], F)
+_DMAS = ["dcd", "dpr", "dw0", "dw1", "dtx", "dpa", "dfo", "dfn", "dyt", "dyw", "dyo"]
+_ARR = ["apa", "adn", "aa0", "ab0", "ac0", "aa1", "ab1", "ac1"]
+SEMAPHORES = ["cv", "cs", "ct", "cg", "sent"] + _DMAS + _ARR
+
+A = AluOpType
+AF = ActivationFunctionType
+BIG = 12288.0
+OWN = 240
+FAR = 8192.0
+
+
+def rank_program(g, core, T, topo):
+    rank = T.rank_of(core)
+    if rank is None:
+        return
+    n = len(T.cores)
+    before, after = T.cores[(rank - 1) % n], T.cores[(rank + 1) % n]
+    eng = {"v": g.vector, "s": g.scalar, "t": g.tensor, "g": g, "y": g.sync}
+    ops, acc = [], {}
+
+    def v(name, a=0, b=None, step=1):
+        b = _SB[name][0] if b is None else b
+        t, o = (T.POOL, _AT[name]) if name in _AT else (T[name], 0)
+        return (t[:, o + a:o + b:step] if step != 1 else t[:, o + a:o + b], [(name, a, b, step)])
+
+    def rv(name, hi, lo):
+        t, o = (T.POOL, _AT[name]) if name in _AT else (T[name], 0)
+        return (t[:, o + hi::-1] if o + lo == 0 else t[:, o + hi:o + lo - 1:-1], [(name, lo, hi + 1)])
+
+    def ind(win, off):
+        return (win[0].indirect(off[0]), win[1] + off[1])
+
+    def indw(win, off):
+        return (win[0].indirect(off[0]), win[1], off[1])
+
+    def col(k):
+        return v("CL", k, k + 1)
+
+    def ap(x):
+        return x[0] if isinstance(x, tuple) else x
+
+    def note(q, fn, reads, writes, sem=None, inc=1):
+        k = len(ops)
+        deps = set()
+        rs = [r for x in reads if isinstance(x, tuple) for r in x[1]] + [r for x in writes if len(x) > 2 for r in x[2]]
+        ws = [r for x in writes for r in x[1]]
+        for lst, isw in ((rs, False), (ws, True)):
+            for r in lst:
+                name, lo, hi, st = (r + (1,))[:4]
+                bank = name not in _SB
+                for lo2, hi2, st2, w2, k2 in acc.get(name, []):
+                    same = ops[k2]["q"] == q and ops[k2]["own"] and sem is None
+                    if bank and not same:
+                        deps.add(k2)
+                    elif lo < hi2 and lo2 < hi and (w2 or isw) and not (st == st2 and (lo - lo2) % st):
+                        if not same or (w2 and q != "t"):
+                            deps.add(k2)
+        for lst, isw in ((rs, False), (ws, True)):
+            for r in lst:
+                acc.setdefault(r[0], []).append((r[1], r[2], (r + (1,))[3], isw, k))
+        ops.append({"q": q, "fn": fn, "deps": deps, "sem": sem or ("c" + q), "inc": inc, "own": sem is None})
+
+    def tt(o, a, b, op):
+        note("v", lambda: g.vector.tensor_tensor(o[0], a[0], b[0], op), [a, b], [o])
+
+    def ts(o, a, s1, op0, s2=None, op1=None):
+        if op1 is None:
+            note("v", lambda: g.vector.tensor_scalar(o[0], a[0], ap(s1), None, op0), [a, s1], [o])
+        else:
+            note("v", lambda: g.vector.tensor_scalar(o[0], a[0], ap(s1), ap(s2), op0, op1), [a, s1, s2], [o])
+
+    def cp(o, a):
+        note("v", lambda: g.vector.tensor_copy(o[0], a[0]), [a], [o])
+
+    def ms(o, c):
+        note("v", lambda: g.vector.memset(o[0], c), [], [o])
+
+    def scan(o, a, b, init, op0, op1):
+        note("v", lambda: g.vector.tensor_tensor_scan(o[0], a[0], b[0], ap(init), op0, op1), [a, b, init], [o])
+
+    def act(o, a, func, bias=None, scale=None):
+        kw = {}
+        if bias is not None:
+            kw["bias"] = ap(bias)
+        if scale is not None:
+            kw["scale"] = ap(scale)
+        note("s", lambda: g.scalar.activation(o[0], a[0], func, **kw), [a, bias, scale], [o])
+
+    def mm(o, l, r, start=True, stop=True):
+        note("t", lambda: g.tensor.matmul(o[0], l[0], r[0], start, stop), [l, r], [o])
+
+    def iota(o, pat, base, ch, flag=True):
+        if flag:
+            note("g", lambda: g.iota(o[0], pat, base, ch, allow_small_or_imprecise_dtypes=True), [], [o])
+        else:
+            note("g", lambda: g.iota(o[0], pat, base, ch), [], [o])
+
+    def dma(q, sem, o, a):
+        note(q, lambda: eng[q].dma_start(o[0], a[0]), [a], [o], sem=sem, inc=16)
+
+    def send(dst, sem, land, src):
+        rid, pid, _se = topo.addr(dst)
+        note("g", lambda: g.remote_dma(T[land][:], src[0], T.sem[sem], T.sem.sent, pid, rid, topo.mask(core, dst)),
+             [src], [], sem="sent", inc=len(topo.engines(core, dst)))
+
+    def arrive(src, sem, land):
+        note(None, None, [], [v(land)], sem=sem, inc=len(topo.engines(src, core)))
+
+    def fold(bank, c0, nn, buf, b0, left, first=True, last=True):
+        for i in range(16):
+            mm(v(bank, c0, c0 + nn), left(i), v(buf, b0 + i, b0 + i + 16 * nn - 15, 16), first and i == 0, last and i == 15)
+
+    def zall(i):
+        return v("Z", 15 - i, 143 - i)
+
+    def zof(r):
+        return lambda i: v("ZP", 144 * r(i) + 15 - i, 144 * r(i) + 143 - i)
+
+    zpat, zrow, zown = zof(lambda i: i - i % 2), zof(lambda i: 0), zof(lambda i: i)
+
+    def zh(sign):
+        return lambda i: v("ZH", 144 * sign + 15 - i, 144 * sign + 143 - i)
+
+    spare = []
+
+    def idle(k):
+        for _ in range(min(k, len(spare))):
+            spare.pop(0)()
+
+    def hb(x):
+        return (x, [])
+
+    dma("y", "dcd", v("CD"), hb(T.cd[:]))
+    dma("s", "dw0", (T.DTI[0:128:2, :], [("DTI", 0, 512)]), hb(T.wit[:]))
+    dma("y", "dw1", (T.DTI[1:128:2, :], [("DTI", 1000, 1001)]), hb(T.wit[:]))
+    dma("s", "dpr", v("PRI"), hb(T.prb[:]))
+    dma("y", "dtx", v("TX", 0, 4096), hb(T.txt[:]))
+    dma("y", "dpa", v("PA0"), hb(T.pat[:]))
+    for sem, land in (("apa", "PA1"), ("adn", "DN"), ("aa0", "LA0"), ("ab0", "LB0"), ("ac0", "LC0")):
+        arrive(after, sem, land)
+    for sem, land in (("aa1", "LA1"), ("ab1", "LB1"), ("ac1", "LC1")):
+        arrive(before, sem, land)
+
+    K, II, G16, ODD, PP, GG, GC, EVEN, NGG, NEG, POS, B256, B512, BB1, BO, PCM, I64 = range(17)
+    iota(v("KI", 0, 1), [[0, 1]], 0, 1, False)
+    iota(v("IS"), [[1, 256]], 0, 0)
+    iota(v("GM"), [[1, 8], [0, 16]], 0, 0)
+    iota(v("MM"), [[0, 16], [1, 16]], 0, 0)
+    iota(v("P21"), [[2048, 8]], -8192, 0)
+    ms(v("DT", 0, 1), -256.0)
+    ms(v("DT", 512, 520), -256.0)
+    ms(v("TX", 4096, 4352), 0.0)
+    k0 = v("KI", 0, 1)
+    ts(v("KI", II, II + 1), k0, 15, A.bitwise_and)
+    ts(v("KI", G16, G16 + 1), k0, 112, A.bitwise_and)
+    ts(v("KI", ODD, ODD + 1), k0, 1, A.bitwise_and)
+    ts(v("KI", PP, PP + 1), k0, 1, A.arith_shift_right, 7, A.bitwise_and)
+    ts(v("KI", GG, GG + 1), k0, 4, A.arith_shift_right, 1, A.bitwise_and)
+    ts(v("KI", GC, GC + 1), k0, 4, A.arith_shift_right)
+    cp(v("CL", 0, 7), v("KI", 0, 7))
+    ts(col(EVEN), col(ODD), -1.0, A.mult, 1.0, A.add)
+    ts(col(NGG), col(GG), -1.0, A.mult, 1.0, A.add)
+    ts(col(NEG), col(ODD), 10000.0, A.mult, -10000.0, A.add)
+    ts(col(POS), col(ODD), 10000.0, A.mult)
+    ts(col(B256), col(PP), 512.0, A.mult, 256.0, A.add)
+    ts(col(B512), col(PP), 512.0, A.mult)
+    i128 = v("IS", 0, 128)
+    ts(v("UP"), i128, col(K), A.subtract, 1.0, A.is_equal)
+    ts(v("TM"), i128, col(K), A.subtract, -1.0, A.is_equal)
+    ts(v("RM"), v("IS", 0, 16), col(II), A.is_equal)
+    ts(v("Z"), v("IS", 0, 144), 15.0, A.subtract, col(G16), A.is_equal)
+    ts(v("FC"), v("UP"), col(EVEN), A.mult)
+    ts(v("BC"), v("TM"), col(ODD), A.mult)
+    tt(v("SW"), v("FC"), v("BC"), A.add)
+    ts(v("ON"), v("GM"), col(GC), A.is_equal)
+
+    def zmake(r):
+        act(v("ZP", 144 * r, 144 * r + 144), v("Z"), AF.Identity, scale=v("RM", r, r + 1))
+
+    def brmake(i):
+        act(v("BR", 128 * i, 128 * i + 128), v("ON"), AF.Identity, scale=v("RM", i, i + 1))
+
+    for r in range(0, 16, 2):
+        zmake(r)
+
+    def starts(t):
+        ae = "AE%d" % t
+
+        def spread(a, h):
+            return lambda: ts(v("XT", 32 * a + 16 * h, 32 * a + 16 * h + 16), v("CD", 64 * t + a, 64 * t + 64, 4), col(GG if h else NGG), A.mult)
+
+        def join(a):
+            tt(v(ae, 1 + 16 * a, 17 + 16 * a), v("YT", 32 * a, 32 * a + 16), v("YT", 32 * a + 16, 32 * a + 32), A.add)
+            if a == 3:
+                mm(v("B7", 0, 2), v("SW"), (T[ae][:, 1:65:63], [(ae, 1, 2), (ae, 64, 65)]))
+
+        return [spread(a, h) for a in range(4) for h in range(2)] + [
+            lambda: note("v", lambda: g.vector.transpose(T.YT[:], T.XT[:]), [v("XT")], [v("YT")]),
+            lambda: join(0), lambda: join(3), lambda: join(1), lambda: join(2),
+            lambda: ts(v(ae, 0, 1), v("B7", 1, 2), col(ODD), A.mult, col(NEG), A.add),
+            lambda: ts(v(ae, 65, 66), v("B7", 0, 1), col(EVEN), A.mult, col(POS), A.add),
+            lambda: tt(v("DE", 0, 65), v(ae, 1, 66), v(ae, 0, 65), A.subtract),
+            lambda: ts(v("OW%d" % t, 0, 65), v("DE", 0, 65), 512.0, A.min, col(B512) if t else 0.0, A.add)]
+
+    def starts2(t):
+        ae = "AE%d" % t
+        return [lambda: act(v("AX%d" % t, 0, 65), v(ae, 0, 65), AF.Identity, bias=256.0),
+                lambda: act(v("C2%d" % t), v("DE", 0, 64), AF.Identity, bias=col(B256), scale=-1.0),
+                lambda: act(v("A1%d" % t), v(ae, 1, 65), AF.Identity, bias=4096.0),
+                lambda: act(v("AB%d" % t), v(ae, 1, 65), AF.Identity, bias=4096.0 - BIG)]
+
+    def select(o, a, pat, op, fill, base, ch):
+        note("g", lambda: g.affine_select(o[0], a[0], pat, op, fill, base, ch), [a], [o])
+
+    dti = (T.DTI[:, 1:512], [("DTI", 0, 512), ("DTI", 1000, 1001)])
+    for f in starts(0):
+        f()
+    ts(v("DT", 1, 512), dti, -256.0, A.add)
+    run = [[1, 128]]
+    act(v("TM"), v("ON"), AF.Identity)
+    act(v("NI"), v("ON"), AF.Identity, scale=-1.0)
+    act(v("IL"), v("IS", 0, 16), AF.Identity, bias=col(II), scale=16.0)
+    for i in range(12):
+        brmake(i)
+    select(v("TRI"), v("ON"), run, A.is_gt, 0.0, 0, -1)
+    select(v("TGE"), v("ON"), [[-1, 128]], A.is_ge, 0.0, 0, 1)
+    select(v("IDF"), v("TM"), run, A.is_equal, 0.0, 0, -1)
+    select(v("WF"), v("NI"), run, A.is_gt, 0.0, 0, -1)
+    select(v("SD"), v("TM"), run, A.is_equal, 0.0, -1, -1)
+    select(v("R0C"), v("TM"), [[0, 8], [1, 16]], A.is_equal, 0.0, 0, 0)
+    select(v("WF"), v("WF"), run, A.not_equal, 1.0, 0, -1)
+    select(v("SD"), v("SD"), run, A.not_equal, -1.0, 0, -1)
+    select(v("IDB"), v("ON"), run, A.is_equal, 0.0, 0, -1)
+    select(v("NI"), v("NI"), run, A.is_equal, 0.0, 0, -1)
+    send(before, "adn", "DN", v("DT"))
+    iota(v("ISB"), [[1, 256]], 0, 0)
+    send(before, "apa", "PA1", v("PA0"))
+    iota(v("FN"), [[0, 4360]], -256, 0)
+    iota(v("FO"), [[0, 4360]], 0, 0)
+
+    early = [
+        lambda: cp(v("PF"), v("PRI")),
+        lambda: cp(v("DTF", 0, 1), (T.DTI[:, 0:1], dti[1])),
+        lambda: ts(col(BB1), col(PP), 512.0, A.mult, BIG, A.add),
+        lambda: ts(col(BO), col(PP), 512.0, A.mult, 256.0 - BIG, A.add),
+        lambda: ts(col(PCM), col(II), 512.0, A.mult, -2048.0, A.add),
+        lambda: ts(col(I64), col(II), 64.0, A.mult, -1024.0, A.add),
+        lambda: ts(v("ZH", 0, 144), v("Z"), v("RM", 0, 1), A.mult),
+        lambda: ts(v("ZH", 144, 288), v("Z"), v("RM", 0, 1), A.mult, -1.0, A.mult),
+        lambda: ts(v("R0H"), v("ON"), v("RM", 0, 1), A.mult),
+        lambda: cp(v("ONH"), v("ON")),
+        lambda: ms(v("HK", 256, 272), -2048.0),
+        lambda: ms(v("HK", 528, 545), 512.0),
+        lambda: ts(v("TR", 0, 16), v("IL"), 2049.0, A.add, 1.0 / FAR, A.mult),
+        lambda: ts(v("TR", 16, 32), v("IL"), 2048.0, A.add, 1.0 / FAR, A.mult),
+    ]
+
+    def early_scalar():
+        for o, c in ((v("UB", 0, 1), 0.0), (v("KB", 64, 66), 0.0), (v("EB", 32, 34), 1.0), (v("NEG1"), -1.0), (v("ZR"), 0.0),
+                     (v("FI", 0, 1), 0.0), (v("FI", 257, 258), 0.0)):
+            act(o, v("IS", 0, o[1][0][2] - o[1][0][1]), AF.Identity, bias=c, scale=0.0)
+        act(v("P21"), v("P21"), AF.Identity, scale=1024.0)
+        act(v("K1"), v("IS", 0, 64), AF.Identity, bias=col(I64))
+        act(v("RS"), v("MM"), AF.Sign)
+        for r in range(1, 16, 2):
+            zmake(r)
+        for nm, src, sc in (("O9", "ON", 512.0), ("O10", "ON", -1024.0), ("O11", "ON", 2048.0)):
+            act(v(nm), v(src), AF.Identity, scale=sc)
+        act(v("DTF", 1, 512), v("DT", 1, 512), AF.Identity, bias=256.0)
+
+    def compare(j, us):
+        bank, e = ("B1", "E") if j == 0 else ("B0", "PX")
+        for u in us:
+            if u == 0:
+                mm(v(bank, 0, 256), v("ON"), v("ZR"), True, False)
+            e0 = 272 * u
+            keys = v("HK", 272 + 16 * u, 528) if j == 0 else v("XW", 16 * u, 256)
+            ts(v(e, e0, 256 * u + 256), keys, 1.0 / FAR, A.mult, v("PR", 16 * j + u, 16 * j + u + 1), A.is_equal)
+            mm(v(bank, 16 * u, 16 * u + 16), v("TRI"), v(e, e0, e0 + 16), False, u == 15)
+            if u < 15:
+                mm(v(bank, 16 * u + 16, 256), v("ON"), v(e, e0 + 16, 256 * u + 256), False, False)
+
+    def places(j, out):
+        a, b = 16 * j, 16 * j + 16
+        if j:
+            tt(v("MK"), v("B0", 0, 256), v("DM"), A.mult)
+            scan(v("QS"), v("RS"), v("MK"), 0.0, A.mult, A.add)
+        tt(v("L1", a, b), v("QS", 15, 256, 16) if j else v("B5", 0, 16), v("PR", a, b), A.add)
+        tt(v("L2", a, b), v("L1", a, b), v("TR", a, b), A.min)
+        ts(out, v("L2", a, b), FAR, A.mult, 2048.0, A.add)
+
+    def differ(out, a, b, bank, later=False):
+        k = out[1][0][2] - out[1][0][1]
+        mm(v(bank, 0, k), v("IDB"), a, True, False)
+        mm(v(bank, 0, k), v("NI"), b, False, True)
+        act(v("EV", 0, k), v(bank, 0, k), AF.Abs)
+        if later:
+            return lambda: act(out, v("EV", 0, k), AF.Sign)
+        act(out, v("EV", 0, k), AF.Sign)
+
+    def duel(t, nn, ychunks):
+        pat = v("PA%d" % t)
+        for a, b in ychunks:
+            act(v("Y", 16 * a, 16 * b), ind(v("TX"), v("OY", a, b)), AF.Copy)
+        off = 16 if nn == 64 else 0
+        c = nn - nn // 4
+        act(v("PX", 16 * c, 16 * nn), ind(pat, v("O1", c, nn)), AF.Copy)
+        differ(v("NQ", 1024 + 16 * c, 1024 + 16 * nn), v("Y", off + 16 * c, off + 16 * nn), v("PX", 16 * c, 16 * nn), "B5")
+        for a, b in ychunks:
+            b = min(b, nn)
+            tt(v("NQ", 16 * a, 16 * b), ind(pat, v("O2", a, b)), v("Y", 16 * a, 16 * b), A.not_equal)
+        fold("B1", 0, nn, "NQ", 0, zall)
+        tt(v("NQ", 1024, 1024 + 16 * c), ind(pat, v("O1", 0, c)), v("Y", off, off + 16 * c), A.not_equal)
+        fold("B1", nn, nn, "NQ", 1024, zall)
+
+    def own_witnesses(vals, offs):
+        ts(indw(v("FO"), offs), vals, 1.0, A.mult, 256.0, A.add)
+
+    def r1(k):
+        return v("R1", k, k + 1)
+
+    def w(a, b):
+        return v("B0", a, b)
+
+    def one_round(t):
+        tab = v("FN") if t else v("DT")
+        pick = zrow if t else zpat
+        pat = v("PA%d" % t)
+        ow = "OW%d" % t
+        pf = v("LC0") if t else v("PF")
+        to = after if t else before
+        if t:
+            cp(indw(v("FN"), v("LB0")), v("LA0"))
+        cp(v("WG", 0, 512), ind(tab, v(ow, 0, 32)))
+        act(v("WG", 512, 1040), ind(tab, v(ow, 32, 65)), AF.Copy)
+        fold("B0", 0, 65, "WG", 0, pick)
+        if t == 0:
+            for f in starts2(0):
+                f()
+            for i in range(12, 16):
+                brmake(i)
+            for f in early[:8]:
+                f()
+        tt(v("T1", 0, 65), w(0, 65), v("AX%d" % t, 0, 65), A.add)
+        ts(v("OY", 0, 65), v("T1", 0, 65), 0.0, A.max)
+        tt(v("T2", 0, 64), w(0, 64), v("C2%d" % t), A.add)
+        ts(v("O1"), w(1, 65), col(B256), A.add)
+        ts(v("O2"), v("T2", 0, 64), 0.0, A.max)
+        ts(v("T3", 0, 65), w(0, 65), -255.5, A.is_lt, 100.0, A.mult)
+        for i in range(16):
+            mm(v("B%d" % (3 + i // 8), 64 * (i % 8), 64 * (i % 8) + 64), v("BR", 128 * i, 128 * i + 128), v("AE%d" % t, 1, 65))
+        if t == 0:
+            for f in early[8:]:
+                f()
+            spare.append(lambda: ts(v("DM"), v("MM"), col(II), A.is_equal))
+            spare.extend(starts(1) + starts2(1))
+            idle(9)
+        duel(t, 64, [(0, 8), (8, 24), (24, 44), (44, 65)])
+        if t == 0:
+            early_scalar()
+            dma("y", "dfn", (T.FN[0:128:16, 0:4096], [("FN", 0, 4096)]), (T.DN[0:128:2, 0:512], [("DN", 0, 520)]))
+            dma("y", "dfo", (T.FO[0:128:16, 0:4096], [("FO", 0, 4096)]), (T.DTF[0:128:2, :], [("DTF", 0, 512)]))
+        ts(v("TH", 0, 64), v("T3", 0, 64), 6.5, A.add)
+        ts(v("TH", 64, 128), v("T3", 1, 65), 6.5, A.add)
+        ts(v("BI"), pf, 4097.0, A.mult)
+        tt(v("BI"), v("BI"), v("P21"), A.add)
+        idle(4)
+        tt(v("OK"), v("B1", 0, 128), v("TH"), A.is_lt)
+        tt(v("AL"), v("OK", 0, 64), v("OK", 64, 128), A.mult)
+        tt(v("UB", 1, 65), v("AL"), v("A1%d" % t), A.mult)
+        scan(v("S1", 0, 65), v("UB", 0, 65), v("UB", 0, 65), 0.0, A.max, A.max)
+        mm(v("B2", 0, 1), v("FC"), v("S1", 64, 65))
+        tt(v("UN"), v("AL"), v("AB%d" % t), A.mult)
+        tt(v("M2"), v("UN", 0, 64, 2), v("UN", 1, 64, 2), A.min)
+        ts(v("PV"), v("S1", 0, 64, 2), v("B2", 0, 1), A.max)
+        tt(v("DD"), v("M2"), v("PV"), A.subtract)
+        ts(v("OW2"), v("DD"), 512.0 - BIG, A.min, col(BB1) if t else BIG, A.add)
+        act(v("WG", 256, 512), ind(tab, v("OW2", 16, 32)), AF.Copy)
+        cp(v("WG", 0, 256), ind(tab, v("OW2", 0, 16)))
+        fold("B0", 0, 32, "WG", 0, pick)
+        ts(v("PVX"), v("PV"), -3840.0, A.add)
+        ts(v("C2B"), v("DD"), -1.0, A.mult, col(BO), A.add)
+        ts(v("EB", 0, 32), v("M2"), -0.5, A.is_gt)
+        ts(v("AO1"), v("AL", 1, 64, 2), 1.0, A.add)
+        ts(v("NE"), v("AL", 0, 64, 2), -1.0, A.mult, 1.0, A.add)
+        idle(5)
+        tt(v("T1", 0, 32), w(0, 32), v("PVX"), A.add)
+        ts(v("OY", 0, 32), v("T1", 0, 32), 0.0, A.max)
+        tt(v("T2", 0, 32), w(0, 32), v("C2B"), A.add)
+        ts(v("O1", 0, 32), w(0, 32), col(B256), A.add)
+        ts(v("O2", 0, 32), v("T2", 0, 32), 0.0, A.max)
+        ts(v("T3", 0, 32), w(0, 32), -255.5, A.is_lt, 100.0, A.mult)
+        duel(t, 32, [(0, 8), (8, 20), (20, 32)])
+        for i in range(16):
+            act(v("VT", i, 1024, 16), v("B%d" % (3 + i // 8), 64 * (i % 8), 64 * (i % 8) + 64), AF.Identity, bias=v("BI", i // 2, i // 2 + 1))
+        ts(v("TH", 0, 32), v("T3", 0, 32), 6.5, A.add)
+        ts(v("TH", 32, 64), v("T3", 0, 32), 6.5, A.add)
+        idle(11)
+        tt(v("KB", 0, 64), v("B1", 0, 64), v("TH", 0, 64), A.is_gt)
+        scan(rv("SR", 32, 0), rv("EB", 32, 0), rv("KB", 64, 32), 0.0, A.mult, A.add)
+        mm(v("B2", 0, 1), v("BC"), v("SR", 0, 1))
+        kj = v("KB", 0, 32)
+        tt(v("T1", 0, 32), v("AL", 0, 64, 2), kj, A.subtract)
+        tt(v("T2", 0, 32), v("NE"), kj, A.mult)
+        tt(v("AEV"), v("T1", 0, 32), v("AO1"), A.mult)
+        tt(v("AOD"), v("AL", 1, 64, 2), v("T2", 0, 32), A.subtract)
+        scan(rv("SQ", 32, 1), rv("EB", 32, 1), rv("KB", 64, 33), v("B2", 0, 1), A.mult, A.add)
+        tt(v("AL2", 0, 64, 2), v("AEV"), v("SQ", 1, 33), A.is_gt)
+        tt(v("AL2", 1, 64, 2), v("AOD"), v("SQ", 1, 33), A.is_gt)
+        scan(v("LOC"), v("AL2"), v("NEG1"), 0.0, A.add, A.add)
+        mm(v("B2", 0, 1), v("TRI"), v("LOC", 63, 64))
+        mm(v("B2", 1, 2), v("ON"), v("LOC", 63, 64))
+        tt(v("T1", 0, 64), v("AL2"), v("K1"), A.mult)
+        tt(v("T3", 0, 64), v("T1", 0, 64), v("LOC"), A.add)
+        ts(v("OC"), v("T3", 0, 64), v("B2", 0, 1), A.add, 1024.0, A.add)
+        cp(indw(v("VS"), v("OC")), v("VT"))
+        act(v("TOT", 0, 1), v("B2", 1, 2), AF.Identity, bias=1024.0)
+        act(v("TOT", 1, 2), v("B2", 1, 2), AF.Identity, bias=1024.0, scale=-1.0)
+        mm(v("B2", 0, 8), v("SD"), pf)
+        act(v("DF"), v("B2", 0, 8), AF.Identity)
+        vs = v("VS", 0, 256)
+        ts(v("W1"), vs, 12, A.arith_shift_right)
+        ts(v("W2"), vs, 4095, A.bitwise_and)
+        ts(v("PO16"), v("W1"), 2048.0, A.add)
+        chunks = [(0, 16), (16, 64), (64, 128), (128, 192), (192, OWN)]
+        cp(v("TO16"), v("W2"))
+        for a, b in chunks[:-1] + [(192, 256)]:
+            act(v("PX", 16 * a, 16 * b), ind(pat, v("PO16", a, b)), AF.Copy)
+        act(v("Y", 0, 4096 - 16 * OWN), ind(v("TX"), v("TO16", OWN, 256)), AF.Copy)
+        tt(v("DW", 1, 256), v("VS", 1, 256), v("VS", 0, 255), A.subtract)
+        ts(v("W4"), v("W1"), -512, A.bitwise_and)
+        ts(v("HK", 545, 800), v("DW", 1, 256), 512.0, A.min, 1.0, A.max)
+        ts(v("HK", 0, 256), v("W2"), -2048.0, A.add)
+        tt(v("HK", 272, 528), v("W4"), v("HK", 544, 800), A.add)
+        fold("B0", 0, 33, "HK", 0, zh(0))
+        fold("B0", 40, 16, "HK", 272, zh(0), True, False)
+        fold("B0", 40, 16, "HK", 271, zh(1), False, False)
+        fold("B0", 40, 16, "HK", 543, zh(0), False, True)
+        mm(v("B7", 0, 256), v("R0H"), v("HK", 0, 256))
+        for j, (a, b) in enumerate(chunks):
+            tt(v("NQ", 16 * a, 16 * b), ind(v("TX"), v("TO16", a, b)), v("PX", 16 * a, 16 * b), A.not_equal)
+            if j == 0:
+                continue
+            a0 = 0 if j == 1 else a
+            fold("B4" if j == 4 else "B3", a0, 64, "NQ", 16 * a0, zall)
+            if j == 3:
+                rest = differ(v("NQ", 16 * OWN, 4096), v("Y", 0, 4096 - 16 * OWN), v("PX", 16 * OWN, 4096), "B1", True)
+                act(v("SB", 0, 192), v("B3", 0, 192), AF.Sign, bias=-6.5)
+                mm(v("B5", 0, 192), v("WF"), v("SB", 0, 192))
+                rest()
+        act(v("SB", 192, 256), v("B4", 192, 256), AF.Sign, bias=-6.5)
+        ts(v("W3"), v("W1"), 511, A.bitwise_and)
+        ts(v("NM"), v("W4"), col(PCM), A.not_equal, 2048.0, A.mult)
+        ts(v("ACT"), v("IL"), v("TOT", 0, 1), A.is_ge, 5000.0, A.mult)
+        for (a, b), gb, qb in (((0, 192), "B5", "B6"), ((192, 256), "B2", "B4")):
+            if a:
+                mm(v(gb, a, b), v("WF"), v("SB", a, b))
+            ts(v("FI", 1 + a, 1 + b), v(gb, a, b), col(II), A.is_gt)
+            tt(v("XP", a, b), v("FI", 1 + a, 1 + b), v("W3", a, b), A.mult)
+            q = v(qb, a, b)
+            mm(q, v("O10"), v("FI", 1 + a, 1 + b), True, False)
+            mm(q, v("O9"), v("FI", a, b), False, False)
+            mm(q, v("ONH"), v("XP", a, b), False, True)
+            if a == 0:
+                ts(v("LS", 0, 33), w(0, 33), 1.0 / FAR, A.mult)
+                ts(v("L1", 0, 16), w(40, 56), -1.0, A.mult, -512.0, A.add)
+                tt(v("LIM"), v("L1", 0, 16), v("ACT"), A.subtract)
+            else:
+                cp(v("XW"), v("B7", 0, 256))
+            tt(v("MK", a, b), q, v("DM", a, b), A.mult)
+            scan(v("QS", a, b), v("RS", a, b), v("MK", a, b), 0.0, A.mult, A.add)
+        mm(v("B3", 0, 256), v("ONH"), v("XP"), True, False)
+        mm(v("B3", 0, 256), v("R0H"), v("HK", 544, 800), False, True)
+        act(v("MA%d" % t), v("B3", 0, 256), AF.Identity, bias=-256.0)
+        send(to, "aa%d" % t, "LA%d" % t, v("MA%d" % t))
+        sc = v("B7", 256, 512)
+        mm(sc, v("NI"), v("ISB"), True, False)
+        mm(sc, v("NI"), v("NM"), False, False)
+        mm(sc, v("O11"), v("FI", 1, 257), False, True)
+        q = v("QS", 15, 256, 16)
+        tt(v("NN", 0, 16), q, v("LIM"), A.is_ge)
+        tt(v("NN", 16, 32), q, v("ACT"), A.is_lt)
+        tt(v("PR", 0, 16), v("NN", 0, 16), v("LS", 17, 33), A.add)
+        tt(v("PR", 16, 32), v("NN", 16, 32), v("LS", 0, 16), A.add)
+        compare(0, range(16))
+        act(v("EV", 0, 256), v("B1", 0, 256), AF.Identity)
+        compare(1, range(4))
+        fold("B5", 0, 16, "EV", 0, zown)
+        compare(1, range(4, 16))
+        places(0, v("MB%d" % t))
+        send(to, "ab%d" % t, "LB%d" % t, v("MB%d" % t))
+        note("v", lambda: g.vector.tensor_reduce(T.R1[:, 0:1], sc[0], AxisListType.X, A.max), [sc], [r1(0)])
+        ts(r1(1), r1(0), v("TOT", 1, 2), A.is_gt)
+        ts(r1(2), r1(0), -1.0, A.mult, 2049.0 - 257.0, A.add)
+        ts(v("SP", 0, 1), r1(2), r1(1), A.mult, 257.0, A.add)
+        places(1, v("OT"))
+        act(v("NV"), ind(v("TX"), v("OT")), AF.Identity, bias=255.0, scale=-1.0)
+        cp(v("F1"), ind(v("FI"), v("SP", 0, 1)))
+        mm(v("B2", 0, 8), v("TGE"), v("F1", 0, 8))
+        tt(v("YO"), v("F1", 0, 8), pf, A.mult)
+        mm(v("B2", 8, 16), v("IDF"), pf, True, False)
+        mm(v("B2", 8, 16), v("R0C"), v("YO"), False, True)
+        tt(v("GD"), v("B2", 0, 8), v("DF"), A.mult)
+        tt(v("MC%d" % t), v("B2", 8, 16), v("GD"), A.add)
+        send(to, "ac%d" % t, "LC%d" % t, v("MC%d" % t))
+        cp(indw(v("TX"), v("OT")), v("NV"))
+        if t:
+            dma("y", "dyt", hb(T.yt[:]), v("TX", 0, 4096))
+            own_witnesses(v("MA0"), v("MB0"))
+            own_witnesses(v("LA1"), v("LB1"))
+            dma("s", "dyw", hb(T.yw[:]), (T.FO[0:128:16, 0:4096], [("FO", 0, 4096)]))
+            dma("y", "dyo", hb(T.yo[:]), v("LC1"))
+
+    one_round(0)
+    one_round(1)
+
+    total, known = {}, {q: {} for q in eng}
+    for o in ops:
+        total[o["sem"]] = total.get(o["sem"], 0) + o["inc"]
+        o["at"] = total[o["sem"]]
+        q = o["q"]
+        if q is None:
+            o["clock"] = {o["sem"]: o["at"]}
+            continue
+        kn = known[q]
+        for k in sorted(o["deps"], reverse=True):
+            d = ops[k]
+            if kn.get(d["sem"], 0) < d["at"]:
+                eng[q].wait_ge(T.sem[d["sem"]], d["at"])
+                for s, c in d["clock"].items():
+                    kn[s] = max(kn.get(s, 0), c)
+        ins = o["fn"]()
+        if o["sem"] != "sent":
+            ins.then_inc(T.sem[o["sem"]], o["inc"])
+        o["clock"] = dict(kn)
+        o["clock"][o["sem"]] = max(o["at"], kn.get(o["sem"], 0))
+    for s, c in total.items():
+        g.wait_ge(T.sem[s], c)

@@ -6,21 +6,21 @@ _SB = {
     "TX": (4352, B), "PA0": (4096, B), "PA1": (4096, B), "FN": (4360, B), "FO": (4360, F),
     "DTI": (512, I), "DT": (520, B), "DN": (520, B), "DTF": (512, F), "CD": (128, I), "PRI": (8, I), "PF": (8, F),
     "KI": (8, I), "CL": (24, F), "RM": (16, F), "IS": (256, F), "GM": (128, F), "MM": (256, F),
-    "Z": (144, B), "ZP": (16 * 144, B), "ZH": (288, H), "R0H": (128, H), "BR": (2048, F),
+    "Z": (144, B), "ZP": (16 * 144, B), "ZH": (288, H), "R0H": (128, H), "R0N": (128, H), "R02": (128, H), "NI4": (128, B), "BR": (2048, F),
     "ON": (128, B), "TRI": (128, B), "TGE": (128, B), "WF": (128, B), "IDF": (128, F), "UP": (128, F), "FC": (128, F),
     "BC": (128, B), "SW": (128, F), "SD": (128, F), "R0C": (128, F), "TM": (128, F),
     "ONH": (128, H), "NI": (128, B), "IDB": (128, B), "O9": (128, B), "O10": (128, B), "O11": (128, B), "ISB": (256, B),
     "DM": (256, B), "RS": (256, B), "ZR": (256, B), "K1": (64, F), "NEG1": (64, F), "IL": (16, F), "TR": (32, F),
     "P21": (8, F), "XT": (128, F), "YT": (128, F),
     "AE0": (66, F), "AE1": (66, F), "DE": (66, F), "OW0": (66, U), "OW1": (66, U), "AX0": (66, F), "AX1": (66, F),
-    "C20": (64, F), "C21": (64, F), "A10": (64, F), "A11": (64, F), "AB0": (64, F), "AB1": (64, F),
+    "C20": (64, F), "C21": (64, F), "A10": (66, F), "A11": (66, F), "AB0": (64, F), "AB1": (64, F),
     "WG": (1040, B), "Y": (1040, B), "NQ": (4096, B), "PX": (4096, B), "E": (4096, B),
     "T1": (66, F), "T2": (66, F), "T3": (66, F), "OY": (66, U), "O1": (64, U), "O2": (64, U), "TH": (128, F), "OK": (128, F),
     "AL": (64, F), "UB": (66, F), "S1": (66, F), "UN": (64, F), "M2": (32, F), "PV": (32, F), "DD": (32, F), "OW2": (32, U),
     "PVX": (32, F), "C2B": (32, F), "KB": (66, F), "EB": (34, F), "SR": (34, B), "SQ": (34, F), "AO1": (32, F), "NE": (32, F),
     "AEV": (32, F), "AOD": (32, F), "AL2": (64, F), "LOC": (64, B), "OC": (64, U), "TOT": (2, F), "ACT": (16, F),
-    "BI": (8, F), "VT": (1024, F), "VS": (1024, I), "W1": (256, I), "W2": (256, I), "W3": (256, I), "W4": (256, I),
-    "PO16": (256, U), "TO16": (256, U), "DW": (256, F), "HK": (800, H), "XW": (256, H), "NM": (256, B),
+    "BI": (8, F), "VT": (1024, F), "VS": (1024, I), "W1": (256, I), "W2": (256, I), "W4": (256, I),
+    "PO16": (256, U), "TO16": (256, U), "DW": (256, F), "HK": (800, H), "XW": (256, U), "C4": (256, B), "O14": (128, B), "NM": (256, B),
     "LS": (34, F), "LIM": (16, F), "SB": (256, B), "FI": (258, B), "XP": (256, H), "MK": (256, F), "QS": (256, F),
     "L1": (32, F), "L2": (32, F), "PR": (32, F), "NN": (32, F), "OT": (16, U), "NV": (256, B), "EV": (512, B),
     "R1": (8, F), "SP": (2, U), "F1": (16, B), "YO": (8, F), "DF": (8, F), "GD": (8, F),
@@ -43,7 +43,7 @@ A = AluOpType
 AF = ActivationFunctionType
 BIG = 12288.0
 OWN = 240
-FAR = 8192.0
+FAR = 16384.0
 
 
 def rank_program(g, core, T, topo):
@@ -242,8 +242,8 @@ def rank_program(g, core, T, topo):
     def starts2(t):
         ae = "AE%d" % t
         return [lambda: act(v("AX%d" % t, 0, 65), v(ae, 0, 65), AF.Identity, bias=256.0),
-                lambda: act(v("C2%d" % t), v("DE", 0, 64), AF.Identity, bias=col(B256), scale=-1.0),
-                lambda: act(v("A1%d" % t), v(ae, 1, 65), AF.Identity, bias=4096.0),
+                lambda: act(v("C2%d" % t), v(ae, 1, 65), AF.Identity, bias=col(B512), scale=-1.0),
+                lambda: act(v("A1%d" % t, 0, 65), v(ae, 0, 65), AF.Identity, bias=0.5, scale=1.0 / 8192.0),
                 lambda: act(v("AB%d" % t), v(ae, 1, 65), AF.Identity, bias=4096.0 - BIG)]
 
     def select(o, a, pat, op, fill, base, ch):
@@ -279,17 +279,19 @@ def rank_program(g, core, T, topo):
         lambda: cp(v("PF"), v("PRI")),
         lambda: cp(v("DTF", 0, 1), (T.DTI[:, 0:1], dti[1])),
         lambda: ts(col(BB1), col(PP), 512.0, A.mult, BIG, A.add),
-        lambda: ts(col(BO), col(PP), 512.0, A.mult, 256.0 - BIG, A.add),
-        lambda: ts(col(PCM), col(II), 512.0, A.mult, -2048.0, A.add),
+        lambda: ts(col(BO), col(PP), 512.0, A.mult, 4096.0 - BIG, A.add),
+        lambda: ts(col(PCM), col(II), -512.0, A.mult, 2048.0, A.add),
         lambda: ts(col(I64), col(II), 64.0, A.mult, -1024.0, A.add),
         lambda: ts(v("ZH", 0, 144), v("Z"), v("RM", 0, 1), A.mult),
         lambda: ts(v("ZH", 144, 288), v("Z"), v("RM", 0, 1), A.mult, -1.0, A.mult),
         lambda: ts(v("R0H"), v("ON"), v("RM", 0, 1), A.mult),
+        lambda: ts(v("R0N"), v("ON"), v("RM", 0, 1), A.mult, -1.0, A.mult),
+        lambda: ts(v("R02"), v("ON"), v("RM", 0, 1), A.mult, 2.0, A.mult),
         lambda: cp(v("ONH"), v("ON")),
         lambda: ms(v("HK", 256, 272), -2048.0),
         lambda: ms(v("HK", 528, 545), 512.0),
-        lambda: ts(v("TR", 0, 16), v("IL"), 2049.0, A.add, 1.0 / FAR, A.mult),
-        lambda: ts(v("TR", 16, 32), v("IL"), 2048.0, A.add, 1.0 / FAR, A.mult),
+        lambda: ts(v("TR", 0, 16), v("IL"), 8193.0, A.add, 1.0 / FAR, A.mult),
+        lambda: ts(v("TR", 16, 32), v("IL"), 4096.0, A.add, 1.0 / FAR, A.mult),
     ]
 
     def early_scalar():
@@ -299,32 +301,28 @@ def rank_program(g, core, T, topo):
         act(v("P21"), v("P21"), AF.Identity, scale=1024.0)
         act(v("K1"), v("IS", 0, 64), AF.Identity, bias=col(I64))
         act(v("RS"), v("MM"), AF.Sign)
-        for r in range(1, 16, 2):
-            zmake(r)
-        for nm, src, sc in (("O9", "ON", 512.0), ("O10", "ON", -1024.0), ("O11", "ON", 2048.0)):
+        act(v("C4"), v("IS"), AF.Identity, bias=4096.0, scale=0.0)
+        for nm, src, sc in (("O14", "ON", 16384.0), ("NI4", "NI", 4.0), ("O9", "ON", 4096.0), ("O10", "ON", -8192.0), ("O11", "ON", 2048.0)):
             act(v(nm), v(src), AF.Identity, scale=sc)
         act(v("DTF", 1, 512), v("DT", 1, 512), AF.Identity, bias=256.0)
 
-    def compare(j, us):
-        bank, e = ("B1", "E") if j == 0 else ("B0", "PX")
-        for u in us:
-            if u == 0:
-                mm(v(bank, 0, 256), v("ON"), v("ZR"), True, False)
+    def compare():
+        mm(v("B1", 0, 256), v("ON"), v("ZR"), True, False)
+        for u in range(16):
             e0 = 272 * u
-            keys = v("HK", 272 + 16 * u, 528) if j == 0 else v("XW", 16 * u, 256)
-            ts(v(e, e0, 256 * u + 256), keys, 1.0 / FAR, A.mult, v("PR", 16 * j + u, 16 * j + u + 1), A.is_equal)
-            mm(v(bank, 16 * u, 16 * u + 16), v("TRI"), v(e, e0, e0 + 16), False, u == 15)
+            ts(v("E", e0, 256 * u + 256), v("XW", 16 * u, 256), 1.0 / FAR, A.mult, v("NN", u, u + 1), A.is_equal)
+            mm(v("B1", 16 * u, 16 * u + 16), v("TRI"), v("E", e0, e0 + 16), False, u == 15)
             if u < 15:
-                mm(v(bank, 16 * u + 16, 256), v("ON"), v(e, e0 + 16, 256 * u + 256), False, False)
+                mm(v("B1", 16 * u + 16, 256), v("ON"), v("E", e0 + 16, 256 * u + 256), False, False)
 
-    def places(j, out):
-        a, b = 16 * j, 16 * j + 16
-        if j:
-            tt(v("MK"), v("B0", 0, 256), v("DM"), A.mult)
-            scan(v("QS"), v("RS"), v("MK"), 0.0, A.mult, A.add)
-        tt(v("L1", a, b), v("QS", 15, 256, 16) if j else v("B5", 0, 16), v("PR", a, b), A.add)
-        tt(v("L2", a, b), v("L1", a, b), v("TR", a, b), A.min)
-        ts(out, v("L2", a, b), FAR, A.mult, 2048.0, A.add)
+    def key_sum(bank, a, b):
+        mm(v(bank, a, b), v("R0H"), v("HK", a, b), True, False)
+        mm(v(bank, a, b), v("NI"), v("C4", a, b), False, False)
+        mm(v(bank, a, b), v("O14"), v("FI", 1 + a, 1 + b), False, True)
+
+    def key_wide(bank, a, b):
+        tt(v("DW", a, b), v(bank, a, b), v("HK", 272 + a, 272 + b), A.min)
+        ts(v("XW", a, b), v("DW", a, b), 6144.0, A.add)
 
     def differ(out, a, b, bank, later=False):
         k = out[1][0][2] - out[1][0][1]
@@ -340,7 +338,7 @@ def rank_program(g, core, T, topo):
         for a, b in ychunks:
             act(v("Y", 16 * a, 16 * b), ind(v("TX"), v("OY", a, b)), AF.Copy)
         off = 16 if nn == 64 else 0
-        c = nn - nn // 4
+        c = 40 if (t, nn) == (0, 64) else nn - nn // 4
         act(v("PX", 16 * c, 16 * nn), ind(pat, v("O1", c, nn)), AF.Copy)
         differ(v("NQ", 1024 + 16 * c, 1024 + 16 * nn), v("Y", off + 16 * c, off + 16 * nn), v("PX", 16 * c, 16 * nn), "B5")
         for a, b in ychunks:
@@ -368,22 +366,25 @@ def rank_program(g, core, T, topo):
         to = after if t else before
         if t:
             cp(indw(v("FN"), v("LB0")), v("LA0"))
+        if t == 0:
+            starts2(0)[0]()
+        mm(w(0, 65), v("IDF"), v("AX%d" % t, 0, 65), True, False)
         cp(v("WG", 0, 512), ind(tab, v(ow, 0, 32)))
         act(v("WG", 512, 1040), ind(tab, v(ow, 32, 65)), AF.Copy)
-        fold("B0", 0, 65, "WG", 0, pick)
+        fold("B0", 0, 65, "WG", 0, pick, False, True)
         if t == 0:
-            for f in starts2(0):
+            for f in starts2(0)[1:]:
                 f()
             for i in range(12, 16):
                 brmake(i)
             for f in early[:8]:
                 f()
-        tt(v("T1", 0, 65), w(0, 65), v("AX%d" % t, 0, 65), A.add)
-        ts(v("OY", 0, 65), v("T1", 0, 65), 0.0, A.max)
+        ts(v("OY", 0, 65), w(0, 65), 0.0, A.max)
         tt(v("T2", 0, 64), w(0, 64), v("C2%d" % t), A.add)
-        ts(v("O1"), w(1, 65), col(B256), A.add)
+        tt(v("T1", 0, 65), w(0, 65), v("AX%d" % t, 0, 65), A.subtract)
         ts(v("O2"), v("T2", 0, 64), 0.0, A.max)
-        ts(v("T3", 0, 65), w(0, 65), -255.5, A.is_lt, 100.0, A.mult)
+        ts(v("O1"), v("T1", 1, 65), col(B256), A.add)
+        ts(v("T3", 0, 65), v("T1", 0, 65), -255.5, A.is_lt, 100.0, A.mult)
         for i in range(16):
             mm(v("B%d" % (3 + i // 8), 64 * (i % 8), 64 * (i % 8) + 64), v("BR", 128 * i, 128 * i + 128), v("AE%d" % t, 1, 65))
         if t == 0:
@@ -403,30 +404,31 @@ def rank_program(g, core, T, topo):
         tt(v("BI"), v("BI"), v("P21"), A.add)
         idle(4)
         tt(v("OK"), v("B1", 0, 128), v("TH"), A.is_lt)
-        tt(v("AL"), v("OK", 0, 64), v("OK", 64, 128), A.mult)
-        tt(v("UB", 1, 65), v("AL"), v("A1%d" % t), A.mult)
-        scan(v("S1", 0, 65), v("UB", 0, 65), v("UB", 0, 65), 0.0, A.max, A.max)
+        tt(v("UB", 1, 65), v("OK", 0, 64), v("OK", 64, 128), A.mult)
+        ale, alo = v("UB", 1, 65, 2), v("UB", 2, 66, 2)
+        scan(v("S1", 0, 65), v("UB", 0, 65), v("A1%d" % t, 0, 65), 0.0, A.max, A.min)
         mm(v("B2", 0, 1), v("FC"), v("S1", 64, 65))
-        tt(v("UN"), v("AL"), v("AB%d" % t), A.mult)
+        tt(v("UN"), v("UB", 1, 65), v("AB%d" % t), A.mult)
         tt(v("M2"), v("UN", 0, 64, 2), v("UN", 1, 64, 2), A.min)
-        ts(v("PV"), v("S1", 0, 64, 2), v("B2", 0, 1), A.max)
+        ts(v("PV"), v("S1", 0, 64, 2), v("B2", 0, 1), A.max, 8192.0, A.mult)
+        act(v("PVX"), v("PV"), AF.Identity, bias=-3840.0)
+        mm(w(0, 32), v("IDF"), v("PVX"), True, False)
         tt(v("DD"), v("M2"), v("PV"), A.subtract)
         ts(v("OW2"), v("DD"), 512.0 - BIG, A.min, col(BB1) if t else BIG, A.add)
         act(v("WG", 256, 512), ind(tab, v("OW2", 16, 32)), AF.Copy)
         cp(v("WG", 0, 256), ind(tab, v("OW2", 0, 16)))
-        fold("B0", 0, 32, "WG", 0, pick)
-        ts(v("PVX"), v("PV"), -3840.0, A.add)
-        ts(v("C2B"), v("DD"), -1.0, A.mult, col(BO), A.add)
+        fold("B0", 0, 32, "WG", 0, pick, False, True)
+        ts(v("C2B"), v("M2"), -1.0, A.mult, col(BO), A.add)
         ts(v("EB", 0, 32), v("M2"), -0.5, A.is_gt)
-        ts(v("AO1"), v("AL", 1, 64, 2), 1.0, A.add)
-        ts(v("NE"), v("AL", 0, 64, 2), -1.0, A.mult, 1.0, A.add)
+        ts(v("AO1"), alo, 1.0, A.add)
+        ts(v("NE"), ale, -1.0, A.mult, 1.0, A.add)
         idle(5)
-        tt(v("T1", 0, 32), w(0, 32), v("PVX"), A.add)
-        ts(v("OY", 0, 32), v("T1", 0, 32), 0.0, A.max)
+        ts(v("OY", 0, 32), w(0, 32), 0.0, A.max)
         tt(v("T2", 0, 32), w(0, 32), v("C2B"), A.add)
-        ts(v("O1", 0, 32), w(0, 32), col(B256), A.add)
+        tt(v("T1", 0, 32), w(0, 32), v("PVX"), A.subtract)
         ts(v("O2", 0, 32), v("T2", 0, 32), 0.0, A.max)
-        ts(v("T3", 0, 32), w(0, 32), -255.5, A.is_lt, 100.0, A.mult)
+        ts(v("O1", 0, 32), v("T1", 0, 32), col(B256), A.add)
+        ts(v("T3", 0, 32), v("T1", 0, 32), -255.5, A.is_lt, 100.0, A.mult)
         duel(t, 32, [(0, 8), (8, 20), (20, 32)])
         for i in range(16):
             act(v("VT", i, 1024, 16), v("B%d" % (3 + i // 8), 64 * (i % 8), 64 * (i % 8) + 64), AF.Identity, bias=v("BI", i // 2, i // 2 + 1))
@@ -437,10 +439,10 @@ def rank_program(g, core, T, topo):
         scan(rv("SR", 32, 0), rv("EB", 32, 0), rv("KB", 64, 32), 0.0, A.mult, A.add)
         mm(v("B2", 0, 1), v("BC"), v("SR", 0, 1))
         kj = v("KB", 0, 32)
-        tt(v("T1", 0, 32), v("AL", 0, 64, 2), kj, A.subtract)
+        tt(v("T1", 0, 32), ale, kj, A.subtract)
         tt(v("T2", 0, 32), v("NE"), kj, A.mult)
         tt(v("AEV"), v("T1", 0, 32), v("AO1"), A.mult)
-        tt(v("AOD"), v("AL", 1, 64, 2), v("T2", 0, 32), A.subtract)
+        tt(v("AOD"), alo, v("T2", 0, 32), A.subtract)
         scan(rv("SQ", 32, 1), rv("EB", 32, 1), rv("KB", 64, 33), v("B2", 0, 1), A.mult, A.add)
         tt(v("AL2", 0, 64, 2), v("AEV"), v("SQ", 1, 33), A.is_gt)
         tt(v("AL2", 1, 64, 2), v("AOD"), v("SQ", 1, 33), A.is_gt)
@@ -470,10 +472,11 @@ def rank_program(g, core, T, topo):
         ts(v("HK", 0, 256), v("W2"), -2048.0, A.add)
         tt(v("HK", 272, 528), v("W4"), v("HK", 544, 800), A.add)
         fold("B0", 0, 33, "HK", 0, zh(0))
-        fold("B0", 40, 16, "HK", 272, zh(0), True, False)
-        fold("B0", 40, 16, "HK", 271, zh(1), False, False)
-        fold("B0", 40, 16, "HK", 543, zh(0), False, True)
-        mm(v("B7", 0, 256), v("R0H"), v("HK", 0, 256))
+        fold("B0", 40, 16, "HK", 271, zh(0), True, False)
+        fold("B0", 40, 16, "HK", 543, zh(1), False, False)
+        fold("B0", 40, 16, "HK", 544, zh(1), False, True)
+        mm(w(256, 512), v("R0H"), v("HK", 272, 528), True, False)
+        mm(w(256, 512), v("R0N"), v("HK", 544, 800), False, True)
         for j, (a, b) in enumerate(chunks):
             tt(v("NQ", 16 * a, 16 * b), ind(v("TX"), v("TO16", a, b)), v("PX", 16 * a, 16 * b), A.not_equal)
             if j == 0:
@@ -486,61 +489,70 @@ def rank_program(g, core, T, topo):
                 mm(v("B5", 0, 192), v("WF"), v("SB", 0, 192))
                 rest()
         act(v("SB", 192, 256), v("B4", 192, 256), AF.Sign, bias=-6.5)
-        ts(v("W3"), v("W1"), 511, A.bitwise_and)
-        ts(v("NM"), v("W4"), col(PCM), A.not_equal, 2048.0, A.mult)
         ts(v("ACT"), v("IL"), v("TOT", 0, 1), A.is_ge, 5000.0, A.mult)
+        ts(v("L1", 0, 16), v("ACT"), 7680.0, A.add)
         for (a, b), gb, qb in (((0, 192), "B5", "B6"), ((192, 256), "B2", "B4")):
             if a:
                 mm(v(gb, a, b), v("WF"), v("SB", a, b))
             ts(v("FI", 1 + a, 1 + b), v(gb, a, b), col(II), A.is_gt)
-            tt(v("XP", a, b), v("FI", 1 + a, 1 + b), v("W3", a, b), A.mult)
+            tt(v("XP", a, b), v("FI", 1 + a, 1 + b), v("W1", a, b), A.mult)
             q = v(qb, a, b)
             mm(q, v("O10"), v("FI", 1 + a, 1 + b), True, False)
             mm(q, v("O9"), v("FI", a, b), False, False)
             mm(q, v("ONH"), v("XP", a, b), False, True)
             if a == 0:
-                ts(v("LS", 0, 33), w(0, 33), 1.0 / FAR, A.mult)
-                ts(v("L1", 0, 16), w(40, 56), -1.0, A.mult, -512.0, A.add)
-                tt(v("LIM"), v("L1", 0, 16), v("ACT"), A.subtract)
+                key_sum("B7", 0, 192)
+                ts(v("LS", 0, 16), w(17, 33), 6144.0, A.add, 1.0 / FAR, A.mult)
+                ts(v("LS", 16, 32), w(0, 16), 2048.0, A.add, 1.0 / FAR, A.mult)
+                tt(v("LIM"), w(40, 56), v("L1", 0, 16), A.subtract)
             else:
-                cp(v("XW"), v("B7", 0, 256))
+                key_sum("B5", 192, 256)
+                key_wide("B7", 0, 192)
             tt(v("MK", a, b), q, v("DM", a, b), A.mult)
             scan(v("QS", a, b), v("RS", a, b), v("MK", a, b), 0.0, A.mult, A.add)
+        act(v("NM"), w(256, 512), AF.Abs, bias=col(PCM))
         mm(v("B3", 0, 256), v("ONH"), v("XP"), True, False)
-        mm(v("B3", 0, 256), v("R0H"), v("HK", 544, 800), False, True)
+        mm(v("B3", 0, 256), v("R0N"), v("HK", 272, 528), False, False)
+        mm(v("B3", 0, 256), v("R02"), v("HK", 544, 800), False, True)
         act(v("MA%d" % t), v("B3", 0, 256), AF.Identity, bias=-256.0)
         send(to, "aa%d" % t, "LA%d" % t, v("MA%d" % t))
         sc = v("B7", 256, 512)
         mm(sc, v("NI"), v("ISB"), True, False)
-        mm(sc, v("NI"), v("NM"), False, False)
+        mm(sc, v("NI4"), v("NM"), False, False)
         mm(sc, v("O11"), v("FI", 1, 257), False, True)
         q = v("QS", 15, 256, 16)
         tt(v("NN", 0, 16), q, v("LIM"), A.is_ge)
         tt(v("NN", 16, 32), q, v("ACT"), A.is_lt)
-        tt(v("PR", 0, 16), v("NN", 0, 16), v("LS", 17, 33), A.add)
-        tt(v("PR", 16, 32), v("NN", 16, 32), v("LS", 0, 16), A.add)
-        compare(0, range(16))
-        act(v("EV", 0, 256), v("B1", 0, 256), AF.Identity)
-        compare(1, range(4))
-        fold("B5", 0, 16, "EV", 0, zown)
-        compare(1, range(4, 16))
-        places(0, v("MB%d" % t))
-        send(to, "ab%d" % t, "LB%d" % t, v("MB%d" % t))
+        tt(v("DW", 192, 256), v("B5", 192, 256), v("HK", 464, 528), A.min)
+        tt(v("PR"), v("NN"), v("LS", 0, 32), A.add)
+        ts(v("XW", 192, 256), v("DW", 192, 256), 6144.0, A.add)
+        tt(v("NN", 0, 16), v("PR", 0, 16), v("PR", 16, 32), A.min)
+        compare()
         note("v", lambda: g.vector.tensor_reduce(T.R1[:, 0:1], sc[0], AxisListType.X, A.max), [sc], [r1(0)])
+        tt(v("MK"), v("B1", 0, 256), v("DM"), A.mult)
         ts(r1(1), r1(0), v("TOT", 1, 2), A.is_gt)
+        scan(v("QS"), v("RS"), v("MK"), 0.0, A.mult, A.add)
         ts(r1(2), r1(0), -1.0, A.mult, 2049.0 - 257.0, A.add)
+        tt(v("L1", 16, 32), q, v("PR", 16, 32), A.add)
+        tt(v("L1", 0, 16), q, v("PR", 0, 16), A.add)
+        tt(v("L2"), v("L1"), v("TR"), A.min)
         ts(v("SP", 0, 1), r1(2), r1(1), A.mult, 257.0, A.add)
-        places(1, v("OT"))
+        ts(v("MB%d" % t), v("L2", 0, 16), FAR, A.mult, -4096.0, A.add)
+        send(to, "ab%d" % t, "LB%d" % t, v("MB%d" % t))
+        ts(v("OT"), v("L2", 16, 32), FAR, A.mult)
         act(v("NV"), ind(v("TX"), v("OT")), AF.Identity, bias=255.0, scale=-1.0)
         cp(v("F1"), ind(v("FI"), v("SP", 0, 1)))
         mm(v("B2", 0, 8), v("TGE"), v("F1", 0, 8))
         tt(v("YO"), v("F1", 0, 8), pf, A.mult)
         mm(v("B2", 8, 16), v("IDF"), pf, True, False)
         mm(v("B2", 8, 16), v("R0C"), v("YO"), False, True)
+        if t == 0:
+            cp(indw(v("TX"), v("OT")), v("NV"))
         tt(v("GD"), v("B2", 0, 8), v("DF"), A.mult)
         tt(v("MC%d" % t), v("B2", 8, 16), v("GD"), A.add)
         send(to, "ac%d" % t, "LC%d" % t, v("MC%d" % t))
-        cp(indw(v("TX"), v("OT")), v("NV"))
+        if t:
+            cp(indw(v("TX"), v("OT")), v("NV"))
         if t:
             dma("y", "dyt", hb(T.yt[:]), v("TX", 0, 4096))
             own_witnesses(v("MA0"), v("MB0"))

@@ -3,47 +3,54 @@ from concourse.mybir import dt, AluOpType, AxisListType, ActivationFunctionType
 
 F, B, I, U, H = "float32", "bfloat16", "int32", "uint16", "float16"
 _SB = {
-    "TX": (4352, B), "PA0": (4096, B), "PA1": (4096, B), "FN": (4360, B), "FO": (4360, F),
+    "TX": (4368, B), "PA0": (4112, B), "PA1": (4112, B), "FN": (4240, B), "FO": (4240, F), "VS": (5136, B),
     "DTI": (512, I), "DT": (520, B), "DN": (520, B), "DTF": (512, F), "CD": (128, I), "PRI": (8, I), "PF": (8, F),
-    "KI": (8, I), "CL": (24, F), "RM": (16, F), "IS": (256, F), "GM": (128, F), "MM": (256, F),
-    "Z": (144, B), "ZP": (16 * 144, B), "ZH": (288, H), "R0H": (128, H), "R0N": (128, H), "R02": (128, H), "NI4": (128, B), "BR": (2048, F),
-    "ON": (128, B), "TRI": (128, B), "TGE": (128, B), "WF": (128, B), "IDF": (128, F), "UP": (128, F), "FC": (128, F),
-    "BC": (128, B), "SW": (128, F), "SD": (128, F), "R0C": (128, F), "TM": (128, F),
-    "ONH": (128, H), "NI": (128, B), "IDB": (128, B), "O9": (128, B), "O10": (128, B), "O11": (128, B), "ISB": (256, B),
-    "DM": (256, B), "RS": (256, B), "ZR": (256, B), "K1": (64, F), "NEG1": (64, F), "IL": (16, F), "TR": (32, F),
-    "P21": (8, F), "XT": (128, F), "YT": (128, F),
-    "AE0": (66, F), "AE1": (66, F), "DE": (66, F), "OW0": (66, U), "OW1": (66, U), "AX0": (66, F), "AX1": (66, F),
-    "C20": (64, F), "C21": (64, F), "A10": (66, F), "A11": (66, F), "AB0": (64, F), "AB1": (64, F),
-    "WG": (1040, B), "Y": (1040, B), "NQ": (4096, B), "PX": (4096, B), "E": (4096, B),
-    "T1": (66, F), "T2": (66, F), "T3": (66, F), "OY": (66, U), "O1": (64, U), "O2": (64, U), "TH": (128, F), "OK": (128, F),
-    "AL": (64, F), "UB": (66, F), "S1": (66, F), "UN": (64, F), "M2": (32, F), "PV": (32, F), "DD": (32, F), "OW2": (32, U),
-    "PVX": (32, F), "C2B": (32, F), "KB": (66, F), "EB": (34, F), "SR": (34, B), "SQ": (34, F), "AO1": (32, F), "NE": (32, F),
-    "AEV": (32, F), "AOD": (32, F), "AL2": (64, F), "LOC": (64, B), "OC": (64, U), "TOT": (2, F), "ACT": (16, F),
-    "BI": (8, F), "VT": (1024, F), "VS": (1024, I), "W1": (256, I), "W2": (256, I), "W4": (256, I),
-    "PO16": (256, U), "TO16": (256, U), "DW": (256, F), "HK": (800, H), "XW": (256, U), "C4": (256, B), "O14": (128, B), "NM": (256, B),
-    "LS": (34, F), "LIM": (16, F), "SB": (256, B), "FI": (258, B), "XP": (256, H), "MK": (256, F), "QS": (256, F),
-    "L1": (32, F), "L2": (32, F), "PR": (32, F), "NN": (32, F), "OT": (16, U), "NV": (256, B), "EV": (512, B),
-    "R1": (8, F), "SP": (2, U), "F1": (16, B), "YO": (8, F), "DF": (8, F), "GD": (8, F),
-    "MA0": (256, F), "MA1": (256, F), "MB0": (16, U), "MB1": (16, U), "MC0": (8, F), "MC1": (8, F),
-    "LA0": (256, F), "LA1": (256, F), "LB0": (16, U), "LB1": (16, U), "LC0": (8, F), "LC1": (8, F),
+    "KI": (8, I), "KF": (18, F), "CL": (40, F), "RM": (16, F), "RP": (8, F), "IS": (256, F), "GM": (128, F), "MM": (256, F),
+    "ID": (160, B), "SH": (128, B), "WR": (128, B), "Z": (144, B), "ZW": (144, B), "ZP": (8 * 144, B), "ZA": (288, B), "Z64": (144, B),
+    "VM": (8 * 130, B), "ON": (128, B), "TM": (128, F), "FC": (128, F), "BC": (128, B), "IDF": (128, F), "SD": (128, F), "R0C": (128, F),
+    "TRI": (128, B), "TRO": (128, B), "TGE": (128, B), "O8K": (128, B), "N8": (128, B), "T8K": (128, B), "G8": (128, B), "OH": (128, B),
+    "I8": (128, B), "NI": (128, B), "NA": (128, B), "NB": (128, B), "O16": (128, B), "N16": (128, B), "RA": (128, B), "RB": (128, B),
+    "PQ4": (128, B), "PMA": (128, B), "PMB": (128, B), "INA": (128, B), "PCH": (128, B), "ISB": (256, B), "DM": (256, B), "RS": (256, B),
+    "TRM": (256, F), "JK": (32, F), "XO": (8, U),
+    "AH": (130, H), "NAH": (130, H), "HI": (128, I), "LO": (128, I), "HB": (128, B), "LB": (128, B), "C1": (128, F), "C2": (128, F),
+    "OW0": (64, U), "OW1": (64, U), "VT0": (512, B), "VT1": (512, B), "A10": (64, F), "A11": (64, F), "AB0": (64, F), "AB1": (64, F),
+    "WG": (1024, B), "Y": (1024, B), "NJ": (1040, B), "N2": (528, B), "NQ": (4096, B), "PX": (4096, B), "E": (4096, B), "EV": (512, B),
+    "T1": (64, F), "T2": (64, F), "T3": (64, F), "T4": (64, F), "T5": (32, F), "T6": (32, F), "T7": (32, F), "OY": (64, U), "O1": (64, U), "O2": (64, U), "TH": (64, F),
+    "UB": (64, F), "S1": (66, F), "UN": (64, F), "M2": (32, F), "PV": (32, F), "DD": (32, F), "OW2": (32, U), "C2B": (32, F),
+    "EB": (34, F), "AO1": (32, F), "NE": (32, F), "O65": (32, F), "KJ": (32, F), "AEV": (32, F), "AOD": (32, F),
+    "SR": (32, B), "SQ": (34, F), "EE": (34, B), "OO": (34, B), "CC": (34, B), "OC": (32, U), "ST": (258, B),
+    "OX0": (128, H), "OTM": (128, H), "O0M": (128, H), "PO16": (256, U), "TO16": (256, U), "XH": (258, H), "XL": (16, F), "OX": (16, U),
+    "GT": (256, B), "SB": (258, B), "FI": (258, B), "R2": (256, H), "R1": (256, F), "XW": (128, H), "NN": (128, B),
+    "MK": (256, F), "QS": (256, F), "MK2": (128, F), "QS2": (128, F), "OT": (16, U), "NV": (256, B),
+    "R0": (8, F), "SP": (2, U), "F1": (16, B), "YO": (8, F), "DF": (8, F), "GD": (8, F),
+    "MA0": (128, F), "MA1": (128, F), "MB0": (8, U), "MB1": (8, U), "MC0": (8, F), "MC1": (8, F),
+    "LA0": (128, F), "LA1": (128, F), "LB0": (8, U), "LB1": (8, U), "LC0": (8, F), "LC1": (8, F),
 }
 _AT = {}
 for _k, (_n, _d) in _SB.items():
-    if _d == F and _n <= 66 and _k[:2] not in ("MC", "LC", "R1") and _k not in ("AE0", "AE1"):
+    if _d == F and _n <= 66 and _k[:2] not in ("MC", "LC"):
         _AT[_k] = 72 * len(_AT)
-SCRATCH = {k: ("sbuf", [128, n], d) for k, (n, d) in _SB.items() if k not in _AT}
+_BT = {}
+for _k, (_n, _d) in _SB.items():
+    if _d == B and _n == 128:
+        _BT[_k] = 128 * len(_BT)
+SCRATCH = {k: ("sbuf", [128, n], d) for k, (n, d) in _SB.items() if k not in _AT and k not in _BT}
 SCRATCH["POOL"] = ("sbuf", [128, 72 * len(_AT)], F)
+SCRATCH["MATS"] = ("sbuf", [128, 128 * len(_BT)], B)
 for _b in range(8):
     SCRATCH["B%d" % _b] = ("psum", [128, 512], F)
-_DMAS = ["dcd", "dpr", "dw0", "dw1", "dtx", "dpa", "dfo", "dfn", "dyt", "dyw", "dyo"]
+_DMAS = ["dcd", "dpr", "dw0", "dw1", "dtx", "dp0", "dp1", "dp2", "dp3", "dfo", "dn0", "dn1", "dyt", "dyw", "dyo"]
 _ARR = ["apa", "adn", "aa0", "ab0", "ac0", "aa1", "ab1", "ac1"]
 SEMAPHORES = ["cv", "cs", "ct", "cg", "sent"] + _DMAS + _ARR
 
 A = AluOpType
 AF = ActivationFunctionType
 BIG = 12288.0
+GATHER, SCATTER, FIX, WAKE, TENSOR = 1.5, 3.5, 50, 70, 0.5
+PASSES, _PLAN = 8, []
 OWN = 240
-FAR = 16384.0
+GATE = 8192.0
+RY, RZ, RJ = 1536, 2560, 3584
 
 
 def rank_program(g, core, T, topo):
@@ -53,19 +60,27 @@ def rank_program(g, core, T, topo):
     n = len(T.cores)
     before, after = T.cores[(rank - 1) % n], T.cores[(rank + 1) % n]
     eng = {"v": g.vector, "s": g.scalar, "t": g.tensor, "g": g, "y": g.sync}
-    ops, acc = [], {}
+    ops, acc, banks, last, loose = [], {}, {}, {}, []
+
+    def anywhere(f, *a, **k):
+        loose.append(1)
+        f(*a, **k)
+        loose.pop()
+
+    def home(name):
+        return (T.POOL, _AT[name]) if name in _AT else (T.MATS, _BT[name]) if name in _BT else (T[name], 0)
 
     def v(name, a=0, b=None, step=1):
         b = _SB[name][0] if b is None else b
-        t, o = (T.POOL, _AT[name]) if name in _AT else (T[name], 0)
+        t, o = home(name)
         return (t[:, o + a:o + b:step] if step != 1 else t[:, o + a:o + b], [(name, a, b, step)])
 
     def rv(name, hi, lo):
-        t, o = (T.POOL, _AT[name]) if name in _AT else (T[name], 0)
+        t, o = home(name)
         return (t[:, o + hi::-1] if o + lo == 0 else t[:, o + hi:o + lo - 1:-1], [(name, lo, hi + 1)])
 
     def ind(win, off):
-        return (win[0].indirect(off[0]), win[1] + off[1])
+        return (win[0].indirect(off[0]), win[1] + off[1], [])
 
     def indw(win, off):
         return (win[0].indirect(off[0]), win[1], off[1])
@@ -76,44 +91,70 @@ def rank_program(g, core, T, topo):
     def ap(x):
         return x[0] if isinstance(x, tuple) else x
 
-    def note(q, fn, reads, writes, sem=None, inc=1):
+    def size(x):
+        name, lo, hi, st = (x[1][0] + (1,))[:4]
+        return (hi - lo + st - 1) // st, 4 if name not in _SB or _SB[name][1] in (F, I) else 2, name not in _SB
+
+    def cycles(o, ins, both=1.0):
+        if len(o) > 2:
+            return FIX + SCATTER * size(ins[0])[0]
+        if ins and len(ins[0]) > 2:
+            return FIX + GATHER * size(o)[0]
+        if both == 2.0:
+            return max(64, size(o)[0] * (1 if any(size(x)[2] for x in ins) else 2))
+        return max(64, size((ins or [o])[0])[0] * (both if all(size(x)[1] == 2 for x in ins + [o]) else 1))
+
+    def note(q, fn, reads, writes, sem=None, inc=1, cost=64, late=0):
         k = len(ops)
-        deps = set()
+        deps, behind = set(), set()
         rs = [r for x in reads if isinstance(x, tuple) for r in x[1]] + [r for x in writes if len(x) > 2 for r in x[2]]
         ws = [r for x in writes for r in x[1]]
         for lst, isw in ((rs, False), (ws, True)):
             for r in lst:
                 name, lo, hi, st = (r + (1,))[:4]
-                bank = name not in _SB
-                for lo2, hi2, st2, w2, k2 in acc.get(name, []):
-                    same = ops[k2]["q"] == q and ops[k2]["own"] and sem is None
-                    if bank and not same:
+                if name not in _SB:
+                    who, now, past = banks.setdefault(name, [q, [], []])
+                    if who != q:
+                        now, past = [], now
+                    if q == "t":
+                        behind.update(now)
+                        now = []
+                    deps.update(past)
+                    banks[name] = [q, now + [k], past]
+                    continue
+                for lo2, hi2, st2, k2 in acc.get((name, True), []) + (acc.get((name, False), []) if isw else []):
+                    if lo < hi2 and lo2 < hi and not (st == st2 and (lo - lo2) % st):
                         deps.add(k2)
-                    elif lo < hi2 and lo2 < hi and (w2 or isw) and not (st == st2 and (lo - lo2) % st):
-                        if not same or (w2 and q != "t"):
-                            deps.add(k2)
+        deps.discard(k)
+        if any(isinstance(x, tuple) and len(x) > 2 for x in reads[:1] + writes) and not loose:
+            if q in last:
+                behind.add(last[q])
+            last[q] = k
         for lst, isw in ((rs, False), (ws, True)):
             for r in lst:
-                acc.setdefault(r[0], []).append((r[1], r[2], (r + (1,))[3], isw, k))
-        ops.append({"q": q, "fn": fn, "deps": deps, "sem": sem or ("c" + q), "inc": inc, "own": sem is None})
+                acc.setdefault((r[0], isw), []).append((r[1], r[2], (r + (1,))[3], k))
+        ops.append({"q": q, "fn": fn, "deps": deps, "behind": behind, "sem": sem or ("c" + q), "inc": inc, "cost": cost, "late": late})
 
     def tt(o, a, b, op):
-        note("v", lambda: g.vector.tensor_tensor(o[0], a[0], b[0], op), [a, b], [o])
+        note("v", lambda: g.vector.tensor_tensor(o[0], a[0], b[0], op), [a, b], [o], cost=cycles(o, [a, b], 2.0))
 
     def ts(o, a, s1, op0, s2=None, op1=None):
         if op1 is None:
-            note("v", lambda: g.vector.tensor_scalar(o[0], a[0], ap(s1), None, op0), [a, s1], [o])
+            note("v", lambda: g.vector.tensor_scalar(o[0], a[0], ap(s1), None, op0), [a, s1], [o], cost=cycles(o, [a], 0.5))
         else:
-            note("v", lambda: g.vector.tensor_scalar(o[0], a[0], ap(s1), ap(s2), op0, op1), [a, s1, s2], [o])
+            note("v", lambda: g.vector.tensor_scalar(o[0], a[0], ap(s1), ap(s2), op0, op1), [a, s1, s2], [o], cost=cycles(o, [a], 0.5))
 
     def cp(o, a):
-        note("v", lambda: g.vector.tensor_copy(o[0], a[0]), [a], [o])
+        note("v", lambda: g.vector.tensor_copy(o[0], a[0]), [a], [o], cost=cycles(o, [a], 0.5))
 
     def ms(o, c):
-        note("v", lambda: g.vector.memset(o[0], c), [], [o])
+        note("v", lambda: g.vector.memset(o[0], c), [], [o], cost=cycles(o, [], 0.5))
 
     def scan(o, a, b, init, op0, op1):
-        note("v", lambda: g.vector.tensor_tensor_scan(o[0], a[0], b[0], ap(init), op0, op1), [a, b, init], [o])
+        note("v", lambda: g.vector.tensor_tensor_scan(o[0], a[0], b[0], ap(init), op0, op1), [a, b, init], [o], cost=cycles(o, [a, b], 0.5))
+
+    def reduce(o, a, op, negate=False):
+        note("v", lambda: g.vector.tensor_reduce(o[0], a[0], AxisListType.X, op, negate=negate), [a], [o], cost=cycles(o, [a]))
 
     def act(o, a, func, bias=None, scale=None):
         kw = {}
@@ -121,450 +162,532 @@ def rank_program(g, core, T, topo):
             kw["bias"] = ap(bias)
         if scale is not None:
             kw["scale"] = ap(scale)
-        note("s", lambda: g.scalar.activation(o[0], a[0], func, **kw), [a, bias, scale], [o])
+        note("s", lambda: g.scalar.activation(o[0], a[0], func, **kw), [a, bias, scale], [o], cost=cycles(o, [a]))
 
     def mm(o, l, r, start=True, stop=True):
-        note("t", lambda: g.tensor.matmul(o[0], l[0], r[0], start, stop), [l, r], [o])
+        note("t", lambda: g.tensor.matmul(o[0], l[0], r[0], start, stop), [l, r], [o],
+             cost=TENSOR * max(64, size(r)[0]) * (4 if size(r)[1] == 4 else 1))
+
+    def msum(o, terms, start=True, stop=True):
+        for j, (l, r) in enumerate(terms):
+            mm(o, l, r, start and j == 0, stop and j == len(terms) - 1)
 
     def iota(o, pat, base, ch, flag=True):
         if flag:
-            note("g", lambda: g.iota(o[0], pat, base, ch, allow_small_or_imprecise_dtypes=True), [], [o])
+            note("g", lambda: g.iota(o[0], pat, base, ch, allow_small_or_imprecise_dtypes=True), [], [o], cost=160 + 2 * size(o)[0])
         else:
-            note("g", lambda: g.iota(o[0], pat, base, ch), [], [o])
+            note("g", lambda: g.iota(o[0], pat, base, ch), [], [o], cost=160 + 2 * size(o)[0])
 
-    def dma(q, sem, o, a):
-        note(q, lambda: eng[q].dma_start(o[0], a[0]), [a], [o], sem=sem, inc=16)
+    def select(o, a, pat, op, fill, base, ch):
+        note("g", lambda: g.affine_select(o[0], a[0], pat, op, fill, base, ch), [a], [o], cost=200 + 2 * size(o)[0])
 
-    def send(dst, sem, land, src):
+    def dma(q, sem, o, a, late=2000):
+        note(q, lambda: eng[q].dma_start(o[0], a[0]), [a], [o], sem=sem, inc=16, late=late)
+
+    def send(dst, src_core, sem, land, src, late=2200):
         rid, pid, _se = topo.addr(dst)
         note("g", lambda: g.remote_dma(T[land][:], src[0], T.sem[sem], T.sem.sent, pid, rid, topo.mask(core, dst)),
-             [src], [], sem="sent", inc=len(topo.engines(core, dst)))
+             [src], [], sem="sent", inc=len(topo.engines(core, dst)), cost=100)
+        note(None, None, [], [v(land)], sem=sem, inc=len(topo.engines(src_core, core)), cost=0, late=late)
+        ops[-1]["behind"].add(len(ops) - 2)
 
-    def arrive(src, sem, land):
-        note(None, None, [], [v(land)], sem=sem, inc=len(topo.engines(src, core)))
+    def to_row(buf, at=0):
+        return lambda i: v(buf, at + 15 - i, at + 143 - i)
+
+    zall = to_row("Z")
 
     def fold(bank, c0, nn, buf, b0, left, first=True, last=True):
         for i in range(16):
             mm(v(bank, c0, c0 + nn), left(i), v(buf, b0 + i, b0 + i + 16 * nn - 15, 16), first and i == 0, last and i == 15)
 
-    def zall(i):
-        return v("Z", 15 - i, 143 - i)
-
-    def zof(r):
-        return lambda i: v("ZP", 144 * r(i) + 15 - i, 144 * r(i) + 143 - i)
-
-    zpat, zrow, zown = zof(lambda i: i - i % 2), zof(lambda i: 0), zof(lambda i: i)
-
-    def zh(sign):
-        return lambda i: v("ZH", 144 * sign + 15 - i, 144 * sign + 143 - i)
-
-    spare = []
-
-    def idle(k):
-        for _ in range(min(k, len(spare))):
-            spare.pop(0)()
-
     def hb(x):
         return (x, [])
 
-    dma("y", "dcd", v("CD"), hb(T.cd[:]))
-    dma("s", "dw0", (T.DTI[0:128:2, :], [("DTI", 0, 512)]), hb(T.wit[:]))
-    dma("y", "dw1", (T.DTI[1:128:2, :], [("DTI", 1000, 1001)]), hb(T.wit[:]))
-    dma("s", "dpr", v("PRI"), hb(T.prb[:]))
-    dma("y", "dtx", v("TX", 0, 4096), hb(T.txt[:]))
-    dma("y", "dpa", v("PA0"), hb(T.pat[:]))
-    for sem, land in (("apa", "PA1"), ("adn", "DN"), ("aa0", "LA0"), ("ab0", "LB0"), ("ac0", "LC0")):
-        arrive(after, sem, land)
-    for sem, land in (("aa1", "LA1"), ("ab1", "LB1"), ("ac1", "LC1")):
-        arrive(before, sem, land)
+    dma("y", "dcd", v("CD"), hb(T.cd[:]), 2000)
+    dma("s", "dw0", (T.DTI[0:128:2, :], [("DTI", 0, 512)]), hb(T.wit[:]), 2300)
+    dma("y", "dw1", (T.DTI[1:128:2, :], [("DTI", 1000, 1001)]), hb(T.wit[:]), 2500)
+    dma("s", "dpr", v("PRI"), hb(T.prb[:]), 2500)
+    dma("y", "dtx", v("TX", 16, 4112), hb(T.txt[:]), 4800)
+    for k in range(4):
+        dma("y", "dp%d" % k, v("PA0", 16 + 1024 * k, 1040 + 1024 * k), hb(T.pat[:, 1024 * k:1024 * k + 1024]), 5400 + 600 * k)
+    for k in range(1, len(ops)):
+        ops[k]["behind"].add(k - 1)
 
-    K, II, G16, ODD, PP, GG, GC, EVEN, NGG, NEG, POS, B256, B512, BB1, BO, PCM, I64 = range(17)
+    (K, II, G16, ODD, PP, GC, EVEN, NE0, MINC, ADDC, WW, C15, SGN, CA, CB, P4, CO1, CBO, BB1, HC, NII, MAB, CMA, CMB, CIN, CJK) = range(26)
     iota(v("KI", 0, 1), [[0, 1]], 0, 1, False)
     iota(v("IS"), [[1, 256]], 0, 0)
+    iota(v("KF"), [[1, 18]], -1, 1)
     iota(v("GM"), [[1, 8], [0, 16]], 0, 0)
+    iota(v("PCH"), [[0, 2], [512, 8], [0, 8]], 272, 0)
     iota(v("MM"), [[0, 16], [1, 16]], 0, 0)
-    iota(v("P21"), [[2048, 8]], -8192, 0)
-    ms(v("DT", 0, 1), -256.0)
-    ms(v("DT", 512, 520), -256.0)
-    ms(v("TX", 4096, 4352), 0.0)
+    iota(v("ISB"), [[1, 256]], 0, 0)
+    for o, c in ((v("DT", 0, 1), -1.0), (v("DT", 512, 520), -1.0), (v("TX", 0, 16), 0.0), (v("PA0", 0, 16), 0.0),
+                 (v("AH", 128, 130), 0.0), (v("NAH", 128, 130), 0.0)):
+        ms(o, c)
     k0 = v("KI", 0, 1)
     ts(v("KI", II, II + 1), k0, 15, A.bitwise_and)
     ts(v("KI", G16, G16 + 1), k0, 112, A.bitwise_and)
     ts(v("KI", ODD, ODD + 1), k0, 1, A.bitwise_and)
     ts(v("KI", PP, PP + 1), k0, 1, A.arith_shift_right, 7, A.bitwise_and)
-    ts(v("KI", GG, GG + 1), k0, 4, A.arith_shift_right, 1, A.bitwise_and)
     ts(v("KI", GC, GC + 1), k0, 4, A.arith_shift_right)
-    cp(v("CL", 0, 7), v("KI", 0, 7))
-    ts(col(EVEN), col(ODD), -1.0, A.mult, 1.0, A.add)
-    ts(col(NGG), col(GG), -1.0, A.mult, 1.0, A.add)
-    ts(col(NEG), col(ODD), 10000.0, A.mult, -10000.0, A.add)
-    ts(col(POS), col(ODD), 10000.0, A.mult)
-    ts(col(B256), col(PP), 512.0, A.mult, 256.0, A.add)
-    ts(col(B512), col(PP), 512.0, A.mult)
-    i128 = v("IS", 0, 128)
-    ts(v("UP"), i128, col(K), A.subtract, 1.0, A.is_equal)
-    ts(v("TM"), i128, col(K), A.subtract, -1.0, A.is_equal)
+    cp(v("CL", 0, 6), v("KI", 0, 6))
+    i128, idb = v("IS", 0, 128), v("ID", 16, 144)
+
+    def kf(d):
+        return v("KF", d + 1, d + 2)
+
+    def rm(r):
+        return v("RM", r, r + 1)
+
+    def lin(k, src, a, b):
+        ts(col(k), src, a, A.mult, b, A.add)
+
     ts(v("RM"), v("IS", 0, 16), col(II), A.is_equal)
+    ts(v("RP"), v("IS", 0, 8), col(PP), A.is_equal)
+    lin(NE0, rm(0), -1.0, 1.0)
+    lin(MINC, col(ODD), -999.0, 1000.0)
+    lin(ADDC, col(ODD), 255.0, -256.0)
+    lin(WW, col(ODD), 16383.0, 1.0)
+    ts(v("ID"), v("IS", 0, 160), kf(16), A.is_equal)
+    ts(v("SH"), i128, kf(-1), A.is_equal, col(NE0), A.mult)
+    ts(v("WR"), i128, kf(15), A.is_equal, rm(0), A.mult)
     ts(v("Z"), v("IS", 0, 144), 15.0, A.subtract, col(G16), A.is_equal)
-    ts(v("FC"), v("UP"), col(EVEN), A.mult)
-    ts(v("BC"), v("TM"), col(ODD), A.mult)
-    tt(v("SW"), v("FC"), v("BC"), A.add)
     ts(v("ON"), v("GM"), col(GC), A.is_equal)
-
-    def zmake(r):
-        act(v("ZP", 144 * r, 144 * r + 144), v("Z"), AF.Identity, scale=v("RM", r, r + 1))
-
-    def brmake(i):
-        act(v("BR", 128 * i, 128 * i + 128), v("ON"), AF.Identity, scale=v("RM", i, i + 1))
-
-    for r in range(0, 16, 2):
-        zmake(r)
-
-    def starts(t):
-        ae = "AE%d" % t
-
-        def spread(a, h):
-            return lambda: ts(v("XT", 32 * a + 16 * h, 32 * a + 16 * h + 16), v("CD", 64 * t + a, 64 * t + 64, 4), col(GG if h else NGG), A.mult)
-
-        def join(a):
-            tt(v(ae, 1 + 16 * a, 17 + 16 * a), v("YT", 32 * a, 32 * a + 16), v("YT", 32 * a + 16, 32 * a + 32), A.add)
-            if a == 3:
-                mm(v("B7", 0, 2), v("SW"), (T[ae][:, 1:65:63], [(ae, 1, 2), (ae, 64, 65)]))
-
-        return [spread(a, h) for a in range(4) for h in range(2)] + [
-            lambda: note("v", lambda: g.vector.transpose(T.YT[:], T.XT[:]), [v("XT")], [v("YT")]),
-            lambda: join(0), lambda: join(3), lambda: join(1), lambda: join(2),
-            lambda: ts(v(ae, 0, 1), v("B7", 1, 2), col(ODD), A.mult, col(NEG), A.add),
-            lambda: ts(v(ae, 65, 66), v("B7", 0, 1), col(EVEN), A.mult, col(POS), A.add),
-            lambda: tt(v("DE", 0, 65), v(ae, 1, 66), v(ae, 0, 65), A.subtract),
-            lambda: ts(v("OW%d" % t, 0, 65), v("DE", 0, 65), 512.0, A.min, col(B512) if t else 0.0, A.add)]
-
-    def starts2(t):
-        ae = "AE%d" % t
-        return [lambda: act(v("AX%d" % t, 0, 65), v(ae, 0, 65), AF.Identity, bias=256.0),
-                lambda: act(v("C2%d" % t), v(ae, 1, 65), AF.Identity, bias=col(B512), scale=-1.0),
-                lambda: act(v("A1%d" % t, 0, 65), v(ae, 0, 65), AF.Identity, bias=0.5, scale=1.0 / 8192.0),
-                lambda: act(v("AB%d" % t), v(ae, 1, 65), AF.Identity, bias=4096.0 - BIG)]
-
-    def select(o, a, pat, op, fill, base, ch):
-        note("g", lambda: g.affine_select(o[0], a[0], pat, op, fill, base, ch), [a], [o])
-
-    dti = (T.DTI[:, 1:512], [("DTI", 0, 512), ("DTI", 1000, 1001)])
-    for f in starts(0):
-        f()
-    ts(v("DT", 1, 512), dti, -256.0, A.add)
-    run = [[1, 128]]
+    lin(C15, rm(15), 512.0, 0.0)
+    lin(EVEN, col(ODD), -1.0, 1.0)
+    act(v("ZW"), v("Z"), AF.Identity, scale=col(WW))
     act(v("TM"), v("ON"), AF.Identity)
-    act(v("NI"), v("ON"), AF.Identity, scale=-1.0)
-    act(v("IL"), v("IS", 0, 16), AF.Identity, bias=col(II), scale=16.0)
-    for i in range(12):
-        brmake(i)
-    select(v("TRI"), v("ON"), run, A.is_gt, 0.0, 0, -1)
-    select(v("TGE"), v("ON"), [[-1, 128]], A.is_ge, 0.0, 0, 1)
+    act(v("O8K"), v("ON"), AF.Identity, scale=GATE)
+    act(v("N8"), v("ON"), AF.Identity, scale=-GATE)
+    for k in range(8):
+        act(v("VM", 130 * k, 130 * k + 130), v("ID", 14 + 2 * k, 144 + 2 * k), AF.Identity, scale=v("RP", k, k + 1))
+
+    ts(v("AH", 0, 128), v("CD"), -2048.0, A.add)
+    ts(v("NAH", 0, 128), v("CD"), -1.0, A.mult, 2048.0, A.add)
+    msum(v("B7", 0, 128), [(v("SH"), v("AH", 0, 128)), (v("WR"), v("AH", 1, 129)), (idb, v("NAH", 0, 128))])
+    msum(v("B6", 0, 128), [(idb, v("NAH", 0, 128)), (idb, v("PCH"))])
+    msum(v("B6", 128, 256), [(v("SH"), v("NAH", 0, 128)), (v("WR"), v("NAH", 1, 129)), (idb, v("PCH"))])
+    dti = (T.DTI[:, 1:512], [("DTI", 0, 512), ("DTI", 1000, 1001)])
+    ts(v("OW0"), v("B7", 0, 64), 512.0, A.min)
+    ts(v("OW0", 7, 64, 8), v("B7", 7, 64, 8), 512.0, A.min, col(C15), A.max)
+    ts(v("DT", 1, 512), dti, col(MINC), A.min, col(ADDC), A.add)
+    act(v("C2"), v("B6", 128, 256), AF.Identity)
+    act(v("C1"), v("B6", 0, 128), AF.Identity)
+    send(before, after, "adn", "DN", v("DT"), 3500)
+    run = [[1, 128]]
     select(v("IDF"), v("TM"), run, A.is_equal, 0.0, 0, -1)
-    select(v("WF"), v("NI"), run, A.is_gt, 0.0, 0, -1)
+    select(v("TRI"), v("ON"), run, A.is_gt, 0.0, 0, -1)
+    select(v("TRO"), v("ON"), [[16, 8], [2, 8], [2, 2]], A.is_gt, 0.0, 0, -1)
+    for a in (0, 16 + RY, 16 + RZ):
+        iota(v("VS", a, a + 272), [[0, 272]], 0, 0)
+    select(v("T8K"), v("O8K"), run, A.is_gt, 0.0, 0, -1)
+    select(v("G8"), v("N8"), run, A.is_gt, 0.0, 0, -1)
+    select(v("G8"), v("G8"), run, A.not_equal, GATE, 0, -1)
+    send(before, after, "apa", "PA1", v("PA0"), 5000)
+    select(v("TGE"), v("ON"), [[-1, 128]], A.is_ge, 0.0, 0, 1)
     select(v("SD"), v("TM"), run, A.is_equal, 0.0, -1, -1)
-    select(v("R0C"), v("TM"), [[0, 8], [1, 16]], A.is_equal, 0.0, 0, 0)
-    select(v("WF"), v("WF"), run, A.not_equal, 1.0, 0, -1)
     select(v("SD"), v("SD"), run, A.not_equal, -1.0, 0, -1)
-    select(v("IDB"), v("ON"), run, A.is_equal, 0.0, 0, -1)
-    select(v("NI"), v("NI"), run, A.is_equal, 0.0, 0, -1)
-    send(before, "adn", "DN", v("DT"))
-    iota(v("ISB"), [[1, 256]], 0, 0)
-    send(before, "apa", "PA1", v("PA0"))
-    iota(v("FN"), [[0, 4360]], -256, 0)
-    iota(v("FO"), [[0, 4360]], 0, 0)
+    select(v("R0C"), v("TM"), [[0, 8], [1, 16]], A.is_equal, 0.0, 0, 0)
+    select(v("OH"), v("O8K"), [[-16, 8], [-2, 16]], A.is_ge, 0.0, 0, 1)
+    select(v("OH"), v("OH"), [[16, 8], [2, 16]], A.is_ge, 0.0, 1, -1)
+    iota(v("FN"), [[0, 4240]], -1, 0)
 
-    early = [
-        lambda: cp(v("PF"), v("PRI")),
-        lambda: cp(v("DTF", 0, 1), (T.DTI[:, 0:1], dti[1])),
-        lambda: ts(col(BB1), col(PP), 512.0, A.mult, BIG, A.add),
-        lambda: ts(col(BO), col(PP), 512.0, A.mult, 4096.0 - BIG, A.add),
-        lambda: ts(col(PCM), col(II), -512.0, A.mult, 2048.0, A.add),
-        lambda: ts(col(I64), col(II), 64.0, A.mult, -1024.0, A.add),
-        lambda: ts(v("ZH", 0, 144), v("Z"), v("RM", 0, 1), A.mult),
-        lambda: ts(v("ZH", 144, 288), v("Z"), v("RM", 0, 1), A.mult, -1.0, A.mult),
-        lambda: ts(v("R0H"), v("ON"), v("RM", 0, 1), A.mult),
-        lambda: ts(v("R0N"), v("ON"), v("RM", 0, 1), A.mult, -1.0, A.mult),
-        lambda: ts(v("R02"), v("ON"), v("RM", 0, 1), A.mult, 2.0, A.mult),
-        lambda: cp(v("ONH"), v("ON")),
-        lambda: ms(v("HK", 256, 272), -2048.0),
-        lambda: ms(v("HK", 528, 545), 512.0),
-        lambda: ts(v("TR", 0, 16), v("IL"), 8193.0, A.add, 1.0 / FAR, A.mult),
-        lambda: ts(v("TR", 16, 32), v("IL"), 4096.0, A.add, 1.0 / FAR, A.mult),
-    ]
+    def early():
+        ts(v("HI"), v("CD"), 4, A.arith_shift_right)
+        ts(v("LO"), v("CD"), 15, A.bitwise_and)
+        cp(v("HB"), v("HI"))
+        cp(v("LB"), v("LO"))
+        ts(col(CA), rm(0), 16.0, A.mult, rm(2), A.add)
+        ts(col(CB), rm(1), 16.0, A.mult, rm(3), A.add)
+        lin(P4, col(PP), 512.0, -2048.0)
+        lin(CO1, col(PP), 512.0, 272.0)
+        lin(CBO, col(PP), 512.0, 272.0 - BIG)
+        lin(BB1, col(PP), 512.0, BIG)
+        lin(SGN, col(ODD), -2.0, 1.0)
+        lin(HC, col(II), -GATE, -18.0 * GATE)
+        lin(NII, col(II), -1.0, 0.0)
+        lin(MAB, rm(0), -256.0, 0.0)
+        lin(CMB, col(EVEN), -GATE, 0.0)
+        ts(col(CMA), col(EVEN), rm(15), A.subtract, GATE, A.mult)
+        lin(CIN, rm(15), -16.0, 0.0)
+        lin(CJK, col(II), 32.0, RJ - RY - RZ + 0.0)
+        ts(v("FC"), i128, kf(1), A.is_equal, col(EVEN), A.mult)
+        ts(v("BC"), i128, kf(-1), A.is_equal, col(ODD), A.mult)
+        ts(v("JK"), v("IS", 0, 32), col(CJK), A.add)
+        ts(v("XO"), v("IS", 0, 8), 0.0, A.mult, col(PP), A.add)
+        cp(v("PF"), v("PRI"))
+        cp(v("DTF", 0, 1), (T.DTI[:, 0:1], dti[1]))
+        ts(v("T3"), v("B7", 64, 128), 512.0, A.min)
+        ts(v("T3", 7, 64, 8), v("B7", 71, 128, 8), 512.0, A.min, col(C15), A.max)
+        tt(v("T4"), v("T3"), v("PCH", 0, 64), A.add)
+        ts(v("OW1"), v("T4"), -272.0, A.add)
+        ts(v("DM"), v("MM"), col(II), A.is_equal)
+        for o in (v("TX", 4112, 4368), v("NJ", 0, 16), v("N2", 512, 528), v("XH", 0, 1)):
+            ms(o, 0.0)
 
-    def early_scalar():
-        for o, c in ((v("UB", 0, 1), 0.0), (v("KB", 64, 66), 0.0), (v("EB", 32, 34), 1.0), (v("NEG1"), -1.0), (v("ZR"), 0.0),
-                     (v("FI", 0, 1), 0.0), (v("FI", 257, 258), 0.0)):
-            act(o, v("IS", 0, o[1][0][2] - o[1][0][1]), AF.Identity, bias=c, scale=0.0)
-        act(v("P21"), v("P21"), AF.Identity, scale=1024.0)
-        act(v("K1"), v("IS", 0, 64), AF.Identity, bias=col(I64))
+    def fill(o, c):
+        act(o, v("IS", 0, o[1][0][2] - o[1][0][1]), AF.Identity, bias=c, scale=0.0)
+
+    def scalar_first():
+        for k in range(8):
+            act(v("ZP", 144 * k, 144 * k + 144), v("ZW"), AF.Identity, scale=v("RP", k, k + 1))
+        act(v("ZA", 0, 144), v("Z"), AF.Identity, scale=col(CA))
+        act(v("ZA", 144, 288), v("Z"), AF.Identity, scale=col(CB))
+        act(v("NI"), idb, AF.Identity, scale=-1.0)
+        for o, c in ((v("S1", 0, 1), 0.0), (v("EB", 32, 33), 1.0), (v("EE", 0, 1), 0.0), (v("OO", 0, 1), 0.0), (v("ST", 0, 1), 0.0),
+                     (v("SB", 0, 1), 0.0), (v("FI", 256, 258), 0.0)):
+            fill(o, c)
+
+    def scalar_second():
+        for nm, src, sc in (("NA", idb, -1.0 * RY), ("NB", idb, -1.0 * RZ), ("PQ4", v("ON"), col(P4)), ("RA", v("ON"), col(CA)),
+                            ("RB", v("ON"), col(CB)), ("INA", v("ON"), col(CIN)), ("O16", v("ON"), 1.0 / 16), ("N16", v("ON"), -1.0 / 16)):
+            act(v(nm), src, AF.Identity, scale=sc)
+        act(v("MK"), v("IS"), AF.Identity, bias=4096.0)
+
+    def scalar_third():
+        for nm, src, sc in (("PMA", v("ON"), col(CMA)), ("PMB", v("ON"), col(CMB)), ("I8", idb, GATE), ("Z64", v("Z"), 1.0 / 64)):
+            act(v(nm), src, AF.Identity, scale=sc)
         act(v("RS"), v("MM"), AF.Sign)
-        act(v("C4"), v("IS"), AF.Identity, bias=4096.0, scale=0.0)
-        for nm, src, sc in (("O14", "ON", 16384.0), ("NI4", "NI", 4.0), ("O9", "ON", 4096.0), ("O10", "ON", -8192.0), ("O11", "ON", 2048.0)):
-            act(v(nm), v(src), AF.Identity, scale=sc)
+        act(v("TRM"), v("QS"), AF.Identity, bias=-2048.0)
         act(v("DTF", 1, 512), v("DT", 1, 512), AF.Identity, bias=256.0)
 
-    def compare():
-        mm(v("B1", 0, 256), v("ON"), v("ZR"), True, False)
-        for u in range(16):
-            e0 = 272 * u
-            ts(v("E", e0, 256 * u + 256), v("XW", 16 * u, 256), 1.0 / FAR, A.mult, v("NN", u, u + 1), A.is_equal)
-            mm(v("B1", 16 * u, 16 * u + 16), v("TRI"), v("E", e0, e0 + 16), False, u == 15)
-            if u < 15:
-                mm(v("B1", 16 * u + 16, 256), v("ON"), v("E", e0 + 16, 256 * u + 256), False, False)
+    def pairs(t, bank):
+        for k in range(32):
+            m0, c0 = 130 * (k % 8), 64 * t + k // 8
+            msum(v(bank, 16 * k, 16 * k + 16), [(v("VM", m0 + 2, m0 + 130), v("HB", c0, 64 * t + 64, 4)),
+                                                (v("VM", m0, m0 + 128), v("LB", c0, 64 * t + 64, 4))])
 
-    def key_sum(bank, a, b):
-        mm(v(bank, a, b), v("R0H"), v("HK", a, b), True, False)
-        mm(v(bank, a, b), v("NI"), v("C4", a, b), False, False)
-        mm(v(bank, a, b), v("O14"), v("FI", 1 + a, 1 + b), False, True)
+    def halves(t, bank):
+        for b in range(2):
+            fold(bank, 32 * b, 32, "VT%d" % t, 0, to_row("ZA", 144 * b))
 
-    def key_wide(bank, a, b):
-        tt(v("DW", a, b), v(bank, a, b), v("HK", 272 + a, 272 + b), A.min)
-        ts(v("XW", a, b), v("DW", a, b), 6144.0, A.add)
+    def halves2(t, bank):
+        for b in range(2):
+            act(v("A1%d" % t, b, 64, 2), v(bank, 32 * b, 32 * b + 32), AF.Identity, bias=0.5, scale=1.0 / 8192.0)
+            act(v("AB%d" % t, b, 64, 2), v(bank, 32 * b, 32 * b + 32), AF.Identity, bias=4096.0 - BIG)
+
+    def places(pf):
+        anywhere(tt, v("OX0"), ind(pf, v("XO")), v("ON"), A.mult)
+        note("v", lambda: g.vector.transpose(T.OTM[:], T.OX0[:]), [v("OX0")], [v("OTM")])
+        reduce(v("R0", 1, 2), v("OTM", 0, 128, 16), A.add)
+        ts(v("O0M"), v("ON"), v("R0", 1, 2), A.mult)
+        mm(v("B3", 0, 8), v("SD"), pf)
+        act(v("DF"), v("B3", 0, 8), AF.Identity)
 
     def differ(out, a, b, bank, later=False):
         k = out[1][0][2] - out[1][0][1]
-        mm(v(bank, 0, k), v("IDB"), a, True, False)
-        mm(v(bank, 0, k), v("NI"), b, False, True)
+        msum(v(bank, 0, k), [(idb, a), (v("NI"), b)])
         act(v("EV", 0, k), v(bank, 0, k), AF.Abs)
-        if later:
-            return lambda: act(out, v("EV", 0, k), AF.Sign)
         act(out, v("EV", 0, k), AF.Sign)
 
-    def duel(t, nn, ychunks):
-        pat = v("PA%d" % t)
-        for a, b in ychunks:
-            act(v("Y", 16 * a, 16 * b), ind(v("TX"), v("OY", a, b)), AF.Copy)
-        off = 16 if nn == 64 else 0
-        c = 40 if (t, nn) == (0, 64) else nn - nn // 4
-        act(v("PX", 16 * c, 16 * nn), ind(pat, v("O1", c, nn)), AF.Copy)
-        differ(v("NQ", 1024 + 16 * c, 1024 + 16 * nn), v("Y", off + 16 * c, off + 16 * nn), v("PX", 16 * c, 16 * nn), "B5")
-        for a, b in ychunks:
-            b = min(b, nn)
-            tt(v("NQ", 16 * a, 16 * b), ind(pat, v("O2", a, b)), v("Y", 16 * a, 16 * b), A.not_equal)
-        fold("B1", 0, nn, "NQ", 0, zall)
-        tt(v("NQ", 1024, 1024 + 16 * c), ind(pat, v("O1", 0, c)), v("Y", off, off + 16 * c), A.not_equal)
-        fold("B1", nn, nn, "NQ", 1024, zall)
-
     def own_witnesses(vals, offs):
-        ts(indw(v("FO"), offs), vals, 1.0, A.mult, 256.0, A.add)
+        anywhere(ts, indw(v("FO"), offs), vals, 1.0, A.mult, 256.0, A.add)
 
-    def r1(k):
-        return v("R1", k, k + 1)
-
-    def w(a, b):
-        return v("B0", a, b)
-
-    def one_round(t):
-        tab = v("FN") if t else v("DT")
-        pick = zrow if t else zpat
-        pat = v("PA%d" % t)
-        ow = "OW%d" % t
+    def reorder(t):
         pf = v("LC0") if t else v("PF")
-        to = after if t else before
-        if t:
-            cp(indw(v("FN"), v("LB0")), v("LA0"))
+        return [lambda: reduce(v("R0", 0, 1), v("B2", 256, 512), A.max, True),
+                lambda: ts(v("SP", 0, 1), v("R0", 0, 1), 2 * GATE, A.add, 256.0, A.min),
+                lambda: anywhere(cp, v("F1"), ind(v("FI"), v("SP", 0, 1))),
+                lambda: (mm(v("B3", 0, 8), v("TGE"), v("F1", 0, 8)), tt(v("YO"), v("F1", 0, 8), pf, A.mult),
+                         msum(v("B5", 0, 8), [(v("IDF"), pf), (v("R0C"), v("YO"))])),
+                lambda: tt(v("GD"), v("B3", 0, 8), v("DF"), A.mult),
+                lambda: (tt(v("MC%d" % t), v("B5", 0, 8), v("GD"), A.add),
+                         send(*ways(t), "ac%d" % t, "LC%d" % t, v("MC%d" % t)))]
+
+    def ways(t):
+        return (after, before) if t else (before, after)
+
+    def stage1(t):
+        ow, c0 = "OW%d" % t, 64 * t
+        mm(v("B0", 0, 64), idb, v("AH", c0, c0 + 64), True, False)
         if t == 0:
-            starts2(0)[0]()
-        mm(w(0, 65), v("IDF"), v("AX%d" % t, 0, 65), True, False)
-        cp(v("WG", 0, 512), ind(tab, v(ow, 0, 32)))
-        act(v("WG", 512, 1040), ind(tab, v(ow, 32, 65)), AF.Copy)
-        fold("B0", 0, 65, "WG", 0, pick, False, True)
-        if t == 0:
-            for f in starts2(0)[1:]:
-                f()
-            for i in range(12, 16):
-                brmake(i)
-            for f in early[:8]:
-                f()
-        ts(v("OY", 0, 65), w(0, 65), 0.0, A.max)
-        tt(v("T2", 0, 64), w(0, 64), v("C2%d" % t), A.add)
-        tt(v("T1", 0, 65), w(0, 65), v("AX%d" % t, 0, 65), A.subtract)
-        ts(v("O2"), v("T2", 0, 64), 0.0, A.max)
-        ts(v("O1"), v("T1", 1, 65), col(B256), A.add)
-        ts(v("T3", 0, 65), v("T1", 0, 65), -255.5, A.is_lt, 100.0, A.mult)
-        for i in range(16):
-            mm(v("B%d" % (3 + i // 8), 64 * (i % 8), 64 * (i % 8) + 64), v("BR", 128 * i, 128 * i + 128), v("AE%d" % t, 1, 65))
-        if t == 0:
-            for f in early[8:]:
-                f()
-            spare.append(lambda: ts(v("DM"), v("MM"), col(II), A.is_equal))
-            spare.extend(starts(1) + starts2(1))
-            idle(9)
-        duel(t, 64, [(0, 8), (8, 24), (24, 44), (44, 65)])
-        if t == 0:
-            early_scalar()
-            dma("y", "dfn", (T.FN[0:128:16, 0:4096], [("FN", 0, 4096)]), (T.DN[0:128:2, 0:512], [("DN", 0, 520)]))
+            for p in range(4):
+                ts(v("WG", 128 * p, 128 * p + 128), ind(v("DT"), v(ow, 8 * p, 8 * p + 8)), v("RP", p, p + 1), A.mult)
+            for p in range(4, 8):
+                act(v("WG", 128 * p, 128 * p + 128), ind(v("DT"), v(ow, 8 * p, 8 * p + 8)), AF.Identity, scale=v("RP", p, p + 1))
+            fold("B0", 0, 64, "WG", 0, to_row("ZW"), False, True)
+            early()
+            scalar_first()
+            scalar_second()
+            tt(v("QS"), v("MK"), v("DM"), A.mult)
+            scalar_third()
+            dma("y", "dn0", (T.FN[0:128:16, 0:4096], [("FN", 0, 4096)]), (T.DN[0:128:2, 0:512], [("DN", 0, 520)]))
+            dma("y", "dn1", (T.FN[1:128:16, 0:4096], [("FN", 5000, 5001)]), (T.DN[1:128:2, 0:512], [("DN", 0, 520), ("FN", 4096, 4240)]))
             dma("y", "dfo", (T.FO[0:128:16, 0:4096], [("FO", 0, 4096)]), (T.DTF[0:128:2, :], [("DTF", 0, 512)]))
-        ts(v("TH", 0, 64), v("T3", 0, 64), 6.5, A.add)
-        ts(v("TH", 64, 128), v("T3", 1, 65), 6.5, A.add)
-        ts(v("BI"), pf, 4097.0, A.mult)
-        tt(v("BI"), v("BI"), v("P21"), A.add)
-        idle(4)
-        tt(v("OK"), v("B1", 0, 128), v("TH"), A.is_lt)
-        tt(v("UB", 1, 65), v("OK", 0, 64), v("OK", 64, 128), A.mult)
-        ale, alo = v("UB", 1, 65, 2), v("UB", 2, 66, 2)
-        scan(v("S1", 0, 65), v("UB", 0, 65), v("A1%d" % t, 0, 65), 0.0, A.max, A.min)
-        mm(v("B2", 0, 1), v("FC"), v("S1", 64, 65))
-        tt(v("UN"), v("UB", 1, 65), v("AB%d" % t), A.mult)
+            for r, (b1, b2) in enumerate((("B3", "B4"), ("B6", "B4"))):
+                pairs(r, b1)
+                act(v("VT%d" % r), v(b1, 0, 512), AF.Identity)
+                halves(r, b2)
+                halves2(r, b2)
+        else:
+            cp(indw((T.FN[:], [("FN", 0, 4240), ("FN", 5000, 5001)]), v("LB0")), v("LA0"))
+            cp(v("WG", 0, 512), ind(v("FN"), v(ow, 0, 32)))
+            act(v("WG", 512, 1024), ind(v("FN"), v(ow, 32, 64)), AF.Copy)
+            fold("B0", 0, 64, "WG", 0, to_row("ZP"), False, True)
+        ts(v("OY"), v("B0", 0, 64), 2320.0, A.add)
+        tt(v("T2"), v("B0", 0, 64), v("C2", c0, c0 + 64), A.add)
+        tt(v("T1"), v("B0", 0, 64), v("C1", c0, c0 + 64), A.add)
+        cp(v("O2"), v("T2"))
+        cp(v("O1"), v("T1"))
+        own = 16
+        ych = [(0, 8), (8, 24), (24, 44), (44, 64)] if t else [(0, 16), (16, 40), (40, 64)]
+        for a, b in ych:
+            act(v("Y", 16 * a, 16 * b), ind(v("TX"), v("OY", a, b)), AF.Copy)
+
+        def win(b):
+            return v("PA1") if t else v("PA0", 0, 16 + 1024 * ((b + 15) // 16))
+
+        act(v("PX", 0, 16 * own), ind(win(own), v("O1", 0, own)), AF.Copy)
+        steps = ([("j", a, b) for a, b in ych] + [("d", 0, own), ("i", own, 48), ("i", 48, 64)] if t else
+                 [("j", 0, 16), ("j", 16, 32), ("i", own, 32), ("d", 0, own), ("j", 32, 48), ("i", 32, 48), ("j", 48, 64), ("i", 48, 64)])
+        done = {"j": [], "i": []}
+        have = {"j": set(), "i": set()}
+        for kind, a, b in steps:
+            if kind == "j":
+                tt(v("NJ", 16 + 16 * a, 16 + 16 * b), ind(win(b), v("O2", a, b)), v("Y", 16 * a, 16 * b), A.not_equal)
+            elif kind == "i":
+                tt(v("NQ", 16 * a, 16 * b), ind(win(b), v("O1", a, b)), v("Y", 16 * a, 16 * b), A.not_equal)
+            else:
+                differ(v("NQ", 0, 16 * own), v("Y", 0, 16 * own), v("PX", 0, 16 * own), "B5")
+                kind = "i"
+            have[kind] |= set(range(a, b))
+            for u in range(16):
+                if u not in done[kind] and have[kind] >= set(range(4 * u, 4 * u + 4)):
+                    done[kind].append(u)
+                    r = v("NJ", 15 + 64 * u, 79 + 64 * u) if kind == "j" else v("NQ", 64 * u, 64 * u + 64)
+                    mm(v("B1" if kind == "j" else "B2", 0, 64), zall(u), r, len(done[kind]) == 1, len(done[kind]) == 16)
+        ts(v("TH"), v("B1", 0, 64), 6.5, A.is_lt, 6.5, A.mult)
+        tt(v("UB"), v("B2", 0, 64), v("TH"), A.is_lt)
+
+    def stage2(t):
+        tab, pat = v("FN") if t else v("DT"), v("PA%d" % t)
+        ale, alo = v("UB", 0, 64, 2), v("UB", 1, 64, 2)
+        w = v("B0", 0, 32)
+        scan(v("S1", 1, 65), v("UB"), v("A1%d" % t), 0.0, A.max, A.min)
+        mm(v("B7", 0, 1), v("FC"), v("S1", 64, 65))
+        tt(v("UN"), v("UB"), v("AB%d" % t), A.mult)
         tt(v("M2"), v("UN", 0, 64, 2), v("UN", 1, 64, 2), A.min)
-        ts(v("PV"), v("S1", 0, 64, 2), v("B2", 0, 1), A.max, 8192.0, A.mult)
-        act(v("PVX"), v("PV"), AF.Identity, bias=-3840.0)
-        mm(w(0, 32), v("IDF"), v("PVX"), True, False)
+        ts(v("PV"), v("S1", 0, 64, 2), v("B7", 0, 1), A.max, 8192.0, A.mult)
+        mm(w, v("IDF"), v("PV"), True, False)
         tt(v("DD"), v("M2"), v("PV"), A.subtract)
         ts(v("OW2"), v("DD"), 512.0 - BIG, A.min, col(BB1) if t else BIG, A.add)
         act(v("WG", 256, 512), ind(tab, v("OW2", 16, 32)), AF.Copy)
         cp(v("WG", 0, 256), ind(tab, v("OW2", 0, 16)))
-        fold("B0", 0, 32, "WG", 0, pick, False, True)
-        ts(v("C2B"), v("M2"), -1.0, A.mult, col(BO), A.add)
+        fold("B0", 0, 32, "WG", 0, lambda i: to_row("ZP", 0 if t else 144 * (i // 2))(i), False, True)
+        ts(v("C2B"), v("M2"), -1.0, A.mult, col(CBO), A.add)
         ts(v("EB", 0, 32), v("M2"), -0.5, A.is_gt)
-        ts(v("AO1"), alo, 1.0, A.add)
-        ts(v("NE"), ale, -1.0, A.mult, 1.0, A.add)
-        idle(5)
-        ts(v("OY", 0, 32), w(0, 32), 0.0, A.max)
-        tt(v("T2", 0, 32), w(0, 32), v("C2B"), A.add)
-        tt(v("T1", 0, 32), w(0, 32), v("PVX"), A.subtract)
-        ts(v("O2", 0, 32), v("T2", 0, 32), 0.0, A.max)
-        ts(v("O1", 0, 32), v("T1", 0, 32), col(B256), A.add)
-        ts(v("T3", 0, 32), v("T1", 0, 32), -255.5, A.is_lt, 100.0, A.mult)
-        duel(t, 32, [(0, 8), (8, 20), (20, 32)])
-        for i in range(16):
-            act(v("VT", i, 1024, 16), v("B%d" % (3 + i // 8), 64 * (i % 8), 64 * (i % 8) + 64), AF.Identity, bias=v("BI", i // 2, i // 2 + 1))
-        ts(v("TH", 0, 32), v("T3", 0, 32), 6.5, A.add)
-        ts(v("TH", 32, 64), v("T3", 0, 32), 6.5, A.add)
-        idle(11)
-        tt(v("KB", 0, 64), v("B1", 0, 64), v("TH", 0, 64), A.is_gt)
-        scan(rv("SR", 32, 0), rv("EB", 32, 0), rv("KB", 64, 32), 0.0, A.mult, A.add)
-        mm(v("B2", 0, 1), v("BC"), v("SR", 0, 1))
-        kj = v("KB", 0, 32)
-        tt(v("T1", 0, 32), ale, kj, A.subtract)
-        tt(v("T2", 0, 32), v("NE"), kj, A.mult)
-        tt(v("AEV"), v("T1", 0, 32), v("AO1"), A.mult)
-        tt(v("AOD"), alo, v("T2", 0, 32), A.subtract)
-        scan(rv("SQ", 32, 1), rv("EB", 32, 1), rv("KB", 64, 33), v("B2", 0, 1), A.mult, A.add)
-        tt(v("AL2", 0, 64, 2), v("AEV"), v("SQ", 1, 33), A.is_gt)
-        tt(v("AL2", 1, 64, 2), v("AOD"), v("SQ", 1, 33), A.is_gt)
-        scan(v("LOC"), v("AL2"), v("NEG1"), 0.0, A.add, A.add)
-        mm(v("B2", 0, 1), v("TRI"), v("LOC", 63, 64))
-        mm(v("B2", 1, 2), v("ON"), v("LOC", 63, 64))
-        tt(v("T1", 0, 64), v("AL2"), v("K1"), A.mult)
-        tt(v("T3", 0, 64), v("T1", 0, 64), v("LOC"), A.add)
-        ts(v("OC"), v("T3", 0, 64), v("B2", 0, 1), A.add, 1024.0, A.add)
-        cp(indw(v("VS"), v("OC")), v("VT"))
-        act(v("TOT", 0, 1), v("B2", 1, 2), AF.Identity, bias=1024.0)
-        act(v("TOT", 1, 2), v("B2", 1, 2), AF.Identity, bias=1024.0, scale=-1.0)
-        mm(v("B2", 0, 8), v("SD"), pf)
-        act(v("DF"), v("B2", 0, 8), AF.Identity)
-        vs = v("VS", 0, 256)
-        ts(v("W1"), vs, 12, A.arith_shift_right)
-        ts(v("W2"), vs, 4095, A.bitwise_and)
-        ts(v("PO16"), v("W1"), 2048.0, A.add)
-        chunks = [(0, 16), (16, 64), (64, 128), (128, 192), (192, OWN)]
-        cp(v("TO16"), v("W2"))
-        for a, b in chunks[:-1] + [(192, 256)]:
-            act(v("PX", 16 * a, 16 * b), ind(pat, v("PO16", a, b)), AF.Copy)
-        act(v("Y", 0, 4096 - 16 * OWN), ind(v("TX"), v("TO16", OWN, 256)), AF.Copy)
-        tt(v("DW", 1, 256), v("VS", 1, 256), v("VS", 0, 255), A.subtract)
-        ts(v("W4"), v("W1"), -512, A.bitwise_and)
-        ts(v("HK", 545, 800), v("DW", 1, 256), 512.0, A.min, 1.0, A.max)
-        ts(v("HK", 0, 256), v("W2"), -2048.0, A.add)
-        tt(v("HK", 272, 528), v("W4"), v("HK", 544, 800), A.add)
-        fold("B0", 0, 33, "HK", 0, zh(0))
-        fold("B0", 40, 16, "HK", 271, zh(0), True, False)
-        fold("B0", 40, 16, "HK", 543, zh(1), False, False)
-        fold("B0", 40, 16, "HK", 544, zh(1), False, True)
-        mm(w(256, 512), v("R0H"), v("HK", 272, 528), True, False)
-        mm(w(256, 512), v("R0N"), v("HK", 544, 800), False, True)
-        for j, (a, b) in enumerate(chunks):
-            tt(v("NQ", 16 * a, 16 * b), ind(v("TX"), v("TO16", a, b)), v("PX", 16 * a, 16 * b), A.not_equal)
-            if j == 0:
-                continue
-            a0 = 0 if j == 1 else a
-            fold("B4" if j == 4 else "B3", a0, 64, "NQ", 16 * a0, zall)
-            if j == 3:
-                rest = differ(v("NQ", 16 * OWN, 4096), v("Y", 0, 4096 - 16 * OWN), v("PX", 16 * OWN, 4096), "B1", True)
-                act(v("SB", 0, 192), v("B3", 0, 192), AF.Sign, bias=-6.5)
-                mm(v("B5", 0, 192), v("WF"), v("SB", 0, 192))
-                rest()
-        act(v("SB", 192, 256), v("B4", 192, 256), AF.Sign, bias=-6.5)
-        ts(v("ACT"), v("IL"), v("TOT", 0, 1), A.is_ge, 5000.0, A.mult)
-        ts(v("L1", 0, 16), v("ACT"), 7680.0, A.add)
-        for (a, b), gb, qb in (((0, 192), "B5", "B6"), ((192, 256), "B2", "B4")):
-            if a:
-                mm(v(gb, a, b), v("WF"), v("SB", a, b))
-            ts(v("FI", 1 + a, 1 + b), v(gb, a, b), col(II), A.is_gt)
-            tt(v("XP", a, b), v("FI", 1 + a, 1 + b), v("W1", a, b), A.mult)
-            q = v(qb, a, b)
-            mm(q, v("O10"), v("FI", 1 + a, 1 + b), True, False)
-            mm(q, v("O9"), v("FI", a, b), False, False)
-            mm(q, v("ONH"), v("XP", a, b), False, True)
-            if a == 0:
-                key_sum("B7", 0, 192)
-                ts(v("LS", 0, 16), w(17, 33), 6144.0, A.add, 1.0 / FAR, A.mult)
-                ts(v("LS", 16, 32), w(0, 16), 2048.0, A.add, 1.0 / FAR, A.mult)
-                tt(v("LIM"), w(40, 56), v("L1", 0, 16), A.subtract)
-            else:
-                key_sum("B5", 192, 256)
-                key_wide("B7", 0, 192)
-            tt(v("MK", a, b), q, v("DM", a, b), A.mult)
-            scan(v("QS", a, b), v("RS", a, b), v("MK", a, b), 0.0, A.mult, A.add)
-        act(v("NM"), w(256, 512), AF.Abs, bias=col(PCM))
-        mm(v("B3", 0, 256), v("ONH"), v("XP"), True, False)
-        mm(v("B3", 0, 256), v("R0N"), v("HK", 272, 528), False, False)
-        mm(v("B3", 0, 256), v("R02"), v("HK", 544, 800), False, True)
-        act(v("MA%d" % t), v("B3", 0, 256), AF.Identity, bias=-256.0)
-        send(to, "aa%d" % t, "LA%d" % t, v("MA%d" % t))
-        sc = v("B7", 256, 512)
-        mm(sc, v("NI"), v("ISB"), True, False)
-        mm(sc, v("NI4"), v("NM"), False, False)
-        mm(sc, v("O11"), v("FI", 1, 257), False, True)
-        q = v("QS", 15, 256, 16)
-        tt(v("NN", 0, 16), q, v("LIM"), A.is_ge)
-        tt(v("NN", 16, 32), q, v("ACT"), A.is_lt)
-        tt(v("DW", 192, 256), v("B5", 192, 256), v("HK", 464, 528), A.min)
-        tt(v("PR"), v("NN"), v("LS", 0, 32), A.add)
-        ts(v("XW", 192, 256), v("DW", 192, 256), 6144.0, A.add)
-        tt(v("NN", 0, 16), v("PR", 0, 16), v("PR", 16, 32), A.min)
-        compare()
-        note("v", lambda: g.vector.tensor_reduce(T.R1[:, 0:1], sc[0], AxisListType.X, A.max), [sc], [r1(0)])
-        tt(v("MK"), v("B1", 0, 256), v("DM"), A.mult)
-        ts(r1(1), r1(0), v("TOT", 1, 2), A.is_gt)
-        scan(v("QS"), v("RS"), v("MK"), 0.0, A.mult, A.add)
-        ts(r1(2), r1(0), -1.0, A.mult, 2049.0 - 257.0, A.add)
-        tt(v("L1", 16, 32), q, v("PR", 16, 32), A.add)
-        tt(v("L1", 0, 16), q, v("PR", 0, 16), A.add)
-        tt(v("L2"), v("L1"), v("TR"), A.min)
-        ts(v("SP", 0, 1), r1(2), r1(1), A.mult, 257.0, A.add)
-        ts(v("MB%d" % t), v("L2", 0, 16), FAR, A.mult, -4096.0, A.add)
-        send(to, "ab%d" % t, "LB%d" % t, v("MB%d" % t))
-        ts(v("OT"), v("L2", 16, 32), FAR, A.mult)
-        act(v("NV"), ind(v("TX"), v("OT")), AF.Identity, bias=255.0, scale=-1.0)
-        cp(v("F1"), ind(v("FI"), v("SP", 0, 1)))
-        mm(v("B2", 0, 8), v("TGE"), v("F1", 0, 8))
-        tt(v("YO"), v("F1", 0, 8), pf, A.mult)
-        mm(v("B2", 8, 16), v("IDF"), pf, True, False)
-        mm(v("B2", 8, 16), v("R0C"), v("YO"), False, True)
+        ts(v("AO1"), alo, 20.0, A.mult, 6.5, A.add)
+        ts(v("NE"), ale, -6.5, A.mult, 6.5, A.add)
+        ts(v("O65"), alo, 6.5, A.mult)
+        places(v("LC0") if t else v("PF"))
+        ts(v("OY", 0, 32), w, -3824.0, A.add)
+        tt(v("T2", 0, 32), w, v("C2B"), A.add)
+        tt(v("T1", 0, 32), w, v("PV"), A.subtract)
+        cp(v("O2", 0, 32), v("T2", 0, 32))
+        ts(v("O1", 0, 32), v("T1", 0, 32), col(CO1), A.add)
+        ych = [(0, 8), (8, 20), (20, 32)]
+        for a, b in ych:
+            act(v("Y", 16 * a, 16 * b), ind(v("TX"), v("OY", a, b)), AF.Copy)
+        act(v("PX", 384, 512), ind(pat, v("O1", 24, 32)), AF.Copy)
+        differ(v("N2", 384, 512), v("Y", 384, 512), v("PX", 384, 512), "B5")
+        for a, b in ych:
+            tt(v("NQ", 16 * a, 16 * b), ind(pat, v("O2", a, b)), v("Y", 16 * a, 16 * b), A.not_equal)
+        fold("B1", 0, 32, "NQ", 0, zall)
+        tt(v("N2", 0, 384), ind(pat, v("O1", 0, 24)), v("Y", 0, 384), A.not_equal)
+        fold("B2", 0, 33, "N2", 0, zall)
+        ts(v("KJ"), v("B1", 0, 32), 6.5, A.is_gt)
+        tt(v("T5"), ale, v("KJ"), A.subtract)
+        tt(v("T6"), v("NE"), v("KJ"), A.mult)
+        tt(v("AEV"), v("T5"), v("AO1"), A.mult)
+        tt(v("AOD"), v("O65"), v("T6"), A.subtract)
+        scan(rv("SR", 31, 0), rv("EB", 31, 0), rv("B2", 31, 0), 0.0, A.mult, A.add)
+        mm(v("B7", 0, 1), v("BC"), v("SR", 0, 1))
+        scan(rv("SQ", 32, 1), rv("EB", 32, 1), rv("B2", 32, 1), v("B7", 0, 1), A.mult, A.add)
+        tt(v("EE", 1, 33), v("AEV"), v("SQ", 1, 33), A.is_gt)
+        tt(v("OO", 1, 33), v("AOD"), v("SQ", 1, 33), A.is_gt)
+
+    def st(a, b, back=0, step=1):
+        return v("ST", 1 + a - back, 1 + b - back, step)
+
+    def start_of(a, b):
+        return [(v("RA"), v("VS", 16 + a, 16 + b)), (v("RB"), v("VS", 15 + a, 15 + b)),
+                (v("RA"), v("VS", 16 + RY + a, 16 + RY + b)), (v("RB"), v("VS", 16 + RZ + a, 16 + RZ + b))]
+
+    def dist(a, b):
+        return [(v("O16"), v("XH", 1 + a, 1 + b)), (v("N16"), v("XH", a, b))]
+
+    def gates(a, b):
+        return [(v("G8"), v("SB", 1 + a, 1 + b)), (v("N8"), v("SB", a, b))]
+
+    def probes(t):
+        pat = v("PA%d" % t)
+        scan(v("CC", 0, 33), v("EE", 0, 33), v("OO", 0, 33), 0.0, A.add, A.add)
+        mm(v("B7", 0, 1), v("TRO"), v("CC", 32, 33))
+        msum(v("B6", 0, 32), [(idb, v("CC", 0, 32)), (v("NB"), v("EE", 1, 33)), (v("NA"), v("OO", 1, 33))])
+        mm(v("B6", 32, 33), v("TRI"), v("CC", 32, 33))
+        ts(st(0, 256), v("ISB"), v("B7", 0, 1), A.is_ge, col(SGN), A.mult)
+        msum(v("B1", 0, 256), [(v("OTM"), st(0, 256)), (v("PQ4"), st(0, 256))])
+        tt(v("T7"), v("B6", 0, 32), v("JK"), A.min)
+        ts(v("OC"), v("T7"), v("B6", 32, 33), A.add, RY + RZ + 0.0, A.add)
+        ts(v("PO16"), v("B1", 0, 256), 2064.0, A.add)
+        cp(indw(v("VS", 16, 5136), v("OC")), v("VT%d" % t))
+        for a in range(0, 256, 64):
+            act(v("PX", 16 * a, 16 * a + 1024), ind(pat, v("PO16", a, a + 64)), AF.Copy)
+        msum(v("B0", 0, 64), [(v("OTM"), st(0, 64))] + start_of(0, 64))
+        msum(v("B2", 64, 256), [(v("OTM"), st(64, 256))] + start_of(64, 256))
+        msum(v("B1", 256, 512), [(v("O0M"), st(0, 256))] + start_of(0, 256))
         if t == 0:
-            cp(indw(v("TX"), v("OT")), v("NV"))
-        tt(v("GD"), v("B2", 0, 8), v("DF"), A.mult)
-        tt(v("MC%d" % t), v("B2", 8, 16), v("GD"), A.add)
-        send(to, "ac%d" % t, "LC%d" % t, v("MC%d" % t))
+            for a in (0, 16 + RY, 16 + RZ):
+                iota(v("VS", a, a + 272), [[0, 272]], 0, 0)
+
+        def compare(a, b):
+            tt(v("NQ", 16 * a, 16 * b), ind(v("TX"), v("TO16", a, b)), v("PX", 16 * a, 16 * b), A.not_equal)
+
+        def count(bank, a):
+            mm(v(bank, a, a + 64), v("INA"), st(a, a + 64), True, False)
+            fold(bank, a, 64, "NQ", 16 * a, zall, False, True)
+
+        ts(v("TO16", 0, 64), v("B0", 0, 64), 16.0, A.add)
+        compare(0, 64)
+        ts(v("TO16", 64, 256), v("B2", 64, 256), 16.0, A.add)
+        ts(v("XH", 1, 257), v("B1", 256, 512), -2048.0, A.add)
+        act(v("Y", 0, 4096 - 16 * OWN), ind(v("TX"), v("TO16", OWN, 256)), AF.Copy)
+        fold("B0", 256, 16, "XH", 1, zall)
+        msum(v("B6", 0, 256), [(v("OTM"), st(0, 256))] + dist(0, 256) + [(v("PMA"), st(0, 256)), (v("PMB"), st(0, 256, 1))])
+        act(v("GT"), v("B6", 0, 256), AF.Sign, bias=511.5, scale=-1.0)
+        count("B3", 0)
+        compare(64, 128)
+        count("B3", 64)
+        ts(v("OX"), v("B0", 256, 272), 1.0 / 16, A.mult, 2064.0, A.add)
+        ts(v("XL"), v("B0", 256, 272), 1.0 / 16, A.mult, 0.25, A.add)
+        compare(128, 192)
+        differ(v("NQ", 16 * OWN, 4096), v("Y", 0, 4096 - 16 * OWN), v("PX", 16 * OWN, 4096), "B5")
+        count("B3", 128)
+        compare(192, OWN)
+
+        def named(b2, b1, a, b, first, last):
+            if first:
+                msum(v(b2, a, b), [(v("I8"), v("GT", a, b))] + dist(a, b), True, False)
+                msum(v(b1, a, b), [(v("I8"), v("GT", a, b)), (v("OTM"), st(a, b))] + dist(a, b), True, False)
+            if last:
+                msum(v(b2, a, b), gates(a, b), False, True)
+                msum(v(b1, a, b), gates(a, b), False, True)
+                mm(v("B1", a, b), v("G8"), v("SB", 1 + a, 1 + b))
+
+        def after_named(b2, b1, a, b):
+            ts(v("R2", a, b), v(b2, a, b), col(HC), A.add, 0.0, A.max)
+            act(v("R1", a, b), v(b1, a, b), AF.Relu, bias=col(HC))
+            act(v("FI", a, b), v("B1", a, b), AF.Relu, bias=col(NII), scale=1.0 / GATE)
+
+        act(v("SB", 1, 193), v("B3", 0, 192), AF.Sign, bias=-6.5)
+        named("B6", "B7", 0, 192, True, True)
+        named("B0", "B2", 192, 256, True, False)
+        count("B4", 192)
+        anywhere(act, v("NV"), ind(v("TX"), v("OX")), AF.Identity, bias=255.0, scale=-1.0)
+        act(v("SB", 193, 257), v("B4", 192, 256), AF.Sign, bias=-6.5)
+        after_named("B6", "B7", 0, 192)
+        named("B0", "B2", 192, 256, False, True)
+        after_named("B0", "B2", 192, 256)
+
+    def writes(t):
+        d2 = [(v("ON"), v("R2", 0, 256, 2)), (v("ON"), v("R2", 1, 256, 2))]
+        key = [(v("PQ4"), st(0, 256, 0, 2))] + d2
+        msum(v("B5", 0, 128), key)
+        msum(v("B3", 0, 128), d2)
+        fold("B0", 0, 16, "SB", 1, to_row("Z64"))
+        msum(v("B7", 256, 384), [(v("R0C"), v("R1", 0, 256, 2)), (v("R0C"), v("R1", 1, 256, 2))])
+        act(v("NN"), v("B3", 0, 128), AF.Relu, bias=1.0, scale=-1.0)
+        act(v("MA%d" % t), v("B7", 256, 384), AF.Identity, bias=col(MAB))
+        send(*ways(t), "aa%d" % t, "LA%d" % t, v("MA%d" % t))
+        tt(v("MK2"), v("B5", 0, 128), v("DM", 0, 128), A.mult)
+        cp(v("XW"), v("B5", 0, 128))
+        scan(v("QS2"), v("RS", 0, 128), v("MK2"), 0.0, A.mult, A.add)
+        msum(v("B6", 0, 128), key + [(v("I8"), v("NN"))], True, False)
+        for u in range(8):
+            e0, e1 = 144 * u, 128 * u + 128
+            ts(v("E", e0, e1), v("XW", 16 * u, 128), v("QS2", 16 * u + 15, 16 * u + 16), A.is_equal)
+            mm(v("B6", 16 * u, 16 * u + 16), v("T8K"), v("E", e0, e0 + 16), False, u == 7)
+            if u < 7:
+                mm(v("B6", 16 * u + 16, 128), v("O8K"), v("E", e0 + 16, e1), False, False)
+
+        def text(u):
+            e0, e1 = 272 * u, 256 * u + 256
+            ts(v("NQ", e0, e1), v("XH", 1 + 16 * u, 257), v("XL", u, u + 1), A.subtract, v("B0", u, u + 1), A.is_equal)
+            mm(v("B4", 16 * u, 16 * u + 16), v("T8K"), v("NQ", e0, e0 + 16), False, u == 15)
+            if u < 15:
+                mm(v("B4", 16 * u + 16, 256), v("O8K"), v("NQ", e0 + 16, e1), False, False)
+
+        msum(v("B4", 0, 256), [(v("O16"), v("XH", 1, 257)), (v("O8K"), v("FI", 0, 256))], True, False)
+        text(0)
+        tt(v("MK2"), v("B6", 0, 128), v("TRM", 16, 144), A.min)
+        text(1)
+        scan(v("QS2"), v("RS", 0, 128), v("MK2"), 0.0, A.mult, A.add)
+        text(2)
+        ts(v("MB%d" % t), v("QS2", 15, 128, 16), 16 * 2048.0, A.add)
+        send(*ways(t), "ab%d" % t, "LB%d" % t, v("MB%d" % t))
+        for u in range(3, 16):
+            text(u)
+        msum(v("B2", 256, 512), [(v("NI"), v("ISB")), (v("OH"), st(0, 256)), (v("O8K"), v("FI", 0, 256))])
+        tt(v("MK"), v("B4", 0, 256), v("TRM"), A.min)
+        scan(v("QS"), v("RS"), v("MK"), 0.0, A.mult, A.add)
+        ts(v("OT"), v("QS", 15, 256, 16), 16 * 2048.0 + 16.0, A.add)
+        cp(indw(v("TX"), v("OT")), v("NV"))
+        for f in reorder(t):
+            f()
         if t:
-            cp(indw(v("TX"), v("OT")), v("NV"))
-        if t:
-            dma("y", "dyt", hb(T.yt[:]), v("TX", 0, 4096))
+            dma("y", "dyt", hb(T.yt[:]), v("TX", 16, 4112), 4000)
             own_witnesses(v("MA0"), v("MB0"))
             own_witnesses(v("LA1"), v("LB1"))
             dma("s", "dyw", hb(T.yw[:]), (T.FO[0:128:16, 0:4096], [("FO", 0, 4096)]))
             dma("y", "dyo", hb(T.yo[:]), v("LC1"))
 
-    one_round(0)
-    one_round(1)
+    for t in range(2):
+        stage1(t)
+        stage2(t)
+        probes(t)
+        writes(t)
 
+    for k in range(len(ops) - 1, -1, -1):
+        o = ops[k]
+        o["way"] = o.get("way", 0) + o["cost"] + o["late"]
+        for j in o["deps"]:
+            ops[j]["way"] = max(ops[j].get("way", 0), o["way"] + WAKE)
+        for j in o["behind"]:
+            ops[j]["way"] = max(ops[j].get("way", 0), o["way"] + 1 - ops[j]["late"])
+    def place(order, lags, floor):
+        busy, at = {q: [] for q in eng}, {}
+        for k in order:
+            o = ops[k]
+            x = max([at[j] + ops[j]["cost"] + lag for j, lag in lags[k]] + [floor[k]])
+            if o["q"] is not None:
+                line, j = busy[o["q"]], 0
+                while j < len(line) and line[j][0] < x + o["cost"]:
+                    x = max(x, line[j][1])
+                    j += 1
+                line.insert(j, (x, x + o["cost"]))
+            at[k] = x
+        return at
+
+    if not _PLAN:
+        every = range(len(ops))
+        ahead = [[(j, ops[j]["late"] + WAKE) for j in o["deps"]] + [(j, 0) for j in o["behind"]] for o in ops]
+        back = [[] for _ in ops]
+        for k in every:
+            for j, lag in ahead[k]:
+                back[j].append((k, lag))
+        order = sorted(every, key=lambda j: (-ops[j]["way"], j))
+        for _ in range(PASSES):
+            at = place(order, ahead, [0] * len(ops))
+            span = max(at[k] + ops[k]["cost"] + ops[k]["late"] for k in every)
+            if not _PLAN or span < _PLAN[0]:
+                _PLAN[:] = [span, at]
+            rev = place(sorted(every, key=lambda j: (-at[j] - ops[j]["cost"], -j)), back, [o["late"] for o in ops])
+            order = sorted(every, key=lambda j: (-rev[j] - ops[j]["cost"], j))
+    for k, o in enumerate(ops):
+        o["start"] = _PLAN[1][k]
+        o["end"] = o["start"] + o["cost"] + o["late"]
     total, known = {}, {q: {} for q in eng}
-    for o in ops:
+    for o in sorted(ops, key=lambda x: x["start"]):
         total[o["sem"]] = total.get(o["sem"], 0) + o["inc"]
         o["at"] = total[o["sem"]]
         q = o["q"]
@@ -572,7 +695,7 @@ def rank_program(g, core, T, topo):
             o["clock"] = {o["sem"]: o["at"]}
             continue
         kn = known[q]
-        for k in sorted(o["deps"], reverse=True):
+        for k in sorted(o["deps"], key=lambda j: -ops[j]["end"]):
             d = ops[k]
             if kn.get(d["sem"], 0) < d["at"]:
                 eng[q].wait_ge(T.sem[d["sem"]], d["at"])

@@ -14,13 +14,14 @@ _SB = {
     "TRM": (256, F), "JK": (32, F), "XO": (8, U),
     "AH": (130, H), "NAH": (130, H), "HI": (128, I), "LO": (128, I), "HB": (128, B), "LB": (128, B), "C1": (128, F), "C2": (128, F),
     "OW0": (64, U), "OW1": (64, U), "VT0": (512, B), "VT1": (512, B), "A10": (64, F), "A11": (64, F), "AB0": (64, F), "AB1": (64, F),
-    "WG": (1024, B), "Y": (1024, B), "NJ": (1040, B), "N2": (528, B), "NQ": (4096, B), "PX": (4096, B), "E": (4096, B), "EV": (512, B),
+    "WG": (1024, B), "Y": (1024, B), "NJ": (1040, B), "N2": (528, B), "NQ": (4096, B), "PX": (4096, B), "E3": (1024, B), "E4": (4096, B), "EV": (512, B),
     "T1": (64, F), "T2": (64, F), "T3": (64, F), "T4": (64, F), "T5": (32, F), "T6": (32, F), "T7": (32, F), "OY": (64, U), "O1": (64, U), "O2": (64, U), "TH": (64, F),
     "UB": (64, F), "S1": (66, F), "UN": (64, F), "M2": (32, F), "PV": (32, F), "DD": (32, F), "OW2": (32, U), "C2B": (32, F),
     "EB": (34, F), "AO1": (32, F), "NE": (32, F), "O65": (32, F), "KJ": (32, F), "AEV": (32, F), "AOD": (32, F),
     "SR": (32, B), "SQ": (34, F), "EE": (34, B), "OO": (34, B), "CC": (34, B), "OC": (32, U), "ST": (258, B),
-    "OX0": (128, H), "OTM": (128, H), "O0M": (128, H), "PO16": (256, U), "TO16": (256, U), "XH": (258, H), "XL": (16, F), "OX": (16, U),
-    "GT": (256, B), "SB": (258, B), "FI": (258, B), "R2": (256, H), "R1": (256, F), "XW": (128, H), "NN": (128, B),
+    "OX0": (128, H), "OTM": (128, H), "O0M": (128, H), "RD": (32, B), "PC": (32, B), "M2I": (32, F), "OQ": (32, U), "PG": (512, B),
+    "PT": (512, B), "LT": (2048, B), "NST": (256, B), "YB": (2816, B), "TO16": (256, U), "XH": (258, H), "XL": (16, F), "OX": (16, U),
+    "GT": (256, B), "SB": (258, B), "FI": (258, B), "R2": (256, H), "R1": (256, H), "XW": (128, H), "NN": (128, B),
     "MK": (256, F), "QS": (256, F), "MK2": (128, F), "QS2": (128, F), "OT": (16, U), "NV": (256, B),
     "R0": (8, F), "SP": (2, U), "F1": (16, B), "YO": (8, F), "DF": (8, F), "GD": (8, F),
     "MA0": (128, F), "MA1": (128, F), "MB0": (8, U), "MB1": (8, U), "MC0": (8, F), "MC1": (8, F),
@@ -35,6 +36,9 @@ for _k, (_n, _d) in _SB.items():
     if _d == B and _n == 128:
         _BT[_k] = 128 * len(_BT)
 SCRATCH = {k: ("sbuf", [128, n], d) for k, (n, d) in _SB.items() if k not in _AT and k not in _BT}
+_ROWS = {"E3": (8, 128), "E4": (16, 256), "LT": (16, 128)}
+for _k, (_r, _n) in _ROWS.items():
+    SCRATCH[_k] = ("sbuf", [128, _r, _n], B)
 SCRATCH["POOL"] = ("sbuf", [128, 72 * len(_AT)], F)
 SCRATCH["MATS"] = ("sbuf", [128, 128 * len(_BT)], B)
 for _b in range(8):
@@ -48,7 +52,7 @@ AF = ActivationFunctionType
 BIG = 12288.0
 GATHER, SCATTER, FIX, WAKE, TENSOR = 1.5, 3.5, 50, 70, 0.5
 PASSES, _PLAN = 8, []
-OWN = 240
+SH, SA, SB1 = 64, 96, 172
 GATE = 8192.0
 RY, RZ, RJ = 1536, 2560, 3584
 
@@ -60,7 +64,7 @@ def rank_program(g, core, T, topo):
     n = len(T.cores)
     before, after = T.cores[(rank - 1) % n], T.cores[(rank + 1) % n]
     eng = {"v": g.vector, "s": g.scalar, "t": g.tensor, "g": g, "y": g.sync}
-    ops, acc, banks, last, loose = [], {}, {}, {}, []
+    ops, acc, banks, last, loose, strict = [], {}, {}, {}, [], []
 
     def anywhere(f, *a, **k):
         loose.append(1)
@@ -126,7 +130,7 @@ def rank_program(g, core, T, topo):
                     if lo < hi2 and lo2 < hi and not (st == st2 and (lo - lo2) % st):
                         deps.add(k2)
         deps.discard(k)
-        if any(isinstance(x, tuple) and len(x) > 2 for x in reads[:1] + writes) and not loose:
+        if (q in strict or any(isinstance(x, tuple) and len(x) > 2 for x in reads[:1] + writes)) and not loose:
             if q in last:
                 behind.add(last[q])
             last[q] = k
@@ -166,7 +170,7 @@ def rank_program(g, core, T, topo):
 
     def mm(o, l, r, start=True, stop=True):
         note("t", lambda: g.tensor.matmul(o[0], l[0], r[0], start, stop), [l, r], [o],
-             cost=TENSOR * max(64, size(r)[0]) * (4 if size(r)[1] == 4 else 1))
+             cost=TENSOR * max(64, size(o)[0]) * (4 if size(r)[1] == 4 else 1))
 
     def msum(o, terms, start=True, stop=True):
         for j, (l, r) in enumerate(terms):
@@ -184,10 +188,10 @@ def rank_program(g, core, T, topo):
     def dma(q, sem, o, a, late=2000):
         note(q, lambda: eng[q].dma_start(o[0], a[0]), [a], [o], sem=sem, inc=16, late=late)
 
-    def send(dst, src_core, sem, land, src, late=2200):
+    def send(dst, src_core, sem, land, src, late=2200, cost=200):
         rid, pid, _se = topo.addr(dst)
         note("g", lambda: g.remote_dma(T[land][:], src[0], T.sem[sem], T.sem.sent, pid, rid, topo.mask(core, dst)),
-             [src], [], sem="sent", inc=len(topo.engines(core, dst)), cost=100)
+             [src], [], sem="sent", inc=len(topo.engines(core, dst)), cost=cost)
         note(None, None, [], [v(land)], sem=sem, inc=len(topo.engines(src_core, core)), cost=0, late=late)
         ops[-1]["behind"].add(len(ops) - 2)
 
@@ -213,14 +217,18 @@ def rank_program(g, core, T, topo):
     for k in range(1, len(ops)):
         ops[k]["behind"].add(k - 1)
 
-    (K, II, G16, ODD, PP, GC, EVEN, NE0, MINC, ADDC, WW, C15, SGN, CA, CB, P4, CO1, CBO, BB1, HC, NII, MAB, CMA, CMB, CIN, CJK) = range(26)
+    (K, II, G16, ODD, PP, GC, GP, EVEN, NE0, MINC, ADDC, WW, C15, SGN, CA, CB, P4, CO1, CBO, BB1, HC, NII, MAB, CMA, CMB, CIN, CJK,
+     CRD, CPC) = range(29)
+    strict[:] = "g"
     iota(v("KI", 0, 1), [[0, 1]], 0, 1, False)
-    iota(v("IS"), [[1, 256]], 0, 0)
+    iota(v("IS", 0, 160), [[1, 160]], 0, 0)
     iota(v("KF"), [[1, 18]], -1, 1)
     iota(v("GM"), [[1, 8], [0, 16]], 0, 0)
     iota(v("PCH"), [[0, 2], [512, 8], [0, 8]], 272, 0)
+    iota(v("IS", 160, 256), [[1, 96]], 160, 0)
     iota(v("MM"), [[0, 16], [1, 16]], 0, 0)
     iota(v("ISB"), [[1, 256]], 0, 0)
+    iota(v("M2I"), [[0, 16], [1, 2]], 0, 0)
     for o, c in ((v("DT", 0, 1), -1.0), (v("DT", 512, 520), -1.0), (v("TX", 0, 16), 0.0), (v("PA0", 0, 16), 0.0),
                  (v("AH", 128, 130), 0.0), (v("NAH", 128, 130), 0.0)):
         ms(o, c)
@@ -230,7 +238,8 @@ def rank_program(g, core, T, topo):
     ts(v("KI", ODD, ODD + 1), k0, 1, A.bitwise_and)
     ts(v("KI", PP, PP + 1), k0, 1, A.arith_shift_right, 7, A.bitwise_and)
     ts(v("KI", GC, GC + 1), k0, 4, A.arith_shift_right)
-    cp(v("CL", 0, 6), v("KI", 0, 6))
+    ts(v("KI", GP, GP + 1), k0, 4, A.arith_shift_right, 1, A.bitwise_and)
+    cp(v("CL", 0, 7), v("KI", 0, 7))
     i128, idb = v("IS", 0, 128), v("ID", 16, 144)
 
     def kf(d):
@@ -242,23 +251,25 @@ def rank_program(g, core, T, topo):
     def lin(k, src, a, b):
         ts(col(k), src, a, A.mult, b, A.add)
 
+    strict[:] = "gvs"
+    ts(v("ID"), v("IS", 0, 160), kf(16), A.is_equal)
     ts(v("RM"), v("IS", 0, 16), col(II), A.is_equal)
+    ts(v("ON"), v("GM"), col(GC), A.is_equal)
+    act(v("TM"), v("ON"), AF.Identity)
+    act(v("N8"), v("ON"), AF.Identity, scale=-GATE)
+    act(v("O8K"), v("ON"), AF.Identity, scale=GATE)
+    strict[:] = "g"
     ts(v("RP"), v("IS", 0, 8), col(PP), A.is_equal)
     lin(NE0, rm(0), -1.0, 1.0)
     lin(MINC, col(ODD), -999.0, 1000.0)
     lin(ADDC, col(ODD), 255.0, -256.0)
     lin(WW, col(ODD), 16383.0, 1.0)
-    ts(v("ID"), v("IS", 0, 160), kf(16), A.is_equal)
     ts(v("SH"), i128, kf(-1), A.is_equal, col(NE0), A.mult)
     ts(v("WR"), i128, kf(15), A.is_equal, rm(0), A.mult)
     ts(v("Z"), v("IS", 0, 144), 15.0, A.subtract, col(G16), A.is_equal)
-    ts(v("ON"), v("GM"), col(GC), A.is_equal)
     lin(C15, rm(15), 512.0, 0.0)
     lin(EVEN, col(ODD), -1.0, 1.0)
     act(v("ZW"), v("Z"), AF.Identity, scale=col(WW))
-    act(v("TM"), v("ON"), AF.Identity)
-    act(v("O8K"), v("ON"), AF.Identity, scale=GATE)
-    act(v("N8"), v("ON"), AF.Identity, scale=-GATE)
     for k in range(8):
         act(v("VM", 130 * k, 130 * k + 130), v("ID", 14 + 2 * k, 144 + 2 * k), AF.Identity, scale=v("RP", k, k + 1))
 
@@ -273,24 +284,26 @@ def rank_program(g, core, T, topo):
     ts(v("DT", 1, 512), dti, col(MINC), A.min, col(ADDC), A.add)
     act(v("C2"), v("B6", 128, 256), AF.Identity)
     act(v("C1"), v("B6", 0, 128), AF.Identity)
-    send(before, after, "adn", "DN", v("DT"), 3500)
     run = [[1, 128]]
-    select(v("IDF"), v("TM"), run, A.is_equal, 0.0, 0, -1)
-    select(v("TRI"), v("ON"), run, A.is_gt, 0.0, 0, -1)
-    select(v("TRO"), v("ON"), [[16, 8], [2, 8], [2, 2]], A.is_gt, 0.0, 0, -1)
+    strict[:] = "g"
     for a in (0, 16 + RY, 16 + RZ):
         iota(v("VS", a, a + 272), [[0, 272]], 0, 0)
-    select(v("T8K"), v("O8K"), run, A.is_gt, 0.0, 0, -1)
-    select(v("G8"), v("N8"), run, A.is_gt, 0.0, 0, -1)
-    select(v("G8"), v("G8"), run, A.not_equal, GATE, 0, -1)
-    send(before, after, "apa", "PA1", v("PA0"), 5000)
-    select(v("TGE"), v("ON"), [[-1, 128]], A.is_ge, 0.0, 0, 1)
+    select(v("IDF"), v("TM"), run, A.is_equal, 0.0, 0, -1)
     select(v("SD"), v("TM"), run, A.is_equal, 0.0, -1, -1)
+    select(v("TRI"), v("ON"), run, A.is_gt, 0.0, 0, -1)
     select(v("SD"), v("SD"), run, A.not_equal, -1.0, 0, -1)
-    select(v("R0C"), v("TM"), [[0, 8], [1, 16]], A.is_equal, 0.0, 0, 0)
+    select(v("TRO"), v("ON"), [[16, 8], [2, 8], [2, 2]], A.is_gt, 0.0, 0, -1)
+    select(v("G8"), v("N8"), run, A.is_gt, 0.0, 0, -1)
+    select(v("T8K"), v("O8K"), run, A.is_gt, 0.0, 0, -1)
+    select(v("G8"), v("G8"), run, A.not_equal, GATE, 0, -1)
     select(v("OH"), v("O8K"), [[-16, 8], [-2, 16]], A.is_ge, 0.0, 0, 1)
+    select(v("R0C"), v("TM"), [[0, 8], [1, 16]], A.is_equal, 0.0, 0, 0)
     select(v("OH"), v("OH"), [[16, 8], [2, 16]], A.is_ge, 0.0, 1, -1)
+    select(v("TGE"), v("ON"), [[-1, 128]], A.is_ge, 0.0, 0, 1)
+    send(before, after, "adn", "DN", v("DT"), 3500, 3000)
+    send(before, after, "apa", "PA1", v("PA0"), 5000)
     iota(v("FN"), [[0, 4240]], -1, 0)
+    strict[:] = ""
 
     def early():
         ts(v("HI"), v("CD"), 4, A.arith_shift_right)
@@ -304,7 +317,13 @@ def rank_program(g, core, T, topo):
         lin(CBO, col(PP), 512.0, 272.0 - BIG)
         lin(BB1, col(PP), 512.0, BIG)
         lin(SGN, col(ODD), -2.0, 1.0)
-        lin(HC, col(II), -GATE, -18.0 * GATE)
+        lin(HC, col(II), -GATE, -25.0 * GATE)
+        ts(col(CRD), col(II), 2.0, A.mult, col(GP), A.add)
+        lin(CPC, col(PP), 512.0, 16.0)
+        ts(v("RD"), v("IS", 0, 32), col(CRD), A.is_equal)
+        ts(v("PC"), v("M2I"), col(GP), A.is_equal, col(CPC), A.mult)
+        for k in range(4):
+            note("v", lambda k=k: g.vector.memset(T.LT[:, 4 * k:4 * k + 4, :], 0.0), [], [(None, [("LT", 5000 + k, 5001 + k)])], cost=256)
         lin(NII, col(II), -1.0, 0.0)
         lin(MAB, rm(0), -256.0, 0.0)
         lin(CMB, col(EVEN), -GATE, 0.0)
@@ -345,7 +364,7 @@ def rank_program(g, core, T, topo):
         act(v("MK"), v("IS"), AF.Identity, bias=4096.0)
 
     def scalar_third():
-        for nm, src, sc in (("PMA", v("ON"), col(CMA)), ("PMB", v("ON"), col(CMB)), ("I8", idb, GATE), ("Z64", v("Z"), 1.0 / 64)):
+        for nm, src, sc in (("PMA", v("ON"), col(CMA)), ("PMB", v("ON"), col(CMB)), ("I8", idb, 8 * GATE), ("Z64", v("Z"), 1.0 / 64)):
             act(v(nm), src, AF.Identity, scale=sc)
         act(v("RS"), v("MM"), AF.Sign)
         act(v("TRM"), v("QS"), AF.Identity, bias=-2048.0)
@@ -366,8 +385,11 @@ def rank_program(g, core, T, topo):
             act(v("A1%d" % t, b, 64, 2), v(bank, 32 * b, 32 * b + 32), AF.Identity, bias=0.5, scale=1.0 / 8192.0)
             act(v("AB%d" % t, b, 64, 2), v(bank, 32 * b, 32 * b + 32), AF.Identity, bias=4096.0 - BIG)
 
-    def places(pf):
-        anywhere(tt, v("OX0"), ind(pf, v("XO")), v("ON"), A.mult)
+    def places(pf, pat):
+        note("v", lambda: g.vector.transpose(T.PT[:], T.PG[:]), [v("PG")], [v("PT")], cost=256)
+        for a in range(4):
+            note("s", lambda a=a: g.scalar.activation(T.LT[32 * a:32 * a + 32, :, 32 * a:32 * a + 32], T.PT[32 * a:32 * a + 32, :], AF.Copy),
+                 [v("PT"), (None, [("LT", 5000, 5004)])], [(None, [("LT", 512 * a, 512 * a + 512)])], cost=512)
         note("v", lambda: g.vector.transpose(T.OTM[:], T.OX0[:]), [v("OX0")], [v("OTM")])
         reduce(v("R0", 1, 2), v("OTM", 0, 128, 16), A.add)
         ts(v("O0M"), v("ON"), v("R0", 1, 2), A.mult)
@@ -381,11 +403,11 @@ def rank_program(g, core, T, topo):
         act(out, v("EV", 0, k), AF.Sign)
 
     def own_witnesses(vals, offs):
-        anywhere(ts, indw(v("FO"), offs), vals, 1.0, A.mult, 256.0, A.add)
+        ts(indw(v("FO"), offs), vals, 1.0, A.mult, 256.0, A.add)
 
     def reorder(t):
         pf = v("LC0") if t else v("PF")
-        return [lambda: reduce(v("R0", 0, 1), v("B2", 256, 512), A.max, True),
+        return [lambda: reduce(v("R0", 0, 1), v("B4", 256, 512), A.max, True),
                 lambda: ts(v("SP", 0, 1), v("R0", 0, 1), 2 * GATE, A.add, 256.0, A.min),
                 lambda: anywhere(cp, v("F1"), ind(v("FI"), v("SP", 0, 1))),
                 lambda: (mm(v("B3", 0, 8), v("TGE"), v("F1", 0, 8)), tt(v("YO"), v("F1", 0, 8), pf, A.mult),
@@ -456,8 +478,15 @@ def rank_program(g, core, T, topo):
                     done[kind].append(u)
                     r = v("NJ", 15 + 64 * u, 79 + 64 * u) if kind == "j" else v("NQ", 64 * u, 64 * u + 64)
                     mm(v("B1" if kind == "j" else "B2", 0, 64), zall(u), r, len(done[kind]) == 1, len(done[kind]) == 16)
+        pf = v("LC0") if t else v("PF")
+        tt(v("OX0"), ind(pf, v("XO")), v("ON"), A.mult)
+        msum(v("B3", 16, 48), [(v("OX0"), v("RD")), (idb, v("PC"))])
+        strict[:] = "v"
         ts(v("TH"), v("B1", 0, 64), 6.5, A.is_lt, 6.5, A.mult)
+        cp(v("OQ"), v("B3", 16, 48))
         tt(v("UB"), v("B2", 0, 64), v("TH"), A.is_lt)
+        strict[:] = ""
+        act(v("PG"), ind(v("PA%d" % t), v("OQ")), AF.Copy)
 
     def stage2(t):
         tab, pat = v("FN") if t else v("DT"), v("PA%d" % t)
@@ -479,7 +508,7 @@ def rank_program(g, core, T, topo):
         ts(v("AO1"), alo, 20.0, A.mult, 6.5, A.add)
         ts(v("NE"), ale, -6.5, A.mult, 6.5, A.add)
         ts(v("O65"), alo, 6.5, A.mult)
-        places(v("LC0") if t else v("PF"))
+        places(v("LC0") if t else v("PF"), pat)
         ts(v("OY", 0, 32), w, -3824.0, A.add)
         tt(v("T2", 0, 32), w, v("C2B"), A.add)
         tt(v("T1", 0, 32), w, v("PV"), A.subtract)
@@ -526,116 +555,190 @@ def rank_program(g, core, T, topo):
         msum(v("B6", 0, 32), [(idb, v("CC", 0, 32)), (v("NB"), v("EE", 1, 33)), (v("NA"), v("OO", 1, 33))])
         mm(v("B6", 32, 33), v("TRI"), v("CC", 32, 33))
         ts(st(0, 256), v("ISB"), v("B7", 0, 1), A.is_ge, col(SGN), A.mult)
-        msum(v("B1", 0, 256), [(v("OTM"), st(0, 256)), (v("PQ4"), st(0, 256))])
         tt(v("T7"), v("B6", 0, 32), v("JK"), A.min)
         ts(v("OC"), v("T7"), v("B6", 32, 33), A.add, RY + RZ + 0.0, A.add)
-        ts(v("PO16"), v("B1", 0, 256), 2064.0, A.add)
         cp(indw(v("VS", 16, 5136), v("OC")), v("VT%d" % t))
-        for a in range(0, 256, 64):
-            act(v("PX", 16 * a, 16 * a + 1024), ind(pat, v("PO16", a, a + 64)), AF.Copy)
-        msum(v("B0", 0, 64), [(v("OTM"), st(0, 64))] + start_of(0, 64))
-        msum(v("B2", 64, 256), [(v("OTM"), st(64, 256))] + start_of(64, 256))
-        msum(v("B1", 256, 512), [(v("O0M"), st(0, 256))] + start_of(0, 256))
+
+        def items(m, a, b, per):
+            return v(("B3", "B4", "B5", "B1")[m // per], (b - a) * (m % per), (b - a) * (m % per + 1))
+
+        def pattern(ms_, a, b, per):
+            for m in ms_:
+                mm(items(m, a, b, per), (T.LT[:, m, :], [("LT", 0, 2048)]), st(a, b))
+
+        strict[:] = "ts"
+        for ms_ in (range(15, 16), range(0, 5), range(5, 10), range(10, 15)):
+            pattern(ms_, 0, SA, 5)
+            for m in ms_:
+                act(v("PX", m, 16 * SA, 16), items(m, 0, SA, 5), AF.Copy)
+        mm(v("B0", SA, SB1), v("OTM"), st(SA, SB1), True, False)
+        mm(v("B2", 0, SA), v("OTM"), st(0, SA), True, False)
+        mm(v("B1", 0, 256), v("O0M"), st(0, 256), True, False)
+        for bank, a, b in (("B6", 0, SB1), ("B7", SB1, 256)):
+            msum(v(bank, a, b), [(v("OTM"), st(a, b)), (v("PMA"), st(a, b)), (v("PMB"), st(a, b, 1))], True, False)
+        pattern(range(12), SA, SB1, 6)
+        msum(v("B0", SA, SB1), start_of(SA, SB1), False, True)
+        msum(v("B2", 0, SA), start_of(0, SA), False, True)
+        strict[:] = "vts"
+        ts(v("TO16", SA, SB1), v("B0", SA, SB1), 16.0, A.add)
+        ts(v("TO16", 0, SA), v("B2", 0, SA), 16.0, A.add)
+        msum(v("B1", 0, 256), start_of(0, 256), False, True)
+        msum(v("B0", SB1, 256), [(v("OTM"), st(SB1, 256))] + start_of(SB1, 256))
+        pattern(range(12, 16), SA, SB1, 6)
         if t == 0:
             for a in (0, 16 + RY, 16 + RZ):
-                iota(v("VS", a, a + 272), [[0, 272]], 0, 0)
+                anywhere(act, v("VS", a, a + 272), v("Y", 0, 272), AF.Identity, scale=0.0)
+
+        def text(a, b):
+            act(v("YB", 16 * (a - SA), 16 * (b - SA)), ind(v("TX"), v("TO16", a, b)), AF.Copy)
 
         def compare(a, b):
             tt(v("NQ", 16 * a, 16 * b), ind(v("TX"), v("TO16", a, b)), v("PX", 16 * a, 16 * b), A.not_equal)
 
-        def count(bank, a):
-            mm(v(bank, a, a + 64), v("INA"), st(a, a + 64), True, False)
-            fold(bank, a, 64, "NQ", 16 * a, zall, False, True)
+        def compare2(bank, c0, a, b, then):
+            mm(v(bank, c0 + a, c0 + b), v("INA"), st(a, b), True, False)
+            for m in range(16):
+                out = v("NQ", 16 * a + (b - a) * m, 16 * a + (b - a) * (m + 1))
+                tt(out, items(m, a, b, 6), v("YB", 16 * (a - SA) + m, 16 * (b - SA), 16), A.not_equal)
+                mm(v(bank, c0 + a, c0 + b), zall(m), out, False, m == 15)
+                then(m)
 
-        ts(v("TO16", 0, 64), v("B0", 0, 64), 16.0, A.add)
-        compare(0, 64)
-        ts(v("TO16", 64, 256), v("B2", 64, 256), 16.0, A.add)
-        ts(v("XH", 1, 257), v("B1", 256, 512), -2048.0, A.add)
-        act(v("Y", 0, 4096 - 16 * OWN), ind(v("TX"), v("TO16", OWN, 256)), AF.Copy)
-        fold("B0", 256, 16, "XH", 1, zall)
-        msum(v("B6", 0, 256), [(v("OTM"), st(0, 256))] + dist(0, 256) + [(v("PMA"), st(0, 256)), (v("PMB"), st(0, 256, 1))])
-        act(v("GT"), v("B6", 0, 256), AF.Sign, bias=511.5, scale=-1.0)
-        count("B3", 0)
-        compare(64, 128)
-        count("B3", 64)
-        ts(v("OX"), v("B0", 256, 272), 1.0 / 16, A.mult, 2064.0, A.add)
-        ts(v("XL"), v("B0", 256, 272), 1.0 / 16, A.mult, 0.25, A.add)
-        compare(128, 192)
-        differ(v("NQ", 16 * OWN, 4096), v("Y", 0, 4096 - 16 * OWN), v("PX", 16 * OWN, 4096), "B5")
-        count("B3", 128)
-        compare(192, OWN)
+        text(SA, SB1)
+        def count(a, b):
+            mm(v("B1", 256 + a, 256 + b), v("INA"), st(a, b), True, False)
+            fold("B1", 256 + a, b - a, "NQ", 16 * a, zall, False, True)
 
-        def named(b2, b1, a, b, first, last):
-            if first:
-                msum(v(b2, a, b), [(v("I8"), v("GT", a, b))] + dist(a, b), True, False)
-                msum(v(b1, a, b), [(v("I8"), v("GT", a, b)), (v("OTM"), st(a, b))] + dist(a, b), True, False)
-            if last:
-                msum(v(b2, a, b), gates(a, b), False, True)
-                msum(v(b1, a, b), gates(a, b), False, True)
-                mm(v("B1", a, b), v("G8"), v("SB", 1 + a, 1 + b))
+        compare(0, 16)
+        ts(v("XH", 1, 257), v("B1", 0, 256), -2048.0, A.add)
+        ts(v("TO16", SB1, 256), v("B0", SB1, 256), 16.0, A.add)
+        for bank, a, b in (("B6", 0, SB1), ("B7", SB1, 256)):
+            msum(v(bank, a, b), dist(a, b), False, True)
+        fold("B2", 256, 16, "XH", 1, zall)
+        msum(v("B0", 256, 256 + SB1), [(v("OTM"), st(0, SB1))] + dist(0, SB1), True, False)
+        compare(16, SH)
+        count(0, SH)
+        for bank, a, b in (("B6", 0, SB1), ("B7", SB1, 256)):
+            act(v("GT", a, b), v(bank, a, b), AF.Sign, bias=511.5, scale=-1.0)
+        text(SB1, 256)
+        ts(v("OX"), v("B2", 256, 272), 1.0 / 16, A.mult, 2064.0, A.add)
+        ts(v("XL"), v("B2", 256, 272), 1.0 / 16, A.mult, 0.25, A.add)
+        compare2("B1", 256, SA, SB1, lambda m: pattern(range(m - m % 6, m + 1), SB1, 256, 6) if m in (5, 11, 15) else None)
+        compare(SH, SA)
+        for bank, a, b in (("B6", 0, SB1), ("B7", SB1, 256)):
+            msum(v(bank, a, b), [(v("I8"), v("GT", a, b))] + dist(a, b), True, False)
+        mm(v("B0", 256, 256 + SB1), v("I8"), v("GT", 0, SB1), False, False)
+        count(SH, SA)
+        act(v("SB", 1, 1 + SB1), v("B1", 256, 256 + SB1), AF.Sign, bias=-6.5)
 
-        def after_named(b2, b1, a, b):
-            ts(v("R2", a, b), v(b2, a, b), col(HC), A.add, 0.0, A.max)
-            act(v("R1", a, b), v(b1, a, b), AF.Relu, bias=col(HC))
-            act(v("FI", a, b), v("B1", a, b), AF.Relu, bias=col(NII), scale=1.0 / GATE)
+        def named(bank, a, b):
+            msum(v(bank, a, b), gates(a, b), False, True)
 
-        act(v("SB", 1, 193), v("B3", 0, 192), AF.Sign, bias=-6.5)
-        named("B6", "B7", 0, 192, True, True)
-        named("B0", "B2", 192, 256, True, False)
-        count("B4", 192)
+        def named2(bank, a, b):
+            ts(v("R2", a, b), v(bank, a, b), col(HC), A.add, 0.0, A.max)
+
+        def value(a, b):
+            ts(v("R1", a, b), v("B0", 256 + a, 256 + b), col(HC), A.add, 0.0, A.max)
+
+        compare2("B2", 0, SB1, 256, lambda m: named("B6", 0, SB1) if m == 8 else None)
+        msum(v("B0", 256, 256 + SB1), gates(0, SB1), False, True)
+        strict[:] = "vt"
         anywhere(act, v("NV"), ind(v("TX"), v("OX")), AF.Identity, bias=255.0, scale=-1.0)
-        act(v("SB", 193, 257), v("B4", 192, 256), AF.Sign, bias=-6.5)
-        after_named("B6", "B7", 0, 192)
-        named("B0", "B2", 192, 256, False, True)
-        after_named("B0", "B2", 192, 256)
+        act(v("SB", 1 + SB1, 257), v("B2", SB1, 256), AF.Sign, bias=-6.5)
+        named2("B6", 0, SB1)
+        value(0, SB1)
 
-    def writes(t):
+        def last():
+            named("B7", SB1, 256)
+            mm(v("B3", 0, 128), v("PQ4"), st(0, 256, 0, 2), True, False)
+            mm(v("B5", 0, 128), v("PQ4"), st(0, 256, 0, 2), True, False)
+            named2("B7", SB1, 256)
+
+        def last_value():
+            msum(v("B0", 256 + SB1, 512), [(v("I8"), v("GT", SB1, 256)), (v("OTM"), st(SB1, 256))] + dist(SB1, 256) + gates(SB1, 256))
+            value(SB1, 256)
+
+        def first():
+            mm(v("B6", 0, 256), v("G8"), v("SB", 1, 257))
+            act(v("FI", 0, 256), v("B6", 0, 256), AF.Relu, bias=col(NII), scale=1.0 / GATE)
+
+        return last, last_value, first
+
+    def rows(name, u, a, b):
+        k, w = _ROWS[name]
+        return (T[name][:, :, a:b], [(name, 0, k * w)]) if u is None else (T[name][:, u, a:b], [(name, w * u + a, w * u + b)])
+
+    def writes(t, last, last_value, first):
         d2 = [(v("ON"), v("R2", 0, 256, 2)), (v("ON"), v("R2", 1, 256, 2))]
-        key = [(v("PQ4"), st(0, 256, 0, 2))] + d2
-        msum(v("B5", 0, 128), key)
-        msum(v("B3", 0, 128), d2)
-        fold("B0", 0, 16, "SB", 1, to_row("Z64"))
-        msum(v("B7", 256, 384), [(v("R0C"), v("R1", 0, 256, 2)), (v("R0C"), v("R1", 1, 256, 2))])
-        act(v("NN"), v("B3", 0, 128), AF.Relu, bias=1.0, scale=-1.0)
-        act(v("MA%d" % t), v("B7", 256, 384), AF.Identity, bias=col(MAB))
-        send(*ways(t), "aa%d" % t, "LA%d" % t, v("MA%d" % t))
-        tt(v("MK2"), v("B5", 0, 128), v("DM", 0, 128), A.mult)
-        cp(v("XW"), v("B5", 0, 128))
-        scan(v("QS2"), v("RS", 0, 128), v("MK2"), 0.0, A.mult, A.add)
-        msum(v("B6", 0, 128), key + [(v("I8"), v("NN"))], True, False)
-        for u in range(8):
-            e0, e1 = 144 * u, 128 * u + 128
-            ts(v("E", e0, e1), v("XW", 16 * u, 128), v("QS2", 16 * u + 15, 16 * u + 16), A.is_equal)
-            mm(v("B6", 16 * u, 16 * u + 16), v("T8K"), v("E", e0, e0 + 16), False, u == 7)
-            if u < 7:
-                mm(v("B6", 16 * u + 16, 128), v("O8K"), v("E", e0 + 16, e1), False, False)
 
-        def text(u):
-            e0, e1 = 272 * u, 256 * u + 256
-            ts(v("NQ", e0, e1), v("XH", 1 + 16 * u, 257), v("XL", u, u + 1), A.subtract, v("B0", u, u + 1), A.is_equal)
-            mm(v("B4", 16 * u, 16 * u + 16), v("T8K"), v("NQ", e0, e0 + 16), False, u == 15)
-            if u < 15:
-                mm(v("B4", 16 * u + 16, 256), v("O8K"), v("NQ", e0 + 16, e1), False, False)
+        def accepted(a, b):
+            for i in range(a, b):
+                mm(v("B2", 0, 16), to_row("Z64")(i), v("SB", 1 + i, 242 + i, 16), i == 0, i == 15)
 
-        msum(v("B4", 0, 256), [(v("O16"), v("XH", 1, 257)), (v("O8K"), v("FI", 0, 256))], True, False)
-        text(0)
-        tt(v("MK2"), v("B6", 0, 128), v("TRM", 16, 144), A.min)
-        text(1)
-        scan(v("QS2"), v("RS", 0, 128), v("MK2"), 0.0, A.mult, A.add)
-        text(2)
-        ts(v("MB%d" % t), v("QS2", 15, 128, 16), 16 * 2048.0, A.add)
-        send(*ways(t), "ab%d" % t, "LB%d" % t, v("MB%d" % t))
-        for u in range(3, 16):
-            text(u)
-        msum(v("B2", 256, 512), [(v("NI"), v("ISB")), (v("OH"), st(0, 256)), (v("O8K"), v("FI", 0, 256))])
-        tt(v("MK"), v("B4", 0, 256), v("TRM"), A.min)
-        scan(v("QS"), v("RS"), v("MK"), 0.0, A.mult, A.add)
-        ts(v("OT"), v("QS", 15, 256, 16), 16 * 2048.0 + 16.0, A.add)
-        cp(indw(v("TX"), v("OT")), v("NV"))
-        for f in reorder(t):
+        def keys():
+            msum(v("B3", 0, 128), d2, False, True)
+            tt(v("MK2"), v("B3", 0, 128), v("DM", 0, 128), A.mult)
+            cp(v("XW"), v("B3", 0, 128))
+            scan(v("QS2"), v("RS", 0, 128), v("MK2"), 0.0, A.mult, A.add)
+
+        def unnamed():
+            msum(v("B4", 0, 128), d2)
+            msum(v("B5", 0, 128), d2, False, False)
+            act(v("NN"), v("B4", 0, 128), AF.Relu, bias=1.0, scale=-1.0)
+
+        def same_key():
+            for u in range(8):
+                ts(rows("E3", u, 0, 128 - 16 * u), v("XW", 16 * u, 128), v("QS2", 16 * u + 15, 16 * u + 16), A.is_equal)
+                if u < 7:
+                    mm(v("B5", 16 * u + 16, 128), v("O8K"), rows("E3", u, 16, 128 - 16 * u), False, False)
+            msum(v("B5", 0, 128), [(v("I8"), v("NN")), (v("T8K"), rows("E3", None, 0, 16))], False, True)
+
+        def values():
+            msum(v("B7", 0, 128), [(v("ON"), v("R1", 0, 256, 2)), (v("ON"), v("R1", 1, 256, 2))])
+            act(v("MA%d" % t), v("B7", 0, 128), AF.Identity, bias=col(MAB), scale=rm(0))
+            send(*ways(t), "aa%d" % t, "LA%d" % t, v("MA%d" % t))
+
+        named = [lambda: tt(v("MK2"), v("B5", 0, 128), v("TRM", 16, 144), A.min),
+                 lambda: scan(v("QS2"), v("RS", 0, 128), v("MK2"), 0.0, A.mult, A.add),
+                 lambda: (ts(v("MB%d" % t), v("QS2", 15, 128, 16), 16 * 2048.0, A.add),
+                          send(*ways(t), "ab%d" % t, "LB%d" % t, v("MB%d" % t)))]
+
+        def same_place():
+            mm(v("B1", 0, 256), v("O16"), v("XH", 1, 257), True, False)
+            for u in range(16):
+                ts(rows("E4", u, 0, 256 - 16 * u), v("XH", 1 + 16 * u, 257), v("XL", u, u + 1), A.subtract, v("B2", u, u + 1), A.is_equal)
+                if u < 15:
+                    mm(v("B1", 16 * u + 16, 256), v("O8K"), rows("E4", u, 16, 256 - 16 * u), False, False)
+            msum(v("B1", 0, 256), [(v("O8K"), v("FI", 0, 256)), (v("T8K"), rows("E4", None, 0, 16))], False, True)
+
+        placed = [lambda: tt(v("MK"), v("B1", 0, 256), v("TRM"), A.min),
+                  lambda: scan(v("QS"), v("RS"), v("MK"), 0.0, A.mult, A.add),
+                  lambda: ts(v("OT"), v("QS", 15, 256, 16), 16 * 2048.0 + 16.0, A.add)]
+
+        def lowest():
+            msum(v("B4", 256, 512), [(v("NI"), v("ISB")), (v("OH"), st(0, 256)), (v("O8K"), v("FI", 0, 256))])
+
+        strict[:] = ""
+        part = {}
+        for nm, f in ([("last", last), ("keys", keys), ("unnamed", unnamed), ("value", last_value), ("values", values), ("key", same_key),
+                       ("acc0", lambda: accepted(0, 6)), ("acc1", lambda: accepted(6, 16)), ("first", first), ("lowest", lowest),
+                       ("place", same_place)] + [("n%d" % j, f) for j, f in enumerate(named)] + [("p%d" % j, f) for j, f in enumerate(placed)]
+                      + [("r%d" % j, f) for j, f in enumerate(reorder(t))] + [("text", lambda: anywhere(cp, indw(v("TX"), v("OT")), v("NV")))]):
+            k = len(ops)
             f()
-        if t:
-            dma("y", "dyt", hb(T.yt[:]), v("TX", 16, 4112), 4000)
+            part[nm] = range(k, len(ops))
+
+        def in_turn(q, names):
+            line = [k for nm in names.split() for k in part[nm] if ops[k]["q"] == q]
+            for a, b in zip(line, line[1:]):
+                ops[b]["behind"].add(a)
+
+        if t == 0:
+            in_turn("t", "last keys unnamed value acc0 values key acc1 first lowest place")
+            in_turn("v", "last keys value key n0 n1 n2 place r0 p0 r1 p1 r2 p2")
+        else:
+            in_turn("t", "acc0 acc1 last first keys place unnamed value key values lowest")
+            in_turn("v", "last place keys key p0 value p1 n0 p2 n1 n2 text r0")
+            dma("y", "dyt", hb(T.yt[:]), v("TX", 16, 4112), 5200)
             own_witnesses(v("MA0"), v("MB0"))
             own_witnesses(v("LA1"), v("LB1"))
             dma("s", "dyw", hb(T.yw[:]), (T.FO[0:128:16, 0:4096], [("FO", 0, 4096)]))
@@ -644,16 +747,8 @@ def rank_program(g, core, T, topo):
     for t in range(2):
         stage1(t)
         stage2(t)
-        probes(t)
-        writes(t)
+        writes(t, *probes(t))
 
-    for k in range(len(ops) - 1, -1, -1):
-        o = ops[k]
-        o["way"] = o.get("way", 0) + o["cost"] + o["late"]
-        for j in o["deps"]:
-            ops[j]["way"] = max(ops[j].get("way", 0), o["way"] + WAKE)
-        for j in o["behind"]:
-            ops[j]["way"] = max(ops[j].get("way", 0), o["way"] + 1 - ops[j]["late"])
     def place(order, lags, floor):
         busy, at = {q: [] for q in eng}, {}
         for k in order:
@@ -675,7 +770,16 @@ def rank_program(g, core, T, topo):
         for k in every:
             for j, lag in ahead[k]:
                 back[j].append((k, lag))
-        order = sorted(every, key=lambda j: (-ops[j]["way"], j))
+        waits, order = [len(x) for x in ahead], [k for k in every if not ahead[k]]
+        for k in order:
+            for j, _lag in back[k]:
+                waits[j] -= 1
+                if not waits[j]:
+                    order.append(j)
+        way = {}
+        for k in reversed(order):
+            way[k] = ops[k]["cost"] + max([ops[k]["late"]] + [way[j] + lag for j, lag in back[k]])
+        order = sorted(every, key=lambda j: (-way[j], j))
         for _ in range(PASSES):
             at = place(order, ahead, [0] * len(ops))
             span = max(at[k] + ops[k]["cost"] + ops[k]["late"] for k in every)

from concourse.bass import DstId, RemoteDMATransfer
from concourse.mybir import dt, AluOpType, AxisListType, ActivationFunctionType

F, B, I, U, H = "float32", "bfloat16", "int32", "uint16", "float16"
_SB = {
    "TX": (4368, B), "PA0": (4112, B), "PA1": (4112, B), "FN": (4240, B), "FO": (4240, F), "VS": (5136, B),
    "DTI": (512, I), "DT": (520, B), "DN": (520, B), "DTF": (512, F), "CD": (128, I), "PRI": (8, I), "PF": (8, F),
    "KI": (8, I), "KF": (18, F), "CL": (40, F), "RM": (16, F), "RP": (8, F), "IS": (256, F), "GM": (128, F), "MM": (256, F),
    "ID": (160, B), "SH": (128, B), "WR": (128, B), "Z": (144, B), "ZW": (144, B), "ZP": (8 * 144, B), "ZA": (288, B), "Z64": (144, B),
    "VM": (8 * 130, B), "ON": (128, B), "TM": (128, F), "FC": (128, F), "BC": (128, B), "IDF": (128, F), "SD": (128, F), "R0C": (128, F),
    "TRI": (128, B), "TRO": (128, B), "TGE": (128, B), "O8K": (128, B), "N8": (128, B), "T8K": (128, B), "G8": (128, B), "OH": (128, B),
    "I8": (128, B), "NI": (128, B), "NA": (128, B), "NB": (128, B), "O16": (128, B), "N16": (128, B), "RA": (128, B), "RB": (128, B),
    "PQ4": (128, B), "PMA": (128, B), "PMB": (128, B), "INA": (128, B), "PCH": (128, B), "ISB": (256, B), "DM": (256, B), "RS": (256, B),
    "TRM": (256, F), "JK": (32, F), "XO": (8, U),
    "AH": (130, H), "NAH": (130, H), "HI": (128, I), "LO": (128, I), "HB": (128, B), "LB": (128, B), "C1": (128, F), "C2": (128, F),
    "OW0": (64, U), "OW1": (64, U), "VT0": (512, B), "VT1": (512, B), "A10": (64, F), "A11": (64, F), "AB0": (64, F), "AB1": (64, F),
    "WG": (1024, B), "Y": (1024, B), "NJ": (1040, B), "N2": (528, B), "NQ": (4096, B), "PX": (4096, B), "E3": (1024, B), "E4": (4096, B), "EV": (512, B),
    "T1": (64, F), "T2": (64, F), "T3": (64, F), "T4": (64, F), "T5": (32, F), "T6": (32, F), "T7": (32, F), "OY": (64, U), "O1": (64, U), "O2": (64, U), "TH": (64, F),
    "UB": (64, F), "S1": (66, F), "UN": (64, F), "M2": (32, F), "PV": (32, F), "DD": (32, F), "OW2": (32, U), "C2B": (32, F),
    "EB": (34, F), "AO1": (32, F), "NE": (32, F), "O65": (32, F), "KJ": (32, F), "AEV": (32, F), "AOD": (32, F),
    "SR": (32, B), "SQ": (34, F), "EE": (34, B), "OO": (34, B), "CC": (34, B), "OC": (32, U), "ST": (258, B),
    "OX0": (128, H), "OTM": (128, H), "O0M": (128, H), "RD": (32, B), "PC": (32, B), "M2I": (32, F), "OQ": (32, U), "PG": (512, B),
    "PT": (512, B), "LT": (2048, B), "NST": (256, B), "YB": (2816, B), "TO16": (256, U), "XH": (258, H), "XL": (16, F), "OX": (16, U),
    "GT": (256, B), "SB": (258, B), "FI": (258, B), "R2": (256, H), "R1": (256, H), "XW": (128, H), "NN": (128, B),
    "MK": (256, F), "QS": (256, F), "MK2": (128, F), "QS2": (128, F), "OT": (16, U), "NV": (256, B),
    "R0": (8, F), "SP": (2, U), "F1": (16, B), "YO": (8, F), "DF": (8, F), "GD": (8, F),
    "MA0": (128, F), "MA1": (128, F), "MB0": (8, U), "MB1": (8, U), "MC0": (8, F), "MC1": (8, F),
    "LA0": (128, F), "LA1": (128, F), "LB0": (8, U), "LB1": (8, U), "LC0": (8, F), "LC1": (8, F),
}
_AT = {}
for _k, (_n, _d) in _SB.items():
    if _d == F and _n <= 66 and _k[:2] not in ("MC", "LC"):
        _AT[_k] = 72 * len(_AT)
_BT = {}
for _k, (_n, _d) in _SB.items():
    if _d == B and _n == 128:
        _BT[_k] = 128 * len(_BT)
SCRATCH = {k: ("sbuf", [128, n], d) for k, (n, d) in _SB.items() if k not in _AT and k not in _BT}
_ROWS = {"E3": (8, 128), "E4": (16, 256), "LT": (16, 128)}
for _k, (_r, _n) in _ROWS.items():
    SCRATCH[_k] = ("sbuf", [128, _r, _n], B)
SCRATCH["POOL"] = ("sbuf", [128, 72 * len(_AT)], F)
SCRATCH["MATS"] = ("sbuf", [128, 128 * len(_BT)], B)
for _b in range(8):
    SCRATCH["B%d" % _b] = ("psum", [128, 512], F)
_DMAS = ["dcd", "dpr", "dw0", "dw1", "dtx", "dp0", "dp1", "dp2", "dp3", "dfo", "dn0", "dn1", "dyt", "dyw", "dyo"]
_ARR = ["apa", "adn", "aa0", "ab0", "ac0", "aa1", "ab1", "ac1"]
SEMAPHORES = ["cv", "cs", "ct", "cg", "sent"] + _DMAS + _ARR

A = AluOpType
AF = ActivationFunctionType
BIG = 12288.0
GATHER, SCATTER, FIX, WAKE, TENSOR = 1.5, 3.5, 50, 70, 0.5
PASSES, _PLAN = 8, []
SH, SA, SB1 = 64, 96, 172
GATE = 8192.0
RY, RZ, RJ = 1536, 2560, 3584


def rank_program(g, core, T, topo):
    rank = T.rank_of(core)
    if rank is None:
        return
    n = len(T.cores)
    before, after = T.cores[(rank - 1) % n], T.cores[(rank + 1) % n]
    eng = {"v": g.vector, "s": g.scalar, "t": g.tensor, "g": g, "y": g.sync}
    ops, acc, banks, last, loose, strict = [], {}, {}, {}, [], []

    def anywhere(f, *a, **k):
        loose.append(1)
        f(*a, **k)
        loose.pop()

    def home(name):
        return (T.POOL, _AT[name]) if name in _AT else (T.MATS, _BT[name]) if name in _BT else (T[name], 0)

    def v(name, a=0, b=None, step=1):
        b = _SB[name][0] if b is None else b
        t, o = home(name)
        return (t[:, o + a:o + b:step] if step != 1 else t[:, o + a:o + b], [(name, a, b, step)])

    def rv(name, hi, lo):
        t, o = home(name)
        return (t[:, o + hi::-1] if o + lo == 0 else t[:, o + hi:o + lo - 1:-1], [(name, lo, hi + 1)])

    def ind(win, off):
        return (win[0].indirect(off[0]), win[1] + off[1], [])

    def indw(win, off):
        return (win[0].indirect(off[0]), win[1], off[1])

    def col(k):
        return v("CL", k, k + 1)

    def ap(x):
        return x[0] if isinstance(x, tuple) else x

    def size(x):
        name, lo, hi, st = (x[1][0] + (1,))[:4]
        return (hi - lo + st - 1) // st, 4 if name not in _SB or _SB[name][1] in (F, I) else 2, name not in _SB

    def cycles(o, ins, both=1.0):
        if len(o) > 2:
            return FIX + SCATTER * size(ins[0])[0]
        if ins and len(ins[0]) > 2:
            return FIX + GATHER * size(o)[0]
        if both == 2.0:
            return max(64, size(o)[0] * (1 if any(size(x)[2] for x in ins) else 2))
        return max(64, size((ins or [o])[0])[0] * (both if all(size(x)[1] == 2 for x in ins + [o]) else 1))

    def note(q, fn, reads, writes, sem=None, inc=1, cost=64, late=0):
        k = len(ops)
        deps, behind = set(), set()
        rs = [r for x in reads if isinstance(x, tuple) for r in x[1]] + [r for x in writes if len(x) > 2 for r in x[2]]
        ws = [r for x in writes for r in x[1]]
        for lst, isw in ((rs, False), (ws, True)):
            for r in lst:
                name, lo, hi, st = (r + (1,))[:4]
                if name not in _SB:
                    who, now, past = banks.setdefault(name, [q, [], []])
                    if who != q:
                        now, past = [], now
                    if q == "t":
                        behind.update(now)
                        now = []
                    deps.update(past)
                    banks[name] = [q, now + [k], past]
                    continue
                for lo2, hi2, st2, k2 in acc.get((name, True), []) + (acc.get((name, False), []) if isw else []):
                    if lo < hi2 and lo2 < hi and not (st == st2 and (lo - lo2) % st):
                        deps.add(k2)
        deps.discard(k)
        if (q in strict or any(isinstance(x, tuple) and len(x) > 2 for x in reads[:1] + writes)) and not loose:
            if q in last:
                behind.add(last[q])
            last[q] = k
        for lst, isw in ((rs, False), (ws, True)):
            for r in lst:
                acc.setdefault((r[0], isw), []).append((r[1], r[2], (r + (1,))[3], k))
        ops.append({"q": q, "fn": fn, "deps": deps, "behind": behind, "sem": sem or ("c" + q), "inc": inc, "cost": cost, "late": late})

    def tt(o, a, b, op):
        note("v", lambda: g.vector.tensor_tensor(o[0], a[0], b[0], op), [a, b], [o], cost=cycles(o, [a, b], 2.0))

    def ts(o, a, s1, op0, s2=None, op1=None):
        if op1 is None:
            note("v", lambda: g.vector.tensor_scalar(o[0], a[0], ap(s1), None, op0), [a, s1], [o], cost=cycles(o, [a], 0.5))
        else:
            note("v", lambda: g.vector.tensor_scalar(o[0], a[0], ap(s1), ap(s2), op0, op1), [a, s1, s2], [o], cost=cycles(o, [a], 0.5))

    def cp(o, a):
        note("v", lambda: g.vector.tensor_copy(o[0], a[0]), [a], [o], cost=cycles(o, [a], 0.5))

    def ms(o, c):
        note("v", lambda: g.vector.memset(o[0], c), [], [o], cost=cycles(o, [], 0.5))

    def scan(o, a, b, init, op0, op1):
        note("v", lambda: g.vector.tensor_tensor_scan(o[0], a[0], b[0], ap(init), op0, op1), [a, b, init], [o], cost=cycles(o, [a, b], 0.5))

    def reduce(o, a, op, negate=False):
        note("v", lambda: g.vector.tensor_reduce(o[0], a[0], AxisListType.X, op, negate=negate), [a], [o], cost=cycles(o, [a]))

    def act(o, a, func, bias=None, scale=None):
        kw = {}
        if bias is not None:
            kw["bias"] = ap(bias)
        if scale is not None:
            kw["scale"] = ap(scale)
        note("s", lambda: g.scalar.activation(o[0], a[0], func, **kw), [a, bias, scale], [o], cost=cycles(o, [a]))

    def mm(o, l, r, start=True, stop=True):
        note("t", lambda: g.tensor.matmul(o[0], l[0], r[0], start, stop), [l, r], [o],
             cost=TENSOR * max(64, size(o)[0]) * (4 if size(r)[1] == 4 else 1))

    def msum(o, terms, start=True, stop=True):
        for j, (l, r) in enumerate(terms):
            mm(o, l, r, start and j == 0, stop and j == len(terms) - 1)

    def iota(o, pat, base, ch, flag=True):
        if flag:
            note("g", lambda: g.iota(o[0], pat, base, ch, allow_small_or_imprecise_dtypes=True), [], [o], cost=160 + 2 * size(o)[0])
        else:
            note("g", lambda: g.iota(o[0], pat, base, ch), [], [o], cost=160 + 2 * size(o)[0])

    def select(o, a, pat, op, fill, base, ch):
        note("g", lambda: g.affine_select(o[0], a[0], pat, op, fill, base, ch), [a], [o], cost=200 + 2 * size(o)[0])

    def dma(q, sem, o, a, late=2000):
        note(q, lambda: eng[q].dma_start(o[0], a[0]), [a], [o], sem=sem, inc=16, late=late)

    def send(dst, src_core, sem, land, src, late=2200, cost=200):
        rid, pid, _se = topo.addr(dst)
        note("g", lambda: g.remote_dma(T[land][:], src[0], T.sem[sem], T.sem.sent, pid, rid, topo.mask(core, dst)),
             [src], [], sem="sent", inc=len(topo.engines(core, dst)), cost=cost)
        note(None, None, [], [v(land)], sem=sem, inc=len(topo.engines(src_core, core)), cost=0, late=late)
        ops[-1]["behind"].add(len(ops) - 2)

    def to_row(buf, at=0):
        return lambda i: v(buf, at + 15 - i, at + 143 - i)

    zall = to_row("Z")

    def fold(bank, c0, nn, buf, b0, left, first=True, last=True):
        for i in range(16):
            mm(v(bank, c0, c0 + nn), left(i), v(buf, b0 + i, b0 + i + 16 * nn - 15, 16), first and i == 0, last and i == 15)

    def hb(x):
        return (x, [])

    dma("y", "dcd", v("CD"), hb(T.cd[:]), 2000)
    dma("s", "dw0", (T.DTI[0:128:2, :], [("DTI", 0, 512)]), hb(T.wit[:]), 2300)
    dma("y", "dw1", (T.DTI[1:128:2, :], [("DTI", 1000, 1001)]), hb(T.wit[:]), 2500)
    dma("s", "dpr", v("PRI"), hb(T.prb[:]), 2500)
    dma("y", "dtx", v("TX", 16, 4112), hb(T.txt[:]), 4800)
    for k in range(4):
        dma("y", "dp%d" % k, v("PA0", 16 + 1024 * k, 1040 + 1024 * k), hb(T.pat[:, 1024 * k:1024 * k + 1024]), 5400 + 600 * k)
    for k in range(1, len(ops)):
        ops[k]["behind"].add(k - 1)

    (K, II, G16, ODD, PP, GC, GP, EVEN, NE0, MINC, ADDC, WW, C15, SGN, CA, CB, P4, CO1, CBO, BB1, HC, NII, MAB, CMA, CMB, CIN, CJK,
     CRD, CPC) = range(29)
    strict[:] = "g"
    iota(v("KI", 0, 1), [[0, 1]], 0, 1, False)
    iota(v("IS", 0, 160), [[1, 160]], 0, 0)
    iota(v("KF"), [[1, 18]], -1, 1)
    iota(v("GM"), [[1, 8], [0, 16]], 0, 0)
    iota(v("PCH"), [[0, 2], [512, 8], [0, 8]], 272, 0)
    iota(v("IS", 160, 256), [[1, 96]], 160, 0)
    iota(v("MM"), [[0, 16], [1, 16]], 0, 0)
    iota(v("ISB"), [[1, 256]], 0, 0)
    iota(v("M2I"), [[0, 16], [1, 2]], 0, 0)
    for o, c in ((v("DT", 0, 1), -1.0), (v("DT", 512, 520), -1.0), (v("TX", 0, 16), 0.0), (v("PA0", 0, 16), 0.0),
                 (v("AH", 128, 130), 0.0), (v("NAH", 128, 130), 0.0)):
        ms(o, c)
    k0 = v("KI", 0, 1)
    ts(v("KI", II, II + 1), k0, 15, A.bitwise_and)
    ts(v("KI", G16, G16 + 1), k0, 112, A.bitwise_and)
    ts(v("KI", ODD, ODD + 1), k0, 1, A.bitwise_and)
    ts(v("KI", PP, PP + 1), k0, 1, A.arith_shift_right, 7, A.bitwise_and)
    ts(v("KI", GC, GC + 1), k0, 4, A.arith_shift_right)
    ts(v("KI", GP, GP + 1), k0, 4, A.arith_shift_right, 1, A.bitwise_and)
    cp(v("CL", 0, 7), v("KI", 0, 7))
    i128, idb = v("IS", 0, 128), v("ID", 16, 144)

    def kf(d):
        return v("KF", d + 1, d + 2)

    def rm(r):
        return v("RM", r, r + 1)

    def lin(k, src, a, b):
        ts(col(k), src, a, A.mult, b, A.add)

    strict[:] = "gvs"
    ts(v("ID"), v("IS", 0, 160), kf(16), A.is_equal)
    ts(v("RM"), v("IS", 0, 16), col(II), A.is_equal)
    ts(v("ON"), v("GM"), col(GC), A.is_equal)
    act(v("TM"), v("ON"), AF.Identity)
    act(v("N8"), v("ON"), AF.Identity, scale=-GATE)
    act(v("O8K"), v("ON"), AF.Identity, scale=GATE)
    strict[:] = "g"
    ts(v("RP"), v("IS", 0, 8), col(PP), A.is_equal)
    lin(NE0, rm(0), -1.0, 1.0)
    lin(MINC, col(ODD), -999.0, 1000.0)
    lin(ADDC, col(ODD), 255.0, -256.0)
    lin(WW, col(ODD), 16383.0, 1.0)
    ts(v("SH"), i128, kf(-1), A.is_equal, col(NE0), A.mult)
    ts(v("WR"), i128, kf(15), A.is_equal, rm(0), A.mult)
    ts(v("Z"), v("IS", 0, 144), 15.0, A.subtract, col(G16), A.is_equal)
    lin(C15, rm(15), 512.0, 0.0)
    lin(EVEN, col(ODD), -1.0, 1.0)
    act(v("ZW"), v("Z"), AF.Identity, scale=col(WW))
    for k in range(8):
        act(v("VM", 130 * k, 130 * k + 130), v("ID", 14 + 2 * k, 144 + 2 * k), AF.Identity, scale=v("RP", k, k + 1))

    ts(v("AH", 0, 128), v("CD"), -2048.0, A.add)
    ts(v("NAH", 0, 128), v("CD"), -1.0, A.mult, 2048.0, A.add)
    msum(v("B7", 0, 128), [(v("SH"), v("AH", 0, 128)), (v("WR"), v("AH", 1, 129)), (idb, v("NAH", 0, 128))])
    msum(v("B6", 0, 128), [(idb, v("NAH", 0, 128)), (idb, v("PCH"))])
    msum(v("B6", 128, 256), [(v("SH"), v("NAH", 0, 128)), (v("WR"), v("NAH", 1, 129)), (idb, v("PCH"))])
    dti = (T.DTI[:, 1:512], [("DTI", 0, 512), ("DTI", 1000, 1001)])
    ts(v("OW0"), v("B7", 0, 64), 512.0, A.min)
    ts(v("OW0", 7, 64, 8), v("B7", 7, 64, 8), 512.0, A.min, col(C15), A.max)
    ts(v("DT", 1, 512), dti, col(MINC), A.min, col(ADDC), A.add)
    act(v("C2"), v("B6", 128, 256), AF.Identity)
    act(v("C1"), v("B6", 0, 128), AF.Identity)
    run = [[1, 128]]
    strict[:] = "g"
    for a in (0, 16 + RY, 16 + RZ):
        iota(v("VS", a, a + 272), [[0, 272]], 0, 0)
    select(v("IDF"), v("TM"), run, A.is_equal, 0.0, 0, -1)
    select(v("SD"), v("TM"), run, A.is_equal, 0.0, -1, -1)
    select(v("TRI"), v("ON"), run, A.is_gt, 0.0, 0, -1)
    select(v("SD"), v("SD"), run, A.not_equal, -1.0, 0, -1)
    select(v("TRO"), v("ON"), [[16, 8], [2, 8], [2, 2]], A.is_gt, 0.0, 0, -1)
    select(v("G8"), v("N8"), run, A.is_gt, 0.0, 0, -1)
    select(v("T8K"), v("O8K"), run, A.is_gt, 0.0, 0, -1)
    select(v("G8"), v("G8"), run, A.not_equal, GATE, 0, -1)
    select(v("OH"), v("O8K"), [[-16, 8], [-2, 16]], A.is_ge, 0.0, 0, 1)
    select(v("R0C"), v("TM"), [[0, 8], [1, 16]], A.is_equal, 0.0, 0, 0)
    select(v("OH"), v("OH"), [[16, 8], [2, 16]], A.is_ge, 0.0, 1, -1)
    select(v("TGE"), v("ON"), [[-1, 128]], A.is_ge, 0.0, 0, 1)
    send(before, after, "adn", "DN", v("DT"), 3500, 3000)
    send(before, after, "apa", "PA1", v("PA0"), 5000)
    iota(v("FN"), [[0, 4240]], -1, 0)
    strict[:] = ""

    def early():
        ts(v("HI"), v("CD"), 4, A.arith_shift_right)
        ts(v("LO"), v("CD"), 15, A.bitwise_and)
        cp(v("HB"), v("HI"))
        cp(v("LB"), v("LO"))
        ts(col(CA), rm(0), 16.0, A.mult, rm(2), A.add)
        ts(col(CB), rm(1), 16.0, A.mult, rm(3), A.add)
        lin(P4, col(PP), 512.0, -2048.0)
        lin(CO1, col(PP), 512.0, 272.0)
        lin(CBO, col(PP), 512.0, 272.0 - BIG)
        lin(BB1, col(PP), 512.0, BIG)
        lin(SGN, col(ODD), -2.0, 1.0)
        lin(HC, col(II), -GATE, -25.0 * GATE)
        ts(col(CRD), col(II), 2.0, A.mult, col(GP), A.add)
        lin(CPC, col(PP), 512.0, 16.0)
        ts(v("RD"), v("IS", 0, 32), col(CRD), A.is_equal)
        ts(v("PC"), v("M2I"), col(GP), A.is_equal, col(CPC), A.mult)
        for k in range(4):
            note("v", lambda k=k: g.vector.memset(T.LT[:, 4 * k:4 * k + 4, :], 0.0), [], [(None, [("LT", 5000 + k, 5001 + k)])], cost=256)
        lin(NII, col(II), -1.0, 0.0)
        lin(MAB, rm(0), -256.0, 0.0)
        lin(CMB, col(EVEN), -GATE, 0.0)
        ts(col(CMA), col(EVEN), rm(15), A.subtract, GATE, A.mult)
        lin(CIN, rm(15), -16.0, 0.0)
        lin(CJK, col(II), 32.0, RJ - RY - RZ + 0.0)
        ts(v("FC"), i128, kf(1), A.is_equal, col(EVEN), A.mult)
        ts(v("BC"), i128, kf(-1), A.is_equal, col(ODD), A.mult)
        ts(v("JK"), v("IS", 0, 32), col(CJK), A.add)
        ts(v("XO"), v("IS", 0, 8), 0.0, A.mult, col(PP), A.add)
        cp(v("PF"), v("PRI"))
        cp(v("DTF", 0, 1), (T.DTI[:, 0:1], dti[1]))
        ts(v("T3"), v("B7", 64, 128), 512.0, A.min)
        ts(v("T3", 7, 64, 8), v("B7", 71, 128, 8), 512.0, A.min, col(C15), A.max)
        tt(v("T4"), v("T3"), v("PCH", 0, 64), A.add)
        ts(v("OW1"), v("T4"), -272.0, A.add)
        ts(v("DM"), v("MM"), col(II), A.is_equal)
        for o in (v("TX", 4112, 4368), v("NJ", 0, 16), v("N2", 512, 528), v("XH", 0, 1)):
            ms(o, 0.0)

    def fill(o, c):
        act(o, v("IS", 0, o[1][0][2] - o[1][0][1]), AF.Identity, bias=c, scale=0.0)

    def scalar_first():
        for k in range(8):
            act(v("ZP", 144 * k, 144 * k + 144), v("ZW"), AF.Identity, scale=v("RP", k, k + 1))
        act(v("ZA", 0, 144), v("Z"), AF.Identity, scale=col(CA))
        act(v("ZA", 144, 288), v("Z"), AF.Identity, scale=col(CB))
        act(v("NI"), idb, AF.Identity, scale=-1.0)
        for o, c in ((v("S1", 0, 1), 0.0), (v("EB", 32, 33), 1.0), (v("EE", 0, 1), 0.0), (v("OO", 0, 1), 0.0), (v("ST", 0, 1), 0.0),
                     (v("SB", 0, 1), 0.0), (v("FI", 256, 258), 0.0)):
            fill(o, c)

    def scalar_second():
        for nm, src, sc in (("NA", idb, -1.0 * RY), ("NB", idb, -1.0 * RZ), ("PQ4", v("ON"), col(P4)), ("RA", v("ON"), col(CA)),
                            ("RB", v("ON"), col(CB)), ("INA", v("ON"), col(CIN)), ("O16", v("ON"), 1.0 / 16), ("N16", v("ON"), -1.0 / 16)):
            act(v(nm), src, AF.Identity, scale=sc)
        act(v("MK"), v("IS"), AF.Identity, bias=4096.0)

    def scalar_third():
        for nm, src, sc in (("PMA", v("ON"), col(CMA)), ("PMB", v("ON"), col(CMB)), ("I8", idb, 8 * GATE), ("Z64", v("Z"), 1.0 / 64)):
            act(v(nm), src, AF.Identity, scale=sc)
        act(v("RS"), v("MM"), AF.Sign)
        act(v("TRM"), v("QS"), AF.Identity, bias=-2048.0)
        act(v("DTF", 1, 512), v("DT", 1, 512), AF.Identity, bias=256.0)

    def pairs(t, bank):
        for k in range(32):
            m0, c0 = 130 * (k % 8), 64 * t + k // 8
            msum(v(bank, 16 * k, 16 * k + 16), [(v("VM", m0 + 2, m0 + 130), v("HB", c0, 64 * t + 64, 4)),
                                                (v("VM", m0, m0 + 128), v("LB", c0, 64 * t + 64, 4))])

    def halves(t, bank):
        for b in range(2):
            fold(bank, 32 * b, 32, "VT%d" % t, 0, to_row("ZA", 144 * b))

    def halves2(t, bank):
        for b in range(2):
            act(v("A1%d" % t, b, 64, 2), v(bank, 32 * b, 32 * b + 32), AF.Identity, bias=0.5, scale=1.0 / 8192.0)
            act(v("AB%d" % t, b, 64, 2), v(bank, 32 * b, 32 * b + 32), AF.Identity, bias=4096.0 - BIG)

    def places(pf, pat):
        note("v", lambda: g.vector.transpose(T.PT[:], T.PG[:]), [v("PG")], [v("PT")], cost=256)
        for a in range(4):
            note("s", lambda a=a: g.scalar.activation(T.LT[32 * a:32 * a + 32, :, 32 * a:32 * a + 32], T.PT[32 * a:32 * a + 32, :], AF.Copy),
                 [v("PT"), (None, [("LT", 5000, 5004)])], [(None, [("LT", 512 * a, 512 * a + 512)])], cost=512)
        note("v", lambda: g.vector.transpose(T.OTM[:], T.OX0[:]), [v("OX0")], [v("OTM")])
        reduce(v("R0", 1, 2), v("OTM", 0, 128, 16), A.add)
        ts(v("O0M"), v("ON"), v("R0", 1, 2), A.mult)
        mm(v("B3", 0, 8), v("SD"), pf)
        act(v("DF"), v("B3", 0, 8), AF.Identity)

    def differ(out, a, b, bank, later=False):
        k = out[1][0][2] - out[1][0][1]
        msum(v(bank, 0, k), [(idb, a), (v("NI"), b)])
        act(v("EV", 0, k), v(bank, 0, k), AF.Abs)
        act(out, v("EV", 0, k), AF.Sign)

    def own_witnesses(vals, offs):
        ts(indw(v("FO"), offs), vals, 1.0, A.mult, 256.0, A.add)

    def reorder(t):
        pf = v("LC0") if t else v("PF")
        return [lambda: reduce(v("R0", 0, 1), v("B4", 256, 512), A.max, True),
                lambda: ts(v("SP", 0, 1), v("R0", 0, 1), 2 * GATE, A.add, 256.0, A.min),
                lambda: anywhere(cp, v("F1"), ind(v("FI"), v("SP", 0, 1))),
                lambda: (mm(v("B3", 0, 8), v("TGE"), v("F1", 0, 8)), tt(v("YO"), v("F1", 0, 8), pf, A.mult),
                         msum(v("B5", 0, 8), [(v("IDF"), pf), (v("R0C"), v("YO"))])),
                lambda: tt(v("GD"), v("B3", 0, 8), v("DF"), A.mult),
                lambda: (tt(v("MC%d" % t), v("B5", 0, 8), v("GD"), A.add),
                         send(*ways(t), "ac%d" % t, "LC%d" % t, v("MC%d" % t)))]

    def ways(t):
        return (after, before) if t else (before, after)

    def stage1(t):
        ow, c0 = "OW%d" % t, 64 * t
        mm(v("B0", 0, 64), idb, v("AH", c0, c0 + 64), True, False)
        if t == 0:
            for p in range(4):
                ts(v("WG", 128 * p, 128 * p + 128), ind(v("DT"), v(ow, 8 * p, 8 * p + 8)), v("RP", p, p + 1), A.mult)
            for p in range(4, 8):
                act(v("WG", 128 * p, 128 * p + 128), ind(v("DT"), v(ow, 8 * p, 8 * p + 8)), AF.Identity, scale=v("RP", p, p + 1))
            fold("B0", 0, 64, "WG", 0, to_row("ZW"), False, True)
            early()
            scalar_first()
            scalar_second()
            tt(v("QS"), v("MK"), v("DM"), A.mult)
            scalar_third()
            dma("y", "dn0", (T.FN[0:128:16, 0:4096], [("FN", 0, 4096)]), (T.DN[0:128:2, 0:512], [("DN", 0, 520)]))
            dma("y", "dn1", (T.FN[1:128:16, 0:4096], [("FN", 5000, 5001)]), (T.DN[1:128:2, 0:512], [("DN", 0, 520), ("FN", 4096, 4240)]))
            dma("y", "dfo", (T.FO[0:128:16, 0:4096], [("FO", 0, 4096)]), (T.DTF[0:128:2, :], [("DTF", 0, 512)]))
            for r, (b1, b2) in enumerate((("B3", "B4"), ("B6", "B4"))):
                pairs(r, b1)
                act(v("VT%d" % r), v(b1, 0, 512), AF.Identity)
                halves(r, b2)
                halves2(r, b2)
        else:
            cp(indw((T.FN[:], [("FN", 0, 4240), ("FN", 5000, 5001)]), v("LB0")), v("LA0"))
            cp(v("WG", 0, 512), ind(v("FN"), v(ow, 0, 32)))
            act(v("WG", 512, 1024), ind(v("FN"), v(ow, 32, 64)), AF.Copy)
            fold("B0", 0, 64, "WG", 0, to_row("ZP"), False, True)
        ts(v("OY"), v("B0", 0, 64), 2320.0, A.add)
        tt(v("T2"), v("B0", 0, 64), v("C2", c0, c0 + 64), A.add)
        tt(v("T1"), v("B0", 0, 64), v("C1", c0, c0 + 64), A.add)
        cp(v("O2"), v("T2"))
        cp(v("O1"), v("T1"))
        own = 16
        ych = [(0, 8), (8, 24), (24, 44), (44, 64)] if t else [(0, 16), (16, 40), (40, 64)]
        for a, b in ych:
            act(v("Y", 16 * a, 16 * b), ind(v("TX"), v("OY", a, b)), AF.Copy)

        def win(b):
            return v("PA1") if t else v("PA0", 0, 16 + 1024 * ((b + 15) // 16))

        act(v("PX", 0, 16 * own), ind(win(own), v("O1", 0, own)), AF.Copy)
        steps = ([("j", a, b) for a, b in ych] + [("d", 0, own), ("i", own, 48), ("i", 48, 64)] if t else
                 [("j", 0, 16), ("j", 16, 32), ("i", own, 32), ("d", 0, own), ("j", 32, 48), ("i", 32, 48), ("j", 48, 64), ("i", 48, 64)])
        done = {"j": [], "i": []}
        have = {"j": set(), "i": set()}
        for kind, a, b in steps:
            if kind == "j":
                tt(v("NJ", 16 + 16 * a, 16 + 16 * b), ind(win(b), v("O2", a, b)), v("Y", 16 * a, 16 * b), A.not_equal)
            elif kind == "i":
                tt(v("NQ", 16 * a, 16 * b), ind(win(b), v("O1", a, b)), v("Y", 16 * a, 16 * b), A.not_equal)
            else:
                differ(v("NQ", 0, 16 * own), v("Y", 0, 16 * own), v("PX", 0, 16 * own), "B5")
                kind = "i"
            have[kind] |= set(range(a, b))
            for u in range(16):
                if u not in done[kind] and have[kind] >= set(range(4 * u, 4 * u + 4)):
                    done[kind].append(u)
                    r = v("NJ", 15 + 64 * u, 79 + 64 * u) if kind == "j" else v("NQ", 64 * u, 64 * u + 64)
                    mm(v("B1" if kind == "j" else "B2", 0, 64), zall(u), r, len(done[kind]) == 1, len(done[kind]) == 16)
        pf = v("LC0") if t else v("PF")
        tt(v("OX0"), ind(pf, v("XO")), v("ON"), A.mult)
        msum(v("B3", 16, 48), [(v("OX0"), v("RD")), (idb, v("PC"))])
        strict[:] = "v"
        ts(v("TH"), v("B1", 0, 64), 6.5, A.is_lt, 6.5, A.mult)
        cp(v("OQ"), v("B3", 16, 48))
        tt(v("UB"), v("B2", 0, 64), v("TH"), A.is_lt)
        strict[:] = ""
        act(v("PG"), ind(v("PA%d" % t), v("OQ")), AF.Copy)

    def stage2(t):
        tab, pat = v("FN") if t else v("DT"), v("PA%d" % t)
        ale, alo = v("UB", 0, 64, 2), v("UB", 1, 64, 2)
        w = v("B0", 0, 32)
        scan(v("S1", 1, 65), v("UB"), v("A1%d" % t), 0.0, A.max, A.min)
        mm(v("B7", 0, 1), v("FC"), v("S1", 64, 65))
        tt(v("UN"), v("UB"), v("AB%d" % t), A.mult)
        tt(v("M2"), v("UN", 0, 64, 2), v("UN", 1, 64, 2), A.min)
        ts(v("PV"), v("S1", 0, 64, 2), v("B7", 0, 1), A.max, 8192.0, A.mult)
        mm(w, v("IDF"), v("PV"), True, False)
        tt(v("DD"), v("M2"), v("PV"), A.subtract)
        ts(v("OW2"), v("DD"), 512.0 - BIG, A.min, col(BB1) if t else BIG, A.add)
        act(v("WG", 256, 512), ind(tab, v("OW2", 16, 32)), AF.Copy)
        cp(v("WG", 0, 256), ind(tab, v("OW2", 0, 16)))
        fold("B0", 0, 32, "WG", 0, lambda i: to_row("ZP", 0 if t else 144 * (i // 2))(i), False, True)
        ts(v("C2B"), v("M2"), -1.0, A.mult, col(CBO), A.add)
        ts(v("EB", 0, 32), v("M2"), -0.5, A.is_gt)
        ts(v("AO1"), alo, 20.0, A.mult, 6.5, A.add)
        ts(v("NE"), ale, -6.5, A.mult, 6.5, A.add)
        ts(v("O65"), alo, 6.5, A.mult)
        places(v("LC0") if t else v("PF"), pat)
        ts(v("OY", 0, 32), w, -3824.0, A.add)
        tt(v("T2", 0, 32), w, v("C2B"), A.add)
        tt(v("T1", 0, 32), w, v("PV"), A.subtract)
        cp(v("O2", 0, 32), v("T2", 0, 32))
        ts(v("O1", 0, 32), v("T1", 0, 32), col(CO1), A.add)
        ych = [(0, 8), (8, 20), (20, 32)]
        for a, b in ych:
            act(v("Y", 16 * a, 16 * b), ind(v("TX"), v("OY", a, b)), AF.Copy)
        act(v("PX", 384, 512), ind(pat, v("O1", 24, 32)), AF.Copy)
        differ(v("N2", 384, 512), v("Y", 384, 512), v("PX", 384, 512), "B5")
        for a, b in ych:
            tt(v("NQ", 16 * a, 16 * b), ind(pat, v("O2", a, b)), v("Y", 16 * a, 16 * b), A.not_equal)
        fold("B1", 0, 32, "NQ", 0, zall)
        tt(v("N2", 0, 384), ind(pat, v("O1", 0, 24)), v("Y", 0, 384), A.not_equal)
        fold("B2", 0, 33, "N2", 0, zall)
        ts(v("KJ"), v("B1", 0, 32), 6.5, A.is_gt)
        tt(v("T5"), ale, v("KJ"), A.subtract)
        tt(v("T6"), v("NE"), v("KJ"), A.mult)
        tt(v("AEV"), v("T5"), v("AO1"), A.mult)
        tt(v("AOD"), v("O65"), v("T6"), A.subtract)
        scan(rv("SR", 31, 0), rv("EB", 31, 0), rv("B2", 31, 0), 0.0, A.mult, A.add)
        mm(v("B7", 0, 1), v("BC"), v("SR", 0, 1))
        scan(rv("SQ", 32, 1), rv("EB", 32, 1), rv("B2", 32, 1), v("B7", 0, 1), A.mult, A.add)
        tt(v("EE", 1, 33), v("AEV"), v("SQ", 1, 33), A.is_gt)
        tt(v("OO", 1, 33), v("AOD"), v("SQ", 1, 33), A.is_gt)

    def st(a, b, back=0, step=1):
        return v("ST", 1 + a - back, 1 + b - back, step)

    def start_of(a, b):
        return [(v("RA"), v("VS", 16 + a, 16 + b)), (v("RB"), v("VS", 15 + a, 15 + b)),
                (v("RA"), v("VS", 16 + RY + a, 16 + RY + b)), (v("RB"), v("VS", 16 + RZ + a, 16 + RZ + b))]

    def dist(a, b):
        return [(v("O16"), v("XH", 1 + a, 1 + b)), (v("N16"), v("XH", a, b))]

    def gates(a, b):
        return [(v("G8"), v("SB", 1 + a, 1 + b)), (v("N8"), v("SB", a, b))]

    def probes(t):
        pat = v("PA%d" % t)
        scan(v("CC", 0, 33), v("EE", 0, 33), v("OO", 0, 33), 0.0, A.add, A.add)
        mm(v("B7", 0, 1), v("TRO"), v("CC", 32, 33))
        msum(v("B6", 0, 32), [(idb, v("CC", 0, 32)), (v("NB"), v("EE", 1, 33)), (v("NA"), v("OO", 1, 33))])
        mm(v("B6", 32, 33), v("TRI"), v("CC", 32, 33))
        ts(st(0, 256), v("ISB"), v("B7", 0, 1), A.is_ge, col(SGN), A.mult)
        tt(v("T7"), v("B6", 0, 32), v("JK"), A.min)
        ts(v("OC"), v("T7"), v("B6", 32, 33), A.add, RY + RZ + 0.0, A.add)
        cp(indw(v("VS", 16, 5136), v("OC")), v("VT%d" % t))

        def items(m, a, b, per):
            return v(("B3", "B4", "B5", "B1")[m // per], (b - a) * (m % per), (b - a) * (m % per + 1))

        def pattern(ms_, a, b, per):
            for m in ms_:
                mm(items(m, a, b, per), (T.LT[:, m, :], [("LT", 0, 2048)]), st(a, b))

        strict[:] = "ts"
        for ms_ in (range(15, 16), range(0, 5), range(5, 10), range(10, 15)):
            pattern(ms_, 0, SA, 5)
            for m in ms_:
                act(v("PX", m, 16 * SA, 16), items(m, 0, SA, 5), AF.Copy)
        mm(v("B0", SA, SB1), v("OTM"), st(SA, SB1), True, False)
        mm(v("B2", 0, SA), v("OTM"), st(0, SA), True, False)
        mm(v("B1", 0, 256), v("O0M"), st(0, 256), True, False)
        for bank, a, b in (("B6", 0, SB1), ("B7", SB1, 256)):
            msum(v(bank, a, b), [(v("OTM"), st(a, b)), (v("PMA"), st(a, b)), (v("PMB"), st(a, b, 1))], True, False)
        pattern(range(12), SA, SB1, 6)
        msum(v("B0", SA, SB1), start_of(SA, SB1), False, True)
        msum(v("B2", 0, SA), start_of(0, SA), False, True)
        strict[:] = "vts"
        ts(v("TO16", SA, SB1), v("B0", SA, SB1), 16.0, A.add)
        ts(v("TO16", 0, SA), v("B2", 0, SA), 16.0, A.add)
        msum(v("B1", 0, 256), start_of(0, 256), False, True)
        msum(v("B0", SB1, 256), [(v("OTM"), st(SB1, 256))] + start_of(SB1, 256))
        pattern(range(12, 16), SA, SB1, 6)
        if t == 0:
            for a in (0, 16 + RY, 16 + RZ):
                anywhere(act, v("VS", a, a + 272), v("Y", 0, 272), AF.Identity, scale=0.0)

        def text(a, b):
            act(v("YB", 16 * (a - SA), 16 * (b - SA)), ind(v("TX"), v("TO16", a, b)), AF.Copy)

        def compare(a, b):
            tt(v("NQ", 16 * a, 16 * b), ind(v("TX"), v("TO16", a, b)), v("PX", 16 * a, 16 * b), A.not_equal)

        def compare2(bank, c0, a, b, then):
            mm(v(bank, c0 + a, c0 + b), v("INA"), st(a, b), True, False)
            for m in range(16):
                out = v("NQ", 16 * a + (b - a) * m, 16 * a + (b - a) * (m + 1))
                tt(out, items(m, a, b, 6), v("YB", 16 * (a - SA) + m, 16 * (b - SA), 16), A.not_equal)
                mm(v(bank, c0 + a, c0 + b), zall(m), out, False, m == 15)
                then(m)

        text(SA, SB1)
        def count(a, b):
            mm(v("B1", 256 + a, 256 + b), v("INA"), st(a, b), True, False)
            fold("B1", 256 + a, b - a, "NQ", 16 * a, zall, False, True)

        compare(0, 16)
        ts(v("XH", 1, 257), v("B1", 0, 256), -2048.0, A.add)
        ts(v("TO16", SB1, 256), v("B0", SB1, 256), 16.0, A.add)
        for bank, a, b in (("B6", 0, SB1), ("B7", SB1, 256)):
            msum(v(bank, a, b), dist(a, b), False, True)
        fold("B2", 256, 16, "XH", 1, zall)
        msum(v("B0", 256, 256 + SB1), [(v("OTM"), st(0, SB1))] + dist(0, SB1), True, False)
        compare(16, SH)
        count(0, SH)
        for bank, a, b in (("B6", 0, SB1), ("B7", SB1, 256)):
            act(v("GT", a, b), v(bank, a, b), AF.Sign, bias=511.5, scale=-1.0)
        text(SB1, 256)
        ts(v("OX"), v("B2", 256, 272), 1.0 / 16, A.mult, 2064.0, A.add)
        ts(v("XL"), v("B2", 256, 272), 1.0 / 16, A.mult, 0.25, A.add)
        compare2("B1", 256, SA, SB1, lambda m: pattern(range(m - m % 6, m + 1), SB1, 256, 6) if m in (5, 11, 15) else None)
        compare(SH, SA)
        for bank, a, b in (("B6", 0, SB1), ("B7", SB1, 256)):
            msum(v(bank, a, b), [(v("I8"), v("GT", a, b))] + dist(a, b), True, False)
        mm(v("B0", 256, 256 + SB1), v("I8"), v("GT", 0, SB1), False, False)
        count(SH, SA)
        act(v("SB", 1, 1 + SB1), v("B1", 256, 256 + SB1), AF.Sign, bias=-6.5)

        def named(bank, a, b):
            msum(v(bank, a, b), gates(a, b), False, True)

        def named2(bank, a, b):
            ts(v("R2", a, b), v(bank, a, b), col(HC), A.add, 0.0, A.max)

        def value(a, b):
            ts(v("R1", a, b), v("B0", 256 + a, 256 + b), col(HC), A.add, 0.0, A.max)

        compare2("B2", 0, SB1, 256, lambda m: named("B6", 0, SB1) if m == 8 else None)
        msum(v("B0", 256, 256 + SB1), gates(0, SB1), False, True)
        strict[:] = "vt"
        anywhere(act, v("NV"), ind(v("TX"), v("OX")), AF.Identity, bias=255.0, scale=-1.0)
        act(v("SB", 1 + SB1, 257), v("B2", SB1, 256), AF.Sign, bias=-6.5)
        named2("B6", 0, SB1)
        value(0, SB1)

        def last():
            named("B7", SB1, 256)
            mm(v("B3", 0, 128), v("PQ4"), st(0, 256, 0, 2), True, False)
            mm(v("B5", 0, 128), v("PQ4"), st(0, 256, 0, 2), True, False)
            named2("B7", SB1, 256)

        def last_value():
            msum(v("B0", 256 + SB1, 512), [(v("I8"), v("GT", SB1, 256)), (v("OTM"), st(SB1, 256))] + dist(SB1, 256) + gates(SB1, 256))
            value(SB1, 256)

        def first():
            mm(v("B6", 0, 256), v("G8"), v("SB", 1, 257))
            act(v("FI", 0, 256), v("B6", 0, 256), AF.Relu, bias=col(NII), scale=1.0 / GATE)

        return last, last_value, first

    def rows(name, u, a, b):
        k, w = _ROWS[name]
        return (T[name][:, :, a:b], [(name, 0, k * w)]) if u is None else (T[name][:, u, a:b], [(name, w * u + a, w * u + b)])

    def writes(t, last, last_value, first):
        d2 = [(v("ON"), v("R2", 0, 256, 2)), (v("ON"), v("R2", 1, 256, 2))]

        def accepted(a, b):
            for i in range(a, b):
                mm(v("B2", 0, 16), to_row("Z64")(i), v("SB", 1 + i, 242 + i, 16), i == 0, i == 15)

        def keys():
            msum(v("B3", 0, 128), d2, False, True)
            tt(v("MK2"), v("B3", 0, 128), v("DM", 0, 128), A.mult)
            cp(v("XW"), v("B3", 0, 128))
            scan(v("QS2"), v("RS", 0, 128), v("MK2"), 0.0, A.mult, A.add)

        def unnamed():
            msum(v("B4", 0, 128), d2)
            msum(v("B5", 0, 128), d2, False, False)
            act(v("NN"), v("B4", 0, 128), AF.Relu, bias=1.0, scale=-1.0)

        def same_key():
            for u in range(8):
                ts(rows("E3", u, 0, 128 - 16 * u), v("XW", 16 * u, 128), v("QS2", 16 * u + 15, 16 * u + 16), A.is_equal)
                if u < 7:
                    mm(v("B5", 16 * u + 16, 128), v("O8K"), rows("E3", u, 16, 128 - 16 * u), False, False)
            msum(v("B5", 0, 128), [(v("I8"), v("NN")), (v("T8K"), rows("E3", None, 0, 16))], False, True)

        def values():
            msum(v("B7", 0, 128), [(v("ON"), v("R1", 0, 256, 2)), (v("ON"), v("R1", 1, 256, 2))])
            act(v("MA%d" % t), v("B7", 0, 128), AF.Identity, bias=col(MAB), scale=rm(0))
            send(*ways(t), "aa%d" % t, "LA%d" % t, v("MA%d" % t))

        named = [lambda: tt(v("MK2"), v("B5", 0, 128), v("TRM", 16, 144), A.min),
                 lambda: scan(v("QS2"), v("RS", 0, 128), v("MK2"), 0.0, A.mult, A.add),
                 lambda: (ts(v("MB%d" % t), v("QS2", 15, 128, 16), 16 * 2048.0, A.add),
                          send(*ways(t), "ab%d" % t, "LB%d" % t, v("MB%d" % t)))]

        def same_place():
            mm(v("B1", 0, 256), v("O16"), v("XH", 1, 257), True, False)
            for u in range(16):
                ts(rows("E4", u, 0, 256 - 16 * u), v("XH", 1 + 16 * u, 257), v("XL", u, u + 1), A.subtract, v("B2", u, u + 1), A.is_equal)
                if u < 15:
                    mm(v("B1", 16 * u + 16, 256), v("O8K"), rows("E4", u, 16, 256 - 16 * u), False, False)
            msum(v("B1", 0, 256), [(v("O8K"), v("FI", 0, 256)), (v("T8K"), rows("E4", None, 0, 16))], False, True)

        placed = [lambda: tt(v("MK"), v("B1", 0, 256), v("TRM"), A.min),
                  lambda: scan(v("QS"), v("RS"), v("MK"), 0.0, A.mult, A.add),
                  lambda: ts(v("OT"), v("QS", 15, 256, 16), 16 * 2048.0 + 16.0, A.add)]

        def lowest():
            msum(v("B4", 256, 512), [(v("NI"), v("ISB")), (v("OH"), st(0, 256)), (v("O8K"), v("FI", 0, 256))])

        strict[:] = ""
        part = {}
        for nm, f in ([("last", last), ("keys", keys), ("unnamed", unnamed), ("value", last_value), ("values", values), ("key", same_key),
                       ("acc0", lambda: accepted(0, 6)), ("acc1", lambda: accepted(6, 16)), ("first", first), ("lowest", lowest),
                       ("place", same_place)] + [("n%d" % j, f) for j, f in enumerate(named)] + [("p%d" % j, f) for j, f in enumerate(placed)]
                      + [("r%d" % j, f) for j, f in enumerate(reorder(t))] + [("text", lambda: anywhere(cp, indw(v("TX"), v("OT")), v("NV")))]):
            k = len(ops)
            f()
            part[nm] = range(k, len(ops))

        def in_turn(q, names):
            line = [k for nm in names.split() for k in part[nm] if ops[k]["q"] == q]
            for a, b in zip(line, line[1:]):
                ops[b]["behind"].add(a)

        if t == 0:
            in_turn("t", "last keys unnamed value acc0 values key acc1 first lowest place")
            in_turn("v", "last keys value key n0 n1 n2 place r0 p0 r1 p1 r2 p2")
        else:
            in_turn("t", "acc0 acc1 last first keys place unnamed value key values lowest")
            in_turn("v", "last place keys key p0 value p1 n0 p2 n1 n2 text r0")
            dma("y", "dyt", hb(T.yt[:]), v("TX", 16, 4112), 5200)
            own_witnesses(v("MA0"), v("MB0"))
            own_witnesses(v("LA1"), v("LB1"))
            dma("s", "dyw", hb(T.yw[:]), (T.FO[0:128:16, 0:4096], [("FO", 0, 4096)]))
            dma("y", "dyo", hb(T.yo[:]), v("LC1"))

    for t in range(2):
        stage1(t)
        stage2(t)
        writes(t, *probes(t))

    def place(order, lags, floor):
        busy, at = {q: [] for q in eng}, {}
        for k in order:
            o = ops[k]
            x = max([at[j] + ops[j]["cost"] + lag for j, lag in lags[k]] + [floor[k]])
            if o["q"] is not None:
                line, j = busy[o["q"]], 0
                while j < len(line) and line[j][0] < x + o["cost"]:
                    x = max(x, line[j][1])
                    j += 1
                line.insert(j, (x, x + o["cost"]))
            at[k] = x
        return at

    if not _PLAN:
        every = range(len(ops))
        ahead = [[(j, ops[j]["late"] + WAKE) for j in o["deps"]] + [(j, 0) for j in o["behind"]] for o in ops]
        back = [[] for _ in ops]
        for k in every:
            for j, lag in ahead[k]:
                back[j].append((k, lag))
        waits, order = [len(x) for x in ahead], [k for k in every if not ahead[k]]
        for k in order:
            for j, _lag in back[k]:
                waits[j] -= 1
                if not waits[j]:
                    order.append(j)
        way = {}
        for k in reversed(order):
            way[k] = ops[k]["cost"] + max([ops[k]["late"]] + [way[j] + lag for j, lag in back[k]])
        order = sorted(every, key=lambda j: (-way[j], j))
        for _ in range(PASSES):
            at = place(order, ahead, [0] * len(ops))
            span = max(at[k] + ops[k]["cost"] + ops[k]["late"] for k in every)
            if not _PLAN or span < _PLAN[0]:
                _PLAN[:] = [span, at]
            rev = place(sorted(every, key=lambda j: (-at[j] - ops[j]["cost"], -j)), back, [o["late"] for o in ops])
            order = sorted(every, key=lambda j: (-rev[j] - ops[j]["cost"], j))
    for k, o in enumerate(ops):
        o["start"] = _PLAN[1][k]
        o["end"] = o["start"] + o["cost"] + o["late"]
    total, known = {}, {q: {} for q in eng}
    for o in sorted(ops, key=lambda x: x["start"]):
        total[o["sem"]] = total.get(o["sem"], 0) + o["inc"]
        o["at"] = total[o["sem"]]
        q = o["q"]
        if q is None:
            o["clock"] = {o["sem"]: o["at"]}
            continue
        kn = known[q]
        for k in sorted(o["deps"], key=lambda j: -ops[j]["end"]):
            d = ops[k]
            if kn.get(d["sem"], 0) < d["at"]:
                eng[q].wait_ge(T.sem[d["sem"]], d["at"])
                for s, c in d["clock"].items():
                    kn[s] = max(kn.get(s, 0), c)
        ins = o["fn"]()
        if o["sem"] != "sent":
            ins.then_inc(T.sem[o["sem"]], o["inc"])
        o["clock"] = dict(kn)
        o["clock"][o["sem"]] = max(o["at"], kn.get(o["sem"], 0))
    for s, c in total.items():
        g.wait_ge(T.sem[s], c)
